import numpy as np, ml_dtypes
CORES = [48,51,52,55]
N = 4
BF = ml_dtypes.bfloat16
def gentries(a):
    return np.ascontiguousarray(a.reshape(8, 16, -1).transpose(0, 2, 1)).reshape(8, -1)
def gtable(e):
    e = np.asarray(e); return np.ascontiguousarray(e.reshape(8, -1, 16).transpose(0, 2, 1)).reshape(128, -1).astype(np.int32)
V, FN, C, S, TV = 4096, 4096, 256, 995, 4
def perms(rng, *shape):
    return np.argsort(rng.random(shape), axis=-1)
def marks(rng, cnt):
    return np.argsort(rng.random(cnt.shape[:-2] + (16, cnt.shape[-1])), axis=-2) < cnt
def lay(loc, xw, nw, pw):
    inv = np.argsort(loc, axis=-1)
    x = np.take_along_axis(xw, inv[:, :, None, :], 3); nm = np.take_along_axis(nw, inv, 2)
    p = np.where(pw >= 0, np.take_along_axis(loc, np.maximum(pw, 0), 2), -1)
    return x, nm, p, np.take_along_axis(np.roll(loc, -1, axis=0), inv, 2)
def two(rng):
    return rng.integers(0, 64, (N, 16, FN)) + 192 * (np.arange(FN) & 1)
def reads(rng, hi):
    m = marks(rng, hi); return rng.integers(0, 64, m.shape) + 192 * m
def loose(rng, share):
    w = perms(rng, N, 8, FN); return np.where((w < V) & (rng.random((N, 8, FN)) < share), w, -1)
def tradition(rng):
    base = np.where(rng.random((8, 16, FN)) < 0.3, rng.choice(np.array([0, 128, 255]), (8, 16, FN)), rng.integers(0, 256, (8, 16, FN)))
    fo = np.where(rng.random((N, 8, 16, FN)) < 0.25, rng.integers(0, 256, (N, 8, 16, FN)), base)
    com = rng.integers(0, FN, (8, FN // 16))
    z = np.where(rng.random((8, V)) < 0.4, np.take_along_axis(com, rng.integers(0, FN // 16, (8, V)), 1), perms(rng, 8, FN)[:, :V])
    zz = np.where(rng.random((N, 8, V)) < 0.1, rng.integers(0, FN, (N, 8, V)), z)
    xw = np.take_along_axis(base[None], zz[:, :, None, :], 3)
    xw = np.where(rng.random((N, 8, 16, V)) < 0.25, rng.integers(0, 256, (N, 8, 16, V)), xw)
    nw = np.where(rng.random((N, 8, V)) < 0.15, rng.integers(0, FN, (N, 8, V)), z)
    pw = np.full((N, 8, FN), -1, np.int64); m = V // 12
    for r in range(N):
        for g in range(8):
            a = pw[r, g]; o = rng.permutation(V); a[z[g, o]] = o; a[rng.random(FN) < 0.3] = -1
            h = np.zeros(V, bool); h[a[a >= 0]] = True
            a[rng.permutation(np.flatnonzero(a < 0))[:m]] = rng.permutation(np.flatnonzero(~h))[:m]
    x, nm, p, cc = lay(perms(rng, N, 8, V), xw, nw, pw)
    for q in range(N):
        for g in range(8):
            i = rng.permutation(V)[:V // 32]; cc[q, g, i] = cc[q, g, rng.permutation(i)]
    return x, fo, nm, p, cc
def pack(x, fo, nm, p, cc):
    return {"tx": np.ascontiguousarray(x.reshape(N, 128, V)).astype(np.float32).astype(BF), "fo": np.ascontiguousarray(fo.reshape(N, 128, FN)).astype(np.float32).astype(BF),
            "nm": np.ascontiguousarray(nm).astype(np.int32), "pl": np.stack([gtable(a) for a in p]), "cc": np.stack([gtable(a) for a in cc])}
def setup_inputs(rng):
    return pack(*tradition(rng))
def setup_inputs_spread(rng):
    x = np.minimum(np.floor(256 * rng.random((N, 8, 16, V)) ** np.exp2(rng.integers(-2, 3, (N, 8, 1, V)))), 255)
    fo = np.minimum(np.floor(256 * rng.random((N, 8, 16, FN)) ** np.exp2(rng.integers(-2, 3, (N, 8, 1, FN)))), 255)
    nm = np.minimum(np.floor(FN * rng.random((N, 8, V)) ** np.exp2(rng.integers(-1, 3, (N, 8, 1)))), FN - 1)
    return pack(x, fo, nm, loose(rng, rng.choice(np.array([0.1, 0.3, 0.6, 1.0]), (N, 8, 1))), perms(rng, N, 8, V))
def setup_inputs_ends(rng):
    u = rng.integers(0, 2, (8, 16, 1)); side = rng.integers(0, 2, (8, 1, FN)); side[:, :, 0] = 0; side[:, :, FN - 1] = 1
    fl = rng.integers(1, 4, (N, 8, 1, FN)) * (rng.random((N, 8, 1, FN)) < 0.5); fl[..., 0] = 0; fl[..., FN - 1] = 0
    fo = 255 * (u ^ side ^ marks(rng, fl).astype(np.int64))
    xs = rng.integers(0, 2, (N, 8, 1, V)); xf = rng.choice(np.array([0, 1, 4, 7, 7, 8, 8, 16]), (N, 8, 1, V))
    e = np.arange(N)[:, None] + np.arange(8)[None, :]; v = np.array([0, 7, 8, 16])
    xs[..., 0] = 1; xs[..., V - 1] = 1; xf[:, :, 0, V - 1] = v[e & 3]; xf[:, :, 0, 0] = v[(e + 1) & 3]
    x = 255 * (u ^ xs ^ marks(rng, xf).astype(np.int64))
    nm = np.where(rng.random((N, 8, V)) < 0.7, (FN - 1) * rng.integers(0, 2, (N, 8, V)), rng.integers(0, FN, (N, 8, V))); nm[..., 0] = 0; nm[..., V - 1] = 0
    p = loose(rng, 0.4); p[(p == 0) | (p == V - 1)] = -1
    cc = np.zeros((N, 8, V), np.int64); cc[..., 1:V - 1] = 1 + perms(rng, N, 8, V - 2)
    for g in range(8):
        a, b = ((0, V - 1), (V - 1, 0))[g & 1]
        p[:, g, 0] = a; p[:, g, FN - 1] = b; cc[:, g, 0] = a; cc[:, g, V - 1] = b
    return pack(x, fo, nm, p, cc)
def hang(rng, un0):
    last = (S * TV - 1) % V; o = rng.permutation(V); o = np.concatenate([np.array([last]), o[o != last]]); un, on = o[:un0], o[un0:]
    phi = rng.permutation(FN)[:len(on)]; odd = phi[(phi & 1) == 1]; j = np.flatnonzero((phi & 1) == 0)[0]
    name = np.zeros(V, np.int64); name[on] = phi; name[un] = rng.choice(odd, un0); name[last] = phi[j]
    nm = np.tile(name, (N, 1)); q = rng.integers(0, N); nm[q, on[j]] = rng.choice(odd)
    hi = rng.choice(np.array([7, 8, 9]), (N, 1, V)); hi[q, 0, on[j]] = 8
    p = np.full(FN, -1, np.int64); p[phi] = on
    return reads(rng, hi), two(rng), nm, np.tile(p, (N, 1)), np.tile(np.arange(V), (N, 1))
def setup_inputs_corners(rng):
    x, fo, nm, p, cc = tradition(rng); o = rng.permutation(8)
    p[:, o[0]] = -1
    w = perms(rng, N, FN); p[:, o[1]] = np.where(w < V, w, -1)
    for r in range(N):
        w = rng.permutation(FN); a = np.where(w < V, w, -1)
        if r & 1: a[rng.choice(np.flatnonzero(a >= 0))] = -1
        else:
            a[:] = -1; a[rng.integers(0, FN)] = (0, V - 1)[(r >> 1) & 1]
        p[r, o[2]] = a
    for i in (3, 4):
        g = o[i]; fo[:, g] = two(rng); x[:, g] = reads(rng, rng.choice(np.array([0, 7, 7, 8, 8, 9, 9, 16]), (N, 1, V))); nm[:, g] = rng.integers(0, FN, (N, V))
        w = perms(rng, N, FN); p[:, g] = np.where((w < V) & ((i == 4) | (rng.random((N, FN)) < 0.5)), w, -1)
    cc[:, o[3]] = (np.arange(V) + 1) % V; cc[:, o[4]] = V - 1 - np.arange(V)
    for i, n in ((5, C - 2), (6, C - 1), (7, C)): x[:, o[i]], fo[:, o[i]], nm[:, o[i]], p[:, o[i]], cc[:, o[i]] = hang(rng, n)
    return pack(x, fo, nm, p, cc)
def late(rng, un0, vis, pair):
    n = len(vis)
    if pair: w = np.stack([rng.permutation(S)[:n], S * TV + rng.permutation(V - S * TV)[:n]])
    else: w = rng.permutation(V)[None, :n]
    o = rng.permutation(V); o = np.concatenate([w.reshape(-1), o[~np.isin(o, w)]]); un, on = o[:un0], o[un0:]
    a = rng.permutation(FN); new, phi = a[:n], a[FN - len(on):]; odd = phi[(phi & 1) == 1]
    name = np.zeros(V, np.int64); name[on] = phi; name[un] = rng.choice(odd, un0)
    nm = np.tile(name, (N, 1)); fo = two(rng); fo[:, :, new] = 255
    for k in range(n):
        r = int(rng.integers(0, N)); nm[(r + vis[k]) % N, w[:, k]] = new[k]; fo[r, :, int(new[k])] = rng.integers(0, 64, 16)
    hi = rng.choice(np.array([7, 8, 9]), (N, 1, V)); hi[:, :, w.reshape(-1)] = 0
    p = np.full(FN, -1, np.int64); p[phi] = on; x = reads(rng, hi)
    if pair: return x, fo, nm, np.tile(p, (N, 1)), np.tile(np.arange(V), (N, 1))
    x, nm, p, cc = lay(perms(rng, N, 1, V), x[:, None], nm[:, None], np.tile(p, (N, 1, 1)))
    return x[:, 0], fo, nm[:, 0], p[:, 0], cc[:, 0]
def turn(rng):
    c = rng.permutation(FN)[:N + 2]; x = rng.integers(0, 64, (N, 16, V)); fo = two(rng); fo[:, :, c] = 255
    nm = np.tile(c[:N, None], (1, V)); i = (S * TV + C) % V; nm[:, i - 1] = c[N]; nm[:, i] = c[N + 1]
    for r in range(N):
        t = 2 + r % (TV - 1); fo[r, :, int(c[(r + t) % N])] = rng.integers(0, 64, 16)
    return x, fo, nm, np.full((N, FN), -1, np.int64), np.tile(np.arange(V), (N, 1))
def setup_inputs_crowd(rng):
    x, fo, nm, p, cc = tradition(rng); o = rng.permutation(8); c = rng.permutation(FN)[:6 + N * TV]; half = loose(rng, 0.5)
    nm[:, o[0]] = c[0]; p[:, o[0]] = -1
    nm[:, o[1]] = c[1]; p[:, o[1]] = -1
    for t in range(1, TV + 1): nm[:, o[1], (S * t + 5) % V] = c[6 + N * (t - 1):6 + N * t]
    nm[:, o[2]] = c[2]; p[:, o[2]] = half[:, o[2]]
    nm[:, o[3]] = rng.choice(np.array([0, FN - 1, c[3]]), (N, V)); p[:, o[3]] = half[:, o[3]]
    nm[:, o[4]] = np.where((np.arange(V) & 1) == 1, c[3], c[4]); p[:, o[4]] = -1; p[1::2, o[4]] = half[1::2, o[4]]
    nm[:, o[5]] = c[5]; p[:, o[5]] = -1; p[:, o[5], c[5]] = V - 1
    x[:, o[6]], fo[:, o[6]], nm[:, o[6]], p[:, o[6]], cc[:, o[6]] = turn(rng)
    x[:, o[7]], fo[:, o[7]], nm[:, o[7]], p[:, o[7]], cc[:, o[7]] = late(rng, C // 2, list(range(1, TV + 1)), True)
    return pack(x, fo, nm, p, cc)
def still(rng, k):
    n = max(k - 1, 0); o = rng.permutation(V); un, on = o[:n], o[n:]
    phi = rng.permutation(FN)[:len(on)]; odd = phi[(phi & 1) == 1]; ev = on[(phi & 1) == 0]
    name = np.zeros(V, np.int64); name[on] = phi; name[un] = rng.choice(odd, n)
    nm = np.tile(name, (N, 1)); hi = rng.choice(np.array([7, 8, 9]), (N, 1, V))
    for q in range(N):
        w = ev[9 * q:9 * q + 9]; nm[q, w[1:]] = rng.choice(odd, 8); hi[q, 0, w[1:]] = rng.choice(np.array([7, 7, 6, 0]), 8)
        if k > 0 and q % 2 == 0:
            nm[q, w[0]] = rng.choice(odd); hi[q, 0, w[0]] = rng.choice(np.array([8, 8, 16]))
    p = np.full(FN, -1, np.int64); p[phi] = on
    x, nm, p, cc = lay(perms(rng, N, 1, V), reads(rng, hi)[:, None], nm[:, None], np.tile(p, (N, 1, 1)))
    return x[:, 0], two(rng), nm[:, 0], p[:, 0], cc[:, 0]
def setup_inputs_calm(rng):
    x, fo, nm, p, cc = tradition(rng); o = rng.permutation(8)
    for k in range(4): x[:, o[k]], fo[:, o[k]], nm[:, o[k]], p[:, o[k]], cc[:, o[k]] = still(rng, k)
    for k, n, vis, pair in ((4, 1, [2], False), (5, 1, [3], False), (6, 2 * TV, list(range(1, TV + 1)), True)):
        x[:, o[k]], fo[:, o[k]], nm[:, o[k]], p[:, o[k]], cc[:, o[k]] = late(rng, n, vis, pair)
    return pack(x, fo, nm, p, cc)
def check_inputs(d):
    bad = []
    for k, lo, hi in (("tx", 0, 255), ("fo", 0, 255), ("nm", 0, FN - 1), ("pl", -1, V - 1), ("cc", 0, V - 1)):
        v = np.asarray(d[k]).astype(np.float64)
        if not np.all((v >= lo) & (v <= hi) & (np.floor(v) == v)): bad.append("range of " + k)
    e = np.sort(np.stack([gentries(np.asarray(a)) for a in d["pl"]]), axis=-1)
    if np.any((e[..., 1:] == e[..., :-1]) & (e[..., 1:] >= 0)): bad.append("pl lists a place twice")
    e = np.sort(np.stack([gentries(np.asarray(a)) for a in d["cc"]]), axis=-1)
    if np.any(e != np.arange(V)): bad.append("cc is no permutation")
    return bad
def reference(tx, fo, nm, pl, cc):
    X = tx.astype(np.float32).astype(np.int32).reshape(N, 8, 16, V); F = fo.astype(np.float32).astype(np.int32).reshape(N, 8, 16, FN)
    name = nm.astype(np.int64).reshape(N, 8, V); P = np.stack([gentries(a) for a in pl]).astype(np.int64); con = np.stack([gentries(a) for a in cc]).astype(np.int64)
    forms = np.arange(FN)[None, :]
    for t in range(1, TV + 1):
        order = (np.arange(V) + S * t) % V
        for r in range(N):
            q = (r + t) % N; left = (r + t - 1) % N
            full = P[r] >= 0; y = np.where(full, np.take_along_axis(con[left], np.maximum(P[r], 0), 1), 0)
            n = np.take_along_axis(name[q], y, 1); x = np.take_along_axis(X[q], y[:, None, :], 2)
            near = np.abs(x - F[r]) < np.abs(x - np.take_along_axis(F[r], n[:, None, :], 2))
            votes = np.add.reduce(near.astype(np.int64), axis=1)
            other = full & (n != forms); amend = other & (votes >= 9)
            g, f = np.nonzero(amend); name[q, g, y[g, f]] = f
            p = np.where(full & ((n == forms) | amend), y, -1)
            listed = np.zeros((8, V), bool); g, f = np.nonzero(p >= 0); listed[g, p[g, f]] = True
            free = ~listed[:, order]; taken = free & (np.add.accumulate(free.astype(np.int64), axis=1) <= C)
            g, i = np.nonzero(taken); place = order[i]
            low = np.full((8, FN), V, np.int64); np.minimum.at(low, (g, name[q][g, place]), place)
            P[r] = np.where((p < 0) & (low < V), low, p)
    return {"yn": name.astype(np.float32), "yp": np.stack([gtable(a) for a in P]).astype(np.float32)}

@@ -1,0 +1,861 @@
+from concourse.bass import DstId, RemoteDMATransfer
+from concourse.mybir import AluOpType as OP, ActivationFunctionType as AF
+
+N, V, C, STEP, TV = 4, 4096, 256, 995, 4
+DUM0 = 4112
+WW = DUM0 + C
+BF, F32, I32, U16 = "bfloat16", "float32", "int32", "uint16"
+
+SB = {
+    "X": (V, BF), "F1": (V, BF), "F2": (V, BF), "F3": (V, BF), "F4": (V, BF),
+    "TW": (2 * V, BF), "LT": (V, BF), "CCT": (V, BF), "QW0": (WW, BF), "QW1": (WW, BF),
+    "IOT": (V, F32), "CIW": (V, F32), "DA": (V, BF), "RA": (V, BF), "DB": (V, BF), "RB": (V, BF), "SG": (V, BF),
+    "PLo": (256, I32), "PLp": (256, I32), "CCo": (256, I32), "IA": (256, I32), "IB": (256, I32), "IC": (256, I32), "ID": (256, I32), "IE": (512, I32),
+    "FA": (256, F32), "FB": (256, F32), "FC": (256, F32), "FD": (256, F32), "DM": (256, F32), "CIL": (256, F32),
+    "CHL": (512, BF), "OWN": (512, BF), "P2": (256, U16), "PT": (256, U16), "SO": (256, U16), "CIo": (256, U16), "CIp": (256, U16),
+    "QO": (256, U16), "QI2": (256, U16), "QI3": (256, U16), "QI4": (256, U16),
+    "NF": (256, F32), "NC": (256, F32), "NHL": (512, BF), "NO": (256, U16),
+    "LO": (256, U16), "LHL": (512, BF), "E1": (256, BF), "E2": (256, BF),
+    "FR": (256, BF), "CS": (272, BF), "LK": (256, F32), "CAND": (V, BF),
+    "DL": (8, F32), "RJ": (256, F32), "RHO": (256, F32), "CT": (16, F32), "RK": (256, F32),
+    "L1": (256, BF), "L2": (256, BF), "L3": (256, BF), "HO": (16, U16), "CO": (16, U16), "CB": (16, BF), "WO": (16, U16), "INV": (256, BF),
+    "NW": (256, F32), "NWT": (256, F32), "NLF": (16, F32), "NOF": (16, U16), "QG": (256, BF), "QC": (16, U16),
+    "EQ": (1920, BF), "ED": (256, BF), "EE": (256, BF), "LF": (256, BF), "TO": (64, F32),
+    "VAL": (256, BF), "OFF": (32, U16), "VI2": (256, BF), "VI3": (256, BF), "VI4": (256, BF),
+    "OI2": (32, U16), "OI3": (32, U16), "OI4": (32, U16),
+    "PI": (8, I32), "COL": (32, F32), "B": (144, BF), "BSEL": (144, BF), "BOUT": (144, BF), "B0": (144, BF), "B2": (144, BF),
+    "BQ": (144, BF), "B256": (144, BF),
+    "IDN": (128, BF), "IDF": (128, F32), "I2": (128, BF), "NI": (128, BF), "N2": (128, BF), "I64": (128, BF), "IBIG": (128, BF), "NBIG": (128, BF),
+    "U": (128, BF), "W": (128, BF), "ONES": (128, BF), "NEG": (128, BF), "TLE": (128, BF), "SUM2": (128, BF),
+    "MB": (512, BF),
+    "TRI": (256, F32), "REP": (16, U16), "DUM": (16, F32), "M1": (256, BF), "Y0": (256, F32),
+}
+SCRATCH = {k: ("sbuf", [128, n], d) for k, (n, d) in SB.items()}
+SCRATCH["NI3"] = ("sbuf", [128, 2, 128], I32)
+SCRATCH["CCD"] = ("dram", [128, 512], BF)
+SCRATCH["LD"] = ("dram", [3, 128, 512], BF)
+SCRATCH["FD3"] = ("dram", [3, 128, 256], BF)
+for _b in range(8):
+    SCRATCH["PS%d" % _b] = ("psum", [128, 512], F32)
+
+MSGS = ["pl", "cc", "f1", "f2", "f3", "ci"] + ["%s%d" % (m, t) for t in (2, 3, 4) for m in ("lh", "fr", "qo", "va", "of", "oq")]
+LOCAL = ["pl", "cc", "nm", "x", "fo", "cct", "cil", "own", "nxt", "yn", "yp"] + ["%s%d" % (m, t) for t in (2, 3, 4, 5) for m in ("lt", "ft")] \
+    + ["nr%d" % t for t in (1, 2, 3, 4)]
+SEMAPHORES = ["eV", "eS", "eP", "eG"] + ["r_" + m for m in MSGS] + ["s_" + m for m in MSGS] + ["d_" + m for m in LOCAL]
+
+CFG = {
+    "q": {1: "VSSSSSSS", 2: "SSSSSSSS", 3: "SSSSSSSS", 4: "SSSSSSSS"},
+    "t": {2: "SSSSSSSS", 3: "SSSSSSSS", 4: "SSSSSSSS"},
+    "bg": {1: "SSSSSSSS", 2: "VVVVVVVV", 3: "VVVVVVVV", 4: "VVVVVVVV"},
+    "ba": {1: "SSSSSSSS", 2: "SSSSSSSS", 3: "SSSSSSSS", 4: "SSSSSSSS"},
+    "aa": {1: "SSSSSVSV", 2: "SSSSSVSV", 3: "SSSSSVSV", 4: "SSSSSVSV"},
+    "ag": {1: "VVVVVVVV", 2: "VVVVVVVV", 3: "VVVVVVVV", 4: "VVVVVVVV"},
+    "cm": {1: "SSSS", 2: "SSSS", 3: "SSSS", 4: "SSSS"},
+    "fin": "SSSSSSSS",
+    "at": (0, 1),
+    "vg": "S", "qg": "S",
+}
+COST = {"cy": 0.00104, "g": 1.55, "s": 3.5, "fix": 0.06, "pe": 0.00052, "hop": 0.12, "self": 0.08,
+        "dma": 2.0, "rem": 2.5, "bw": 150e3, "rounds": 1, "steps": 24000, "tol": 0.2, "look": 0.15, "wait": 0.5}
+SPREAD = [({}, 2 / 170), ({"cy": 0.0009, "g": 1.15, "s": 2.0, "pe": 0.00045}, 1 / 130),
+          ({"cy": 0.00115, "g": 1.95, "s": 5.2, "pe": 0.0008, "hop": 0.2, "dma": 2.5, "rem": 3.2}, 1 / 230)]
+MEMO = {}
+SHIFT = {}
+GOALS = ["Gcc.0", "Gpl.0", "VPT.0", "VP2.0", "Gf1.0", "VNO.0", "SQW1.0", "SDB.0", "VTW.0", "SRB.0", "SCIW.0"]
+for _t in range(1, TV + 1):
+    GOALS += ["VLO.%d" % _t, "Gqo%d.%d" % (_t + 1, _t if _t > 1 else 0), "VQO.%d" % _t, "Glh%d.%d" % (_t + 1, _t), "VFR.%d" % _t,
+              "Gfr%d.%d" % (_t + 1, _t), "Gci.0", "VDL.%d" % _t, "VNO.%d" % _t, "Gof%d.%d" % (_t + 1, _t), "VOFF.%d" % _t,
+              "Goq%d.%d" % (_t + 1, _t), "STW.%d" % _t, "SDB.%d" % _t, "VDB.%d" % _t, "SRB.%d" % _t, "VRB.%d" % _t,
+              "SQW%d.%d" % ((_t + 1) % 2, _t)]
+GOALS = list(dict.fromkeys(GOALS))
+LATE = ["STW", "VTW", "SDB", "VDB", "PPS0", "PPS1", "SRB", "VRB", "SQW0", "SQW1", "VQW0", "VQW1", "VNHL", "GTW.0", "SCIW.0", "Gf2.0", "Gf3.0", "GCAND.0", "VQO.0"]
+LAZY = [x + ".0" for x in "VCOL VBSEL VB VBOUT VB0 VBBIG VB256 VB2 VIDN VI2 VNI VN2 VI64 VIBIG VNBIG VU VW VONES VNEG VSUM2 VTLE VMB SPS2 VTRI VREP "
+        "VDUM VOWN VM1 VCS VQW0 GNW GTO GOWN VBQ VIDF VLT VPI".split()]
+
+
+def build(g, core, T, topo, COST=COST):
+    q = T.rank_of(core)
+    ops = []
+    phase = [0, False]
+    cy, G, S, FIX = COST["cy"], COST["g"], COST["s"], COST["fix"]
+    eng = {"V": g.vector, "S": g.scalar, "P": g.tensor, "G": g, "Y": g.sync}
+
+    def a(name, lo=0, hi=None, st=None):
+        n = 512 if name[:2] == "PS" else SB[name][0]
+        hi = n if hi is None else hi
+        ap = T[name][:, lo:hi] if st is None else T[name][:, lo:hi:st]
+        cnt = hi - lo if st is None else (hi - lo + st - 1) // st
+        two = name[:2] != "PS" and SB[name][1] in (BF, U16)
+        return {"ap": ap, "reg": [(name, lo, hi)], "n": cnt, "two": two, "ps": name[:2] == "PS", "ind": False}
+
+    def ind(win, off):
+        return {"ap": win["ap"].indirect(off["ap"]), "reg": win["reg"], "off": off["reg"], "n": 16 * off["n"],
+                "two": False, "ps": False, "ind": True}
+
+    def add(e, fn, outs, ins, cost, kind="c", name=None):
+        r, w = [], []
+        for x in ins:
+            if isinstance(x, dict):
+                r += x["reg"] + x.get("off", [])
+        for x in outs:
+            w += x["reg"]
+            r += x.get("off", [])
+        ops.append({"e": e, "fn": fn, "r": r, "w": w, "cost": cost, "kind": kind, "name": name,
+                    "key": "%s%s.%d" % (e, name or w[0][0], phase[0]), "late": phase[0] == 0 or phase[1]})
+
+    def val(x):
+        return x["ap"] if isinstance(x, dict) else x
+
+    def vcost(o, i, base):
+        per = S if o["ind"] else G if i["ind"] else base
+        return FIX + cy * max(64, per * o["n"])
+
+    def cp(o, i):
+        add("V", lambda: g.vector.tensor_copy(o["ap"], i["ap"]), [o], [i], vcost(o, i, 0.5 if o["two"] and i["two"] else 1))
+
+    def tt(o, i0, i1, op):
+        add("V", lambda: g.vector.tensor_tensor(o["ap"], i0["ap"], i1["ap"], op), [o], [i0, i1],
+            vcost(o, i0, 1 if i0["ps"] or i1["ps"] else 2))
+
+    def ts(o, i, s1, op0, s2=None, op1=None):
+        c = vcost(o, i, 0.5 if o["two"] and i["two"] else 1)
+        if op1 is None:
+            add("V", lambda: g.vector.tensor_scalar(o["ap"], i["ap"], val(s1), None, op0), [o], [i, s1], c)
+        else:
+            add("V", lambda: g.vector.tensor_scalar(o["ap"], i["ap"], val(s1), val(s2), op0, op1), [o], [i, s1, s2], c)
+
+    def ms(o, c):
+        add("V", lambda: g.vector.memset(o["ap"], c), [o], [], vcost(o, o, 0.5 if o["two"] else 1))
+
+    def act(o, i, f, bias=None):
+        if bias is None:
+            add("S", lambda: g.scalar.activation(o["ap"], i["ap"], f), [o], [i], vcost(o, i, 1))
+        else:
+            add("S", lambda: g.scalar.activation(o["ap"], i["ap"], f, bias=bias), [o], [i], vcost(o, i, 1))
+
+    def mm(items, first=True, last=True):
+        def fn():
+            r = None
+            for k, (o, l, x) in enumerate(items):
+                r = g.tensor.matmul(o["ap"], l["ap"], x["ap"], first and k == 0, last and k == len(items) - 1)
+            return r
+        add("P", fn, [items[0][0]], [y for it in items for y in it[1:]], FIX + COST["pe"] * sum(max(64, it[2]["n"]) for it in items))
+
+    def mms(groups, out):
+        def fn():
+            r = None
+            for items in groups:
+                for k, (o, l, x) in enumerate(items):
+                    r = g.tensor.matmul(o["ap"], l["ap"], x["ap"], k == 0, k == len(items) - 1)
+            return r
+        add("P", fn, [out], [y for items in groups for it in items for y in it[1:]], FIX + COST["pe"] * 64 * sum(len(x) for x in groups))
+
+    def iota(o, pat, base, cm):
+        if SB[o["reg"][0][0]][1] == I32:
+            add("G", lambda: g.iota(o["ap"], pat, base, cm), [o], [], 0.13 + 2 * cy * o["n"])
+        else:
+            add("G", lambda: g.iota(o["ap"], pat, base, cm, allow_small_or_imprecise_dtypes=True), [o], [], 0.13 + 2 * cy * o["n"])
+
+    def clear(name, n, when):
+        for lo in range(0, n, 512):
+            hi = min(n, lo + 512)
+            iota(a(name, lo, hi), [[0, hi - lo]], 0, 0)
+            ops[-1]["when"] = when
+
+    def dma(e, name, pairs, outs, ins, nbytes):
+        add(e, lambda: [eng[e].dma_start(o, i) for o, i in pairs], outs, ins, COST["dma"] + nbytes / COST["bw"], "d", name)
+
+    def send(name, step, src, dst_ap, dst_reg, nbytes):
+        to = T.cores[(q + step) % N]
+        fr = T.cores[(q - step) % N]
+        rid, pid, _ = topo.addr(to)
+        add("G", lambda: g.remote_dma(dst_ap, src["ap"], T.sem["r_" + name], T.sem["s_" + name], pid, rid, topo.mask(core, to)),
+            [], [src], COST["rem"] + nbytes / COST["bw"], "s", name)
+        ops[-1]["cnt"] = len(topo.engines(core, to))
+        add("R", None, [{"reg": dst_reg}], [], 0.0, "r", name)
+        ops[-1]["cnt"] = len(topo.engines(fr, core))
+
+    def od(mat, i):
+        return a(mat, 15 - i, 143 - i)
+
+    def pick(out, mat, buf, lo, n):
+        return [(out, od(mat, i), a(buf, lo + i, lo + 16 * n, 16)) for i in range(16)]
+
+    def col(k):
+        return a("COL", k, k + 1)
+
+    def reg(name, lo=0, hi=1 << 20):
+        return {"reg": [(name, lo, hi)]}
+
+    dma("Y", "cc", [(T.CCo[:, :], T.cc[:, :])], [a("CCo")], [], 131072)
+    dma("S", "pl", [(T.PLo[:, :], T.pl[:, :])], [a("PLo")], [], 131072)
+    dma("Y", "fo", [(T.F4[:, :], T.fo[:, :])], [a("F4")], [], 1 << 20)
+    dma("Y", "nm", [(T.NI3[:, :, 16 * k:16 * k + 16], T.nm[k]) for k in range(8)], [reg("NI3")], [], 600000)
+    dma("Y", "x", [(T.X[:, :], T.tx[:, :])], [a("X")], [], 1 << 20)
+    ms(a("CCT"), 0.0)
+    iota(a("IOT", 0, 256), [[1, 256]], 1, 0)
+    iota(a("PI", 0, 1), [[0, 1]], 0, 1)
+    iota(col(0), [[0, 1]], 1, 1)
+    for n in (256, 512, 1024, 2048):
+        act(a("IOT", n, 2 * n), a("IOT", 0, n), AF.Identity, float(n))
+    ts(a("IE", 0, 256), a("CCo"), 4, OP.logical_shift_right)
+    ts(a("IE", 256, 512), a("CCo"), 15, OP.bitwise_and)
+    cp(a("CHL", 0, 256), a("IE", 0, 256))
+    ts(a("CHL", 256, 512), a("IE", 256, 512), 256.0, OP.mult)
+    send("cc", 1, a("CHL"), T.CCD[:, :], [("CCD", 0, 512)], 131072)
+    send("pl", 1, a("PLo"), T.PLp[:, :], a("PLp")["reg"], 131072)
+    for t in (1, 2, 3):
+        send("f%d" % t, t, a("F4"), T["F%d" % t][:, :], a("F%d" % t)["reg"], 1 << 20)
+    dma("Y", "cct", [(T.CCT[2::16, :], T.CCD[:, 0:256]), (T.CCT[3::16, :], T.CCD[:, 256:512])], [a("CCT")], [reg("CCD")], 131072)
+    clear("TW", V, 1.5)
+    clear("CAND", V, 12.0)
+    dma("Y", "nxt", [(T.CAND[2::16, :], T.CHL[:, 0:256]), (T.CAND[3::16, :], T.CHL[:, 256:512])], [a("CAND")], [a("CHL")], 131072)
+
+    ts(a("IC"), a("CCo"), 255, OP.bitwise_and)
+    ts(a("ID"), a("CCo"), 8, OP.logical_shift_right)
+    ts(a("RJ"), a("IC"), 16.0, OP.mult)
+    tt(a("RHO"), a("RJ"), a("ID"), OP.add)
+    cp(a("P2"), a("RHO"))
+    for k in range(4):
+        act(ind(a("CIW"), a("P2", 64 * k, 64 * k + 64)), a("IOT", 1024 * k, 1024 * k + 1024), AF.Silu)
+
+    k128, k144, k256 = a("IOT", 0, 128), a("IOT", 0, 144), a("IOT", 0, 256)
+    ts(a("PI", 1, 2), a("PI", 0, 1), 15, OP.bitwise_and)
+    cp(col(1), a("PI", 1, 2))
+    tt(col(2), col(0), col(1), OP.subtract)
+    ts(col(3), col(2), 15.0, OP.add)
+    ts(col(4), col(1), 0.0, OP.is_equal)
+    ts(col(5), col(1), 2.0, OP.is_lt)
+    ts(col(6), col(1), 3.0, OP.is_equal, 1.0 / 256, OP.mult)
+    ts(col(10), col(1), 2.0, OP.is_equal)
+    ts(col(7), col(10), 16.0, OP.mult, col(6), OP.add)
+    ts(col(8), col(1), 1.0, OP.is_equal)
+    ts(col(9), col(1), 1.0, OP.add)
+    ts(col(22), col(1), 4.0, OP.is_lt, col(5), OP.subtract)
+    ts(col(23), col(1), 4.0, OP.is_equal, -8192.0, OP.mult)
+    ts(col(24), col(23), col(5), OP.add)
+    for nm_, w in (("BQ", col(22)), ("BSEL", col(24)), ("B", 1.0), ("BOUT", col(7)), ("B0", col(10)), ("B256", 256.0)):
+        ts(a(nm_), k144, col(3), OP.is_equal, w, OP.mult)
+    if any("V" in s for s in CFG["cm"].values()):
+        ts(a("B2"), k144, col(3), OP.is_equal, 2.0, OP.mult)
+    ts(a("IDF"), k128, col(0), OP.is_equal)
+    for nm_, w in (("IDN", 1.0), ("I2", 2.0), ("NI", -1.0), ("N2", -2.0), ("I64", 64.0), ("IBIG", 8192.0), ("NBIG", -8192.0)):
+        if (nm_ != "I2" or any("V" in s for s in CFG["ba"].values())) and (nm_ != "N2" or any("V" in s for s in CFG["aa"].values())):
+            ts(a(nm_), k128, col(0), OP.is_equal, w, OP.mult)
+    ts(a("U"), k128, col(2), OP.is_ge)
+    ts(a("W"), k128, col(3), OP.is_le)
+    tt(a("ONES"), a("U"), a("W"), OP.mult)
+    ts(a("NEG"), a("ONES"), -1.0, OP.mult)
+    ts(a("SUM2"), a("ONES"), col(5), OP.mult)
+    ts(a("U"), k128, col(0), OP.is_ge)
+    tt(a("TLE"), a("U"), a("W"), OP.mult)
+    for t in range(1, TV + 1):
+        ts(col(10 + t), col(1), float((STEP * t) % V % 16), OP.is_lt)
+        ts(a("MB", 128 * t - 128, 128 * t), a("ONES"), col(10 + t), OP.mult)
+    act(a("PS2", 256, 512), k256, AF.Identity)
+    iota(a("NW"), [[0, 16], [1, 16]], 0, 0)
+    ts(a("TRI"), a("NW"), col(1), OP.is_gt)
+    ts(a("REP"), a("IOT", 0, 16), -1.0, OP.add)
+    iota(a("TO", 0, 16), [[16, 16]], DUM0, 0)
+    ts(a("DUM"), a("TO", 0, 16), col(1), OP.add)
+    iota(a("FD"), [[16, 256]], V, 0)
+    iota(a("OWN", 0, 256), [[16, 256]], 0, 0)
+    ts(a("OWN", 256, 512), k256, 0.0, OP.mult, col(9), OP.add)
+    ms(a("M1"), -1.0)
+    ms(a("CS", 0, 1), 0.0)
+    ms(a("CS", 257, 258), 16.0)
+    ms(a("QW0", 0, 1), 0.0)
+    ms(a("QW1", 0, 1), 0.0)
+    ts(a("LT", 0, 64), a("IOT", 0, 64), col(8), OP.mult)
+    for k in range(6):
+        n = 64 << k
+        ts(col(16 + k), col(4), float(n), OP.mult)
+        ts(a("LT", n, 2 * n), a("LT", 0, n), col(16 + k), OP.add)
+
+    for h in range(2):
+        add("V", lambda h=h: g.vector.tensor_scalar(T.NF[:, 128 * h:128 * h + 128], T.NI3[:, h, :], 1.0, None, OP.add),
+            [a("NF", 128 * h, 128 * h + 128)], [reg("NI3")], FIX + 128 * cy)
+        add("P", lambda h=h: g.tensor.transpose(T.PS7[:, 128 * h:128 * h + 128], T.NF[:, 128 * h:128 * h + 128], T.IDF[:, :]),
+            [a("PS7")], [a("NF", 128 * h, 128 * h + 128), a("IDF")], FIX + 512 * COST["pe"])
+    for h in range(2):
+        cp(a("NC", h, 256, 2), a("PS7", 128 * h, 128 * h + 128))
+
+    def names(t):
+        if t <= TV:
+            ts(a("NO"), a("NC"), -1.0, OP.add)
+        act(a("NHL", 0, 256), a("NC"), AF.Identity)
+        tt(a("NHL", 256, 512), a("NC"), a("NHL", 0, 256), OP.subtract)
+
+    def name_rows(t):
+        dma("Y", "nr%d" % t, [(T.CAND[0::16, :], T.NHL[:, 0:256]), (T.CAND[1::16, :], T.NHL[:, 256:512])], [a("CAND")], [a("NHL")], 131072)
+    names(1)
+    name_rows(1)
+
+    def tilde(src, out):
+        ts(a("IA"), src, 15, OP.bitwise_and)
+        ts(a("IB"), src, 4, OP.logical_shift_right, 255, OP.bitwise_and)
+        ts(a("FA"), a("IA"), 256.0, OP.mult)
+        tt(a("FB"), a("FA"), a("IB"), OP.add)
+        cp(out, a("FB"))
+
+    def gather(e, out, win, off):
+        if e == "V":
+            cp(out, ind(win, off))
+        else:
+            act(out, ind(win, off), AF.Identity)
+
+    def hints(t, offs):
+        for k in range(8):
+            gather(CFG["q"][t][k], a("QW%d" % (t % 2), 1 + 512 * k, 513 + 512 * k), a("CCT"), a(offs, 32 * k, 32 * k + 32))
+
+    dbank = [0]
+
+    def named(t):
+        for k in range(8):
+            lo, hi = 512 * k, 512 * k + 512
+            w, off = a("F%d" % t), a("NO", 32 * k, 32 * k + 32)
+            if CFG["bg"][t][k] == "V":
+                tt(a("DB", lo, hi), ind(w, off), a("X", lo, hi), OP.subtract)
+                if CFG["ba"][t][k] == "V":
+                    ts(a("RB", lo, hi), a("DB", lo, hi), 0.0, OP.max)
+                else:
+                    act(a("RB", lo, hi), a("DB", lo, hi), AF.Abs)
+            else:
+                act(a("DB", lo, hi), ind(w, off), AF.Identity)
+                p = a("PS%d" % (dbank[0] % 2))
+                dbank[0] += 1
+                mm([(p, a("IDN"), a("DB", lo, hi)), (p, a("NI"), a("X", lo, hi))])
+                act(a("RB", lo, hi), p, AF.Abs)
+
+    tilde(a("PLp"), a("PT"))
+    ts(a("FC"), a("PLp"), 0.0, OP.is_lt)
+    ts(a("FD"), a("FD"), col(1), OP.add)
+    tt(a("DM"), a("FC"), a("FD"), OP.mult)
+    hints(1, "PT")
+    for k in range(4):
+        p = a("PS%d" % (5 + k % 2), 0, 64)
+        mm(pick(p, "BQ", "QW1", 1 + 1024 * k, 64))
+        tt(a("FC", 64 * k, 64 * k + 64), p, a("DM", 64 * k, 64 * k + 64), OP.max)
+        cp(a("QO", 64 * k, 64 * k + 64), p)
+        cp(a("SO", 64 * k, 64 * k + 64), a("FC", 64 * k, 64 * k + 64))
+        cp(ind(a("TW"), a("SO", 64 * k, 64 * k + 64)), a("LT", 1024 * k, 1024 * k + 1024))
+    send("qo2", 1, a("QO"), T.QI2[:, :], a("QI2")["reg"], 65536)
+    named(1)
+    dma("Y", "cil", [(T.CIL[:, :], T.CIW[0::16, :])], [a("CIL")], [a("CIW")], 131072)
+    ts(a("CIL"), a("CIL"), -1.0, OP.add)
+    cp(a("IC"), a("CIL"))
+    tilde(a("IC"), a("CIo"))
+    send("ci", 1, a("CIo"), T.CIp[:, :], a("CIp")["reg"], 65536)
+
+    for t in range(1, TV + 1):
+        phase[0] = t
+        QW = "QW%d" % (t % 2)
+        s = (STEP * t) % V
+        ca = s // 16
+        if t > 1:
+            cp(ind(a("TW", 0, WW), a("OI%d" % t, 16, 32)), a("VI%d" % t))
+        for h in range(2):
+            lo, hi = 128 * h, 128 * h + 128
+            p = a("PS%d" % (3 + h), 128, 256)
+            mm([(p, od("BSEL", i), a("TW", 256 * i + lo, 256 * i + hi)) for i in range(16)])
+            ts(a("LO", lo, hi), p, -1.0, OP.add, 0.0, OP.max)
+            act(a("LHL", lo, hi), p, AF.Identity)
+            tt(a("LHL", 256 + lo, 256 + hi), p, a("LHL", lo, hi), OP.subtract)
+            tt(a("E1", lo, hi), p, a("NC", lo, hi), OP.is_equal)
+            ts(a("E2", lo, hi), a("LHL", lo, hi), 0.5, OP.is_lt, -1.0, OP.mult)
+        if t < TV:
+            send("lh%d" % (t + 1), 1, a("LHL"), T.LD[t - 1], [("LD%d" % t, 0, 512)], 131072)
+        def pass_hints(step):
+            if step == CFG["at"][0]:
+                cp(ind(a(QW), a("OI%d" % t, 0, 16)), a("VI%d" % t))
+            if 0 <= step - CFG["at"][1] < 4:
+                h = step - CFG["at"][1]
+                mm(pick(a("PS5", 64 * h, 64 * h + 64), "BQ", QW, 1 + 1024 * h, 64))
+            if step == CFG["at"][1] + 3:
+                cp(a("QO"), a("PS5", 0, 256))
+                if t < TV:
+                    send("qo%d" % (t + 1), 1, a("QO"), T["QI%d" % (t + 1)][:, :], a("QI%d" % (t + 1))["reg"], 65536)
+        if t == TV:
+            clear("TW", V + 16, 0.0)
+        if t < TV:
+            dma("Y", "lt%d" % (t + 1), [(T.LT[0::16, :], T.LD[t - 1][:, 0:256]), (T.LT[1::16, :], T.LD[t - 1][:, 256:512])],
+                [a("LT")], [reg("LD%d" % t)], 131072)
+        else:
+            dma("Y", "lt5", [(T.LT[0::16, :], T.LHL[:, 0:256]), (T.LT[1::16, :], T.LHL[:, 256:512])], [a("LT")], [a("LHL")], 131072)
+        for k in range(8):
+            lo, hi = 512 * k, 512 * k + 512
+            w, off = a("F%d" % t), a("LO", 32 * k, 32 * k + 32)
+            if CFG["ag"][t][k] == "V":
+                tt(a("DA", lo, hi), ind(w, off), a("X", lo, hi), OP.subtract)
+            else:
+                act(a("DA", lo, hi), ind(w, off), AF.Identity)
+                p = a("PS%d" % (0, 1, 6, 7)[(k + 2) % 4])
+                mm([(p, a("IDN"), a("DA", lo, hi)), (p, a("NI"), a("X", lo, hi))])
+                act(a("RA", lo, hi), p, AF.Abs)
+            p = a("PS%d" % (6, 7, 0, 1)[k % 4])
+            if CFG["bg"][t][k] == "V" and CFG["ba"][t][k] == "V":
+                items = [(p, a("I2"), a("RB", lo, hi)), (p, a("NI"), a("DB", lo, hi))]
+            else:
+                items = [(p, a("IDN"), a("RB", lo, hi))]
+            if CFG["ag"][t][k] == "S":
+                items += [(p, a("NI"), a("RA", lo, hi))]
+            elif CFG["aa"][t][k] == "V":
+                ts(a("RA", lo, hi), a("DA", lo, hi), 0.0, OP.max)
+                items += [(p, a("IDN"), a("DA", lo, hi)), (p, a("N2"), a("RA", lo, hi))]
+            else:
+                act(a("RA", lo, hi), a("DA", lo, hi), AF.Abs)
+                items += [(p, a("NI"), a("RA", lo, hi))]
+            mm(items)
+            if CFG["cm"][t][k // 2] == "V":
+                ts(a("SG", lo, hi), p, 0.5, OP.is_gt, -0.5, OP.add)
+            else:
+                act(a("SG", lo, hi), p, AF.Sign, -0.5)
+            if t > 1:
+                pass_hints(k)
+            if k % 2:
+                j = k // 2
+                p = a("PS2", 64 * j, 64 * j + 64)
+                mm([(p, a("I64"), a("E1", 64 * j, 64 * j + 64)), (p, a("I64"), a("E2", 64 * j, 64 * j + 64))]
+                   + pick(p, "B2" if CFG["cm"][t][j] == "V" else "B", "SG", 1024 * j, 64))
+        votes = a("PS2", 0, 256)
+        ts(a("FR"), votes, 1.0, OP.is_lt)
+        add("V", lambda: g.vector.tensor_tensor_scan(T.CS[:, 1:257], T.FR[:, :], T.FR[:, :], 0.0, OP.add, OP.max),
+            [a("CS", 1, 257)], [a("FR")], FIX + 128 * cy)
+        if t < TV:
+            send("fr%d" % (t + 1), 1, a("FR"), T.FD3[t - 1], [("FD%d" % t, 0, 256)], 65536)
+            dma("Y", "ft%d" % (t + 1), [(T.LT[4::16, :], T.FD3[t - 1])], [a("LT")], [reg("FD%d" % t)], 65536)
+        else:
+            dma("Y", "ft5", [(T.LT[4::16, :], T.FR[:, :])], [a("LT")], [a("FR")], 65536)
+        p = a("PS6", 0, 256)
+        mm([(p, a("IDN"), a("LHL", 0, 256)), (p, a("IDN"), a("LHL", 256, 512)), (p, a("NBIG"), a("FR"))])
+        act(a("LK"), p, AF.Identity)
+        p = a("PS6", 256, 512)
+        mm([(p, a("IDN"), a("NHL", 0, 256)), (p, a("IDN"), a("NHL", 256, 512)), (p, a("IBIG"), a("M1")), (p, a("IBIG"), a("FR"))])
+        tt(a("NC"), p, a("LK"), OP.max)
+        phase[1] = True
+        names(t + 1)
+        if t < TV:
+            named(t + 1)
+            hints(t + 1, "QI%d" % (t + 1))
+            for k in range(8):
+                gather(CFG["t"][t + 1][k], a("TW", 512 * k, 512 * k + 512), a("LT"), a("CIp", 32 * k, 32 * k + 32))
+        phase[1] = False
+        below = [(a("ONES"), a("CS", ca, ca + 1)), (a("MB", 128 * t - 128, 128 * t), a("FR", ca, ca + 1))]
+        tot, c16 = a("CS", 256, 257), a("CS", 257, 258)
+        pa, pt, px = a("PS3", 0, 1), a("PS3", 1, 2), a("PS3", 2, 3)
+        mms([[(pa, l, x) for l, x in below], [(pt, a("ONES"), tot), (pt, a("NEG"), c16)],
+             [(px, a("NEG"), tot), (px, a("ONES"), c16)] + [(px, l, x) for l, x in below]], a("PS3", 0, 3))
+        pb = a("PS5", 256, 257)
+        mm([(pb, od("B", i), a("CS", 16 * i + 16, 16 * i + 17)) for i in range(16)])
+        mm(pick(a("PS4", 0, 16), "B", "CS", 1, 16))
+        p = a("PS7", 256, 512)
+        mm([(p, a("ONES"), a("CS", 0, 256)), (p, a("TLE"), a("FR"))])
+        act(a("CT"), a("PS4", 0, 16), AF.Identity)
+        act(a("RK"), p, AF.Identity)
+        ts(a("DL", 0, 1), pt, pa, OP.min, 0.0, OP.max)
+        ts(a("RJ"), k256, px, OP.is_gt, a("DL", 0, 1), OP.mult)
+        ts(a("INV"), k256, -256.0, OP.add, pt, OP.is_gt)
+        tt(a("RHO"), a("RJ"), a("PS2", 256, 512), OP.add)
+        ts(a("L1"), a("RHO"), pb, OP.is_gt, 16.0, OP.mult)
+        ph, pc, pp = a("PS4", 32, 48), a("PS3", 16, 32), a("PS4", 64, 80)
+        mm(pick(ph, "B", "L1", 0, 16))
+        ts(a("HO"), ph, 1.0 / 16, OP.mult, 15.0, OP.min)
+        act(a("CB"), ph, AF.Identity)
+        tt(a("L2"), ind(a("CT"), a("HO")), a("RHO"), OP.is_lt)
+        mm(pick(pc, "B", "L2", 0, 16) + [(pc, a("IDN"), a("CB"))])
+        ts(a("CO"), pc, 255.0, OP.min)
+        act(a("CB"), pc, AF.Identity)
+        tt(a("L3"), ind(a("RK"), a("CO")), a("RHO"), OP.is_lt)
+        mm(pick(pp, "B256", "L3", 0, 16) + [(pp, a("IDN"), a("CB"))])
+        ts(a("WO"), pp, float(V - 1), OP.min)
+        gather(CFG["vg"], a("VAL"), a("CAND"), a("WO"))
+        if t < TV:
+            send("va%d" % (t + 1), 1, a("VAL"), T["VI%d" % (t + 1)][:, :], a("VI%d" % (t + 1))["reg"], 65536)
+            name_rows(t + 1)
+        if t == TV - 1:
+            dma("Y", "own", [(T.CAND[2::16, :], T.OWN[:, 0:256]), (T.CAND[3::16, :], T.OWN[:, 256:512])], [a("CAND")], [a("OWN")], 131072)
+        pn, pw, pl_, po, pq = a("PS3", 32, 48), a("PS2", 0, 256), a("PS7", 0, 256), a("PS6", 0, 16), a("PS4", 96, 112)
+        mm(pick(pn, "BSEL", "VAL", 0, 16))
+        mm([(pw, a("SUM2"), a("VAL"))])
+        cp(a("NOF"), pn)
+        cp(a("NLF"), pn)
+        act(a("NW"), pw, AF.Identity)
+        gather(CFG["qg"], a("QG"), a(QW), a("NOF"))
+        mm(pick(pq, "B0", "QG", 0, 16))
+        mm([(pl_, a("ONES"), a("INV"))], True, False)
+        mm(pick(po, "BQ" if t < TV else "BSEL", "VAL", 0, 16), True, False)
+        at, items = 0, []
+        for i in range(15):
+            n = 240 - 16 * i
+            ts(a("EQ", at, at + n), a("NW", 256 - n, 256), a("NLF", i, i + 1), OP.is_equal)
+            items.append((a("PS7", 256 - n, 256), a("ONES"), a("EQ", at, at + n)))
+            at += n
+            if i in (3, 8, 14):
+                mm(items, False, False)
+                items = []
+        tt(a("NWT"), pw, a("TRI"), OP.mult)
+        tt(a("ED"), ind(a("NLF"), a("REP")), a("NWT"), OP.is_equal)
+        mm([(pl_, a("ONES"), a("ED"))], False, False)
+        cp(a("QC"), pq)
+        tt(a("EE"), ind(a("LK"), a("QC")), a("NW"), OP.is_equal)
+        mm([(pl_, a("ONES"), a("EE"))], False, True)
+        ts(a("LF"), pl_, 0.5, OP.is_gt, 512.0, OP.mult)
+        mm(pick(po, "B", "LF", 0, 16), False, True)
+        lo = 16 if t < TV else 0
+        tt(a("TO", lo, lo + 16), po, a("DUM"), OP.min)
+        cp(a("OFF", lo, lo + 16), a("TO", lo, lo + 16))
+        if t < TV:
+            OI = "OI%d" % (t + 1)
+            send("of%d" % (t + 1), 1, a("OFF", 16, 32), T[OI][:, 16:32], a(OI, 16, 32)["reg"], 4096)
+            ts(a("TO", 32, 48), a("TO", 16, 32), -4100.0, OP.add, 1000.0, OP.mult)
+            tt(a("TO", 48, 64), a("TO", 32, 48), a("NLF"), OP.max)
+            tt(a("TO", 0, 16), a("TO", 48, 64), a("DUM"), OP.min)
+            cp(a("OFF", 0, 16), a("TO", 0, 16))
+            send("oq%d" % (t + 1), 1, a("OFF", 0, 16), T[OI][:, 0:16], a(OI, 0, 16)["reg"], 4096)
+
+    for k in range(8):
+        gather(CFG["fin"][k], a("DA", 512 * k, 512 * k + 512), a("LT"), a("QO", 32 * k, 32 * k + 32))
+        if k % 4 == 3:
+            lo, hi = 128 * (k // 4), 128 * (k // 4) + 128
+            p = a("PS0", lo, hi)
+            mm(pick(p, "BSEL", "DA", 16 * lo, 128) + [(p, a("NI"), a("OWN", lo, hi)), (p, a("NI"), a("OWN", 256 + lo, 256 + hi))])
+            ts(a("E1", lo, hi), p, 0.0, OP.not_equal)
+            p = a("PS1", lo, hi)
+            mm(pick(p, "BOUT", "QW0", 1 + 16 * lo, 128), True, False)
+            mm([(p, a("NBIG"), a("E1", lo, hi))], False, True)
+            ts(a("Y0", lo, hi), p, -1.0, OP.max)
+    for k in range(8):
+        for h in range(2):
+            p = a("PS5", 32 * k + 16 * h, 32 * k + 16 * h + 16)
+            mm([(p, a("NHL", h, 256, 2), a("IDN", 16 * k, 16 * k + 16)), (p, a("NHL", 256 + h, 512, 2), a("IDN", 16 * k, 16 * k + 16))])
+    act(a("FA"), a("PS5", 0, 256), AF.Identity, -1.0)
+    dma("Y", "yn", [(T.yn[k], T.FA[:, 32 * k:32 * k + 32]) for k in range(8)], [], [a("FA")], 300000)
+    cp(ind(a("TW", 0, WW), a("OFF", 0, 16)), a("VAL"))
+    for h in range(2):
+        p = a("PS%d" % (3 + h), 0, 128)
+        mm([(p, a("IDN"), a("M1", 0, 128))] + pick(p, "BQ", "TW", 1 + 2048 * h, 128))
+        tt(a("FB", 128 * h, 128 * h + 128), p, a("Y0", 128 * h, 128 * h + 128), OP.max)
+    dma("Y", "yp", [(T.yp[:, :], T.FB[:, :])], [], [a("FB")], 131072)
+    return ops
+
+
+def hazards(ops):
+    hist = {}
+    sent = {}
+    for i, o in enumerate(ops):
+        deps = {}
+        acc = [(x, False) for x in o["r"]] + [(x, True) for x in o["w"]]
+        for (nm_, lo, hi), wr in acc:
+            bank = nm_[:2] == "PS"
+            for j, l2, h2, w2 in hist.get(nm_, []):
+                over = lo < h2 and l2 < hi
+                if over and (wr or w2):
+                    deps[j] = deps.get(j, False) or (w2 and not wr)
+                elif bank and (ops[j]["e"] != o["e"] or wr):
+                    deps[j] = deps.get(j, False)
+        if o["kind"] == "s":
+            sent[o["name"]] = i
+        if o["kind"] == "r":
+            deps = {sent[o["name"]]: True}
+        for (nm_, lo, hi), wr in acc:
+            h = hist.setdefault(nm_, [])
+            if wr and nm_[:2] != "PS":
+                h[:] = [e for e in h if not (lo <= e[1] and e[2] <= hi)]
+            elif nm_[:2] == "PS":
+                h[:] = h[-48:]
+            h.append((i, lo, hi, wr))
+        deps.pop(i, None)
+        o["deps"] = deps
+
+
+def order(ops):
+    n = len(ops)
+    succ = [[] for _ in range(n)]
+    for i, o in enumerate(ops):
+        for j in o["deps"]:
+            succ[j].append(i)
+    pri = [0.0] * n
+    early = [0.0] * n
+    for i, o in enumerate(ops):
+        early[i] = o["cost"] + max([early[j] for j in o["deps"]] + [0.0])
+    done = [False] * n
+    count = [0]
+
+    def pull(i):
+        stack = [(i, False)]
+        while stack:
+            j, ripe = stack.pop()
+            if ripe:
+                pri[j] = -count[0]
+                count[0] += 1
+            elif not done[j]:
+                done[j] = True
+                stack.append((j, True))
+                stack += [(k, False) for k in sorted(ops[j]["deps"], key=lambda k: early[k])]
+    stage = {k: x for x, k in enumerate(GOALS)}
+    for i in sorted(range(n), key=lambda i: (stage.get(ops[i]["key"], len(GOALS)), i)):
+        pull(i)
+    pri = [p + SHIFT.get(o["key"], 0.0) for p, o in zip(pri, ops)]
+    pred = [list(o["deps"]) for o in ops]
+    cost = [o["cost"] for o in ops]
+    hold = [o["cost"] if o["kind"] == "c" else 0.0 if o["e"] == "R" else 0.3 for o in ops]
+
+    def gap(j, i):
+        if ops[j]["e"] == ops[i]["e"] and ops[j]["kind"] == "c":
+            return COST["self"] if ops[i]["e"] != "P" else 1e-6
+        return COST["hop"]
+
+    def sweep(rank, back):
+        before, after = (succ, pred) if back else (pred, succ)
+        left = [len(x) for x in before]
+        t0 = [0.0] * n
+        busy = {e: [] for e in "VSPGYR"}
+        pool = sorted((rank[i], i) for i in range(n) if not left[i])
+        while pool:
+            i = pool.pop()[1]
+            t = max([t0[j] + cost[j] + (gap(i, j) if back else gap(j, i)) for j in before[i]] + [0.0])
+            lead = cost[i] - hold[i] if back else 0.0
+            t += lead
+            b = busy[ops[i]["e"]]
+            k = len(b)
+            while k and b[k - 1][1] > t:
+                k -= 1
+            fit = hold[i] - (COST["tol"] if hold[i] > 0.8 else 0.0)
+            while k < len(b) and b[k][0] < t + fit:
+                t = max(t, b[k][1])
+                k += 1
+            if hold[i]:
+                b.insert(k, (t, t + fit))
+            t0[i] = t - lead
+            for j in after[i]:
+                left[j] -= 1
+                if not left[j]:
+                    x = (rank[j], j)
+                    k = len(pool)
+                    while k and pool[k - 1] > x:
+                        k -= 1
+                    pool.insert(k, x)
+        return t0
+
+    best = None
+    rank = pri
+    for _ in range(COST["rounds"]):
+        t0 = sweep(rank, False)
+        end = max(t0[i] + cost[i] for i in range(n))
+        if best is None or end < best[0]:
+            best = (end, t0)
+        tb = sweep([t0[i] + cost[i] for i in range(n)], True)
+        rank = [tb[i] + cost[i] for i in range(n)]
+    for o, t in zip(ops, best[1]):
+        o["t0"], o["t1"] = t, t + o["cost"]
+    return sorted(range(n), key=lambda i: (best[1][i], i))
+
+
+def first_order(ops):
+    n = len(ops)
+    succ = [[] for _ in range(n)]
+    end = {}
+    for i, o in enumerate(ops):
+        end[o["key"][-1]] = i
+        for j in o["deps"]:
+            succ[j].append(i)
+    pri = []
+    for i, o in enumerate(ops):
+        k = o["key"][:-2] + (".0" if o["key"][-1] == "0" else "")
+        pri.append(end[o["key"][-1]] + LATE.index(k) / 100 + i / 1e6 if k in LATE and o.get("late", True) else i)
+    for i in range(n - 1, -1, -1):
+        if ops[i]["key"] in LAZY:
+            pri[i] = min([pri[k] for k in succ[i]] + [n]) - 1e-3
+    left = [len(o["deps"]) for o in ops]
+    ready = [0.0] * n
+    free = {e: 0.0 for e in "VSPGYR"}
+    pool = {e: [] for e in "VSPGYR"}
+    for i, o in enumerate(ops):
+        if not left[i]:
+            pool[o["e"]].append(i)
+    seq = []
+    while len(seq) < n:
+        cand = []
+        for e in pool:
+            if pool[e]:
+                now = max(free[e], min(ready[i] for i in pool[e]))
+                i = min((i for i in pool[e] if ready[i] <= now + COST["look"]), key=lambda i: pri[i])
+                wide = ops[i]["kind"] == "c" and ops[i]["cost"] > 0.5 and e != "P"
+                if wide:
+                    i = min((k for k in pool[e] if ready[k] <= now + ops[i]["cost"] - COST["tol"] or k == i), key=lambda k: pri[k])
+                cand.append((now + (COST["wait"] if wide else 0.0), now, e, i))
+        _, now, e, i = min(cand)
+        pool[e].remove(i)
+        o = ops[i]
+        t0 = max(now, ready[i])
+        t1 = t0 + o["cost"]
+        free[e] = t1 if o["kind"] == "c" else t0 + (0.0 if e == "R" else 0.3)
+        seq.append(i)
+        for k in succ[i]:
+            same = ops[k]["e"] == e and o["kind"] == "c"
+            ready[k] = max(ready[k], t1 + ((COST["self"] if e != "P" else 0.0) if same else COST["hop"]))
+            left[k] -= 1
+            if not left[k]:
+                pool[ops[k]["e"]].append(k)
+    return seq
+
+
+def polish(ops, seq, sets, steps):
+    n = len(ops)
+    qs = "VSPGYR"
+    en = [qs.index(o["e"]) for o in ops]
+    full = [o["kind"] == "c" for o in ops]
+    pred = [list(o["deps"]) for o in ops]
+    pset = [set(x) for x in pred]
+    tabs = []
+    for cost, c, w in sets:
+        dl = [[(j, (c["self"] if en[i] != 2 else 0.0) if en[j] == en[i] and full[j] else c["hop"]) for j in pred[i]] for i in range(n)]
+        tabs.append((cost, [cost[i] if full[i] else 0.0 if en[i] == 5 else 0.3 for i in range(n)], dl, w))
+
+    def play(s, tab, trace=False):
+        cost, hold, dl, _ = tab
+        free, last = [0.0] * 6, [-1] * 6
+        t1, why = [0.0] * n, [-1] * n
+        for i in s:
+            e = en[i]
+            t, y = free[e], last[e]
+            for j, d in dl[i]:
+                u = t1[j] + d
+                if u >= t:
+                    t, y = u, j
+            t1[i] = t + cost[i]
+            free[e] = t + hold[i]
+            last[e] = i
+            why[i] = y
+        return (t1, why) if trace else max(t1)
+
+    def worth(s):
+        return sum(play(s, tab) * tab[3] for tab in tabs)
+    seed = [12345]
+
+    def rnd(k):
+        seed[0] = (seed[0] * 1103515245 + 12345) % 2147483648
+        return (seed[0] >> 8) % k
+    cur = best = worth(seq)
+    keep = seq
+    pairs = None
+    for it in range(steps):
+        if pairs is None or it % 8 == 0:
+            t1, why = play(seq, tabs[rnd(len(tabs))], True)
+            i = max(range(n), key=lambda x: t1[x])
+            pairs = []
+            while why[i] >= 0:
+                if why[i] not in pset[i]:
+                    pairs.append((why[i], i))
+                i = why[i]
+            if not pairs:
+                break
+        j, i = pairs[rnd(len(pairs))]
+        a, b = seq.index(j), seq.index(i)
+        if a >= b:
+            continue
+        far = rnd(4) if rnd(2) else 0
+        if rnd(2):
+            while far and a > 0:
+                a -= 1
+                far -= en[seq[a]] == en[i]
+            need, up = set(pred[i]), [i]
+            for x in reversed(seq[a:b]):
+                if x in need:
+                    up.append(x)
+                    need |= pset[x]
+            if j in need:
+                continue
+            u = set(up)
+            new = seq[:a] + up[::-1] + [x for x in seq[a:b] if x not in u] + seq[b + 1:]
+        else:
+            while far and b < n - 1:
+                b += 1
+                far -= en[seq[b]] == en[j]
+            down = {j}
+            for x in seq[a + 1:b + 1]:
+                if pset[x] & down:
+                    down.add(x)
+            if i in down:
+                continue
+            part = seq[a:b + 1]
+            new = seq[:a] + [x for x in part if x not in down] + [x for x in part if x in down] + seq[b + 1:]
+        w = worth(new)
+        if w <= cur + 0.004 * (1 - it / steps) * rnd(100) / 100:
+            seq, cur, pairs = new, w, None
+            if w < best:
+                best, keep = w, new
+    t1, _ = play(keep, tabs[0], True)
+    for i, o in enumerate(ops):
+        o["t1"] = t1[i]
+        o["t0"] = t1[i] - o["cost"]
+    return keep
+
+
+def plan(g, core, T, topo):
+    sets = []
+    for ch, w in SPREAD:
+        c = dict(COST)
+        c.update(ch)
+        sets.append(([o["cost"] for o in build(g, core, T, topo, c)], c, w))
+    ops = build(g, core, T, topo, COST)
+    hazards(ops)
+    if "seq" not in MEMO:
+        MEMO["seq"] = polish(ops, first_order(ops), sets, COST["steps"])
+        MEMO["t"] = [(o["t0"], o["t1"]) for o in ops]
+    for o, t in zip(ops, MEMO["t"]):
+        o["t0"], o["t1"] = t
+    return ops, MEMO["seq"]
+
+
+def emit(g, T, ops, seq):
+    eng = {"V": g.vector, "S": g.scalar, "P": g.tensor, "G": g, "Y": g.sync}
+    known = {e: {} for e in eng}
+    count = {}
+    for i in seq:
+        o = ops[i]
+        e = o["e"]
+        if o["kind"] == "r":
+            o["tok"], o["clock"] = ("r_" + o["name"], o["cnt"]), {}
+            count[o["tok"][0]] = o["cnt"]
+            continue
+        kn = known[e]
+        for j in sorted(o["deps"], key=lambda j: -ops[j]["t1"]):
+            d = ops[j]
+            if d["e"] == e == "P":
+                continue
+            s, v = d["tok"]
+            if kn.get(s, 0) >= v:
+                continue
+            eng[e].wait_ge(T.sem[s], v)
+            kn[s] = v
+            for s2, v2 in d["clock"].items():
+                kn[s2] = max(kn.get(s2, 0), v2)
+        r = o["fn"]()
+        if o["kind"] == "c":
+            s = "e" + e
+            count[s] = count.get(s, 0) + 1
+            r.then_inc(T.sem[s], 1)
+        elif o["kind"] == "d":
+            s = "d_" + o["name"]
+            for x in r:
+                x.then_inc(T.sem[s], 16)
+            count[s] = 16 * len(r)
+        else:
+            s = "s_" + o["name"]
+            count[s] = o["cnt"]
+        o["tok"], o["clock"] = (s, count[s]), dict(kn)
+    seen = {}
+    for kn in known.values():
+        for s, v in kn.items():
+            seen[s] = max(seen.get(s, 0), v)
+    for s, v in count.items():
+        if seen.get(s, 0) < v:
+            g.sync.wait_ge(T.sem[s], v)
+
+
+def rank_program(g, core, T, topo):
+    if T.rank_of(core) is None:
+        return
+    ops, seq = plan(g, core, T, topo)
+    emit(g, T, ops, seq)

@@ -1,98 +1,95 @@
-from concourse.bass import DstId, RemoteDMATransfer
 from concourse.mybir import AluOpType as OP, ActivationFunctionType as AF
 
 N, V, C, STEP, TV = 4, 4096, 256, 995, 4
-DUM0 = 4112
-WW = DUM0 + C
+WW = V + C + 16
 BF, F32, I32, U16 = "bfloat16", "float32", "int32", "uint16"
 
-SB = {
-    "X": (V, BF), "F1": (V, BF), "F2": (V, BF), "F3": (V, BF), "F4": (V, BF),
-    "TW": (2 * V, BF), "LT": (V, BF), "CCT": (V, BF), "QW0": (WW, BF), "QW1": (WW, BF),
-    "IOT": (V, F32), "CIW": (V, F32), "DA": (V, BF), "RA": (V, BF), "DB": (V, BF), "RB": (V, BF), "SG": (V, BF),
-    "PLo": (256, I32), "PLp": (256, I32), "CCo": (256, I32), "IA": (256, I32), "IB": (256, I32), "IC": (256, I32), "ID": (256, I32), "IE": (512, I32),
-    "FA": (256, F32), "FB": (256, F32), "FC": (256, F32), "FD": (256, F32), "DM": (256, F32), "CIL": (256, F32),
-    "CHL": (512, BF), "OWN": (512, BF), "P2": (256, U16), "PT": (256, U16), "SO": (256, U16), "CIo": (256, U16), "CIp": (256, U16),
-    "QO": (256, U16), "QI2": (256, U16), "QI3": (256, U16), "QI4": (256, U16),
-    "NF": (256, F32), "NC": (256, F32), "NHL": (512, BF), "NO": (256, U16),
-    "LO": (256, U16), "LHL": (512, BF), "E1": (256, BF), "E2": (256, BF),
-    "FR": (256, BF), "CS": (272, BF), "LK": (256, F32), "CAND": (V, BF),
-    "DL": (8, F32), "RJ": (256, F32), "RHO": (256, F32), "CT": (16, F32), "RK": (256, F32),
-    "L1": (256, BF), "L2": (256, BF), "L3": (256, BF), "HO": (16, U16), "CO": (16, U16), "CB": (16, BF), "WO": (16, U16), "INV": (256, BF),
-    "NW": (256, F32), "NWT": (256, F32), "NLF": (16, F32), "NOF": (16, U16), "QG": (256, BF), "QC": (16, U16),
-    "EQ": (1920, BF), "ED": (256, BF), "EE": (256, BF), "LF": (256, BF), "TO": (64, F32),
-    "VAL": (256, BF), "OFF": (32, U16), "VI2": (256, BF), "VI3": (256, BF), "VI4": (256, BF),
-    "OI2": (32, U16), "OI3": (32, U16), "OI4": (32, U16),
-    "PI": (8, I32), "COL": (32, F32), "B": (144, BF), "BSEL": (144, BF), "BOUT": (144, BF), "B0": (144, BF), "B2": (144, BF),
-    "BQ": (144, BF), "B256": (144, BF),
-    "IDN": (128, BF), "IDF": (128, F32), "I2": (128, BF), "NI": (128, BF), "N2": (128, BF), "I64": (128, BF), "IBIG": (128, BF), "NBIG": (128, BF),
-    "U": (128, BF), "W": (128, BF), "ONES": (128, BF), "NEG": (128, BF), "TLE": (128, BF), "SUM2": (128, BF),
-    "MB": (512, BF),
-    "TRI": (256, F32), "REP": (16, U16), "DUM": (16, F32), "M1": (256, BF), "Y0": (256, F32),
+WIDE = {"X": (V, BF), "F1": (V, BF), "F2": (V, BF), "F3": (V, BF), "F4": (V, BF), "TW": (2 * V + 128, BF), "LT": (V, BF),
+        "QW0": (WW, BF), "QW1": (WW, BF), "IT": (V, F32), "CIW": (V, F32), "BB": (V, BF), "RB": (V, BF), "UU": (V, BF), "UR": (V, BF),
+        "XM": (V, BF), "CAND": (V + 16, BF)}
+SMALL = {
+    "PLo": (256, I32), "PLp": (256, I32), "CCo": (256, I32), "IA": (256, I32), "IB": (256, I32), "IC": (256, I32), "IE": (512, I32), "PI": (16, I32),
+    "IOT": (256, F32), "FA": (256, F32), "FB": (256, F32), "FC": (256, F32), "FD": (256, F32), "DM": (256, F32), "CIL": (256, F32),
+    "NF": (256, F32), "NC": (256, F32), "LK": (256, F32), "DL": (16, F32), "RHO": (256, F32), "CT": (16, F32), "RK": (256, F32),
+    "NW": (256, F32), "NWT": (256, F32), "NLF": (32, F32), "TO": (32, F32), "COL": (16, F32), "ROW": (16, F32), "LOW": (16, F32), "LC": (32, F32),
+    "IDF": (128, F32), "TRI": (256, F32), "Y0": (256, F32),
+    "P2": (256, U16), "PT": (256, U16), "SO": (256, U16), "CIo": (256, U16), "CIp": (256, U16), "QO": (256, U16),
+    "QI2": (256, U16), "QI3": (256, U16), "QI4": (256, U16), "NO": (256, U16), "LO": (256, U16), "HO": (16, U16), "CO": (16, U16), "WO": (16, U16),
+    "NU": (256, U16), "QC": (16, U16), "SPC": (32, U16), "SI2": (32, U16), "SI3": (32, U16), "SI4": (32, U16),
+    "OFF": (32, U16), "OI2": (32, U16), "OI3": (32, U16), "OI4": (32, U16), "REP": (16, U16),
+    "CHL": (512, BF), "OWN": (512, BF), "NHL": (512, BF), "LHL": (768, BF), "E1": (256, BF), "SGN": (256, BF), "FR": (512, BF), "CS": (272, BF),
+    "L1": (256, BF), "L2": (256, BF), "L3": (256, BF), "CB": (16, BF), "TRB": (256, BF), "OUT4": (128, BF), "QG": (256, BF), "EQ": (1920, BF),
+    "ED": (256, BF), "EE": (256, BF), "LF": (256, BF), "VAL": (256, BF), "VI2": (256, BF), "VI3": (256, BF), "VI4": (256, BF),
+    "BS": (256, BF), "BT": (256, BF), "XS": (256, BF), "XT": (256, BF), "US": (256, BF), "VJ": (256, BF), "K16": (256, BF), "DUMW": (256, BF), "M1": (256, BF),
+    "B": (144, BF), "BH": (144, BF), "BSEL": (144, BF), "BOUT": (144, BF), "B0": (144, BF), "BQ": (144, BF), "B256": (144, BF),
+    "IDN": (128, BF), "I2": (128, BF), "NI": (128, BF), "N2": (128, BF), "I32": (128, BF), "IBIG": (128, BF), "NBIG": (128, BF),
+    "ONES": (128, BF), "ONEB": (128, BF), "NEG": (128, BF), "TLE": (128, BF), "SUM2": (128, BF), "MB": (512, BF),
 }
-SCRATCH = {k: ("sbuf", [128, n], d) for k, (n, d) in SB.items()}
-SCRATCH["NI3"] = ("sbuf", [128, 2, 128], I32)
+SB = dict(WIDE)
+SB.update(SMALL)
+HOME, _fill = {k: (k, 0) for k in WIDE}, {}
+for _k, (_n, _d) in SMALL.items():
+    HOME[_k] = ("S" + _d, _fill.get(_d, 0))
+    _fill[_d] = _fill.get(_d, 0) + _n
+SCRATCH = {k: ("sbuf", [128, n], d) for k, (n, d) in WIDE.items()}
+for _d, _n in _fill.items():
+    SCRATCH["S" + _d] = ("sbuf", [128, _n], _d)
+SCRATCH["NI3"] = ("sbuf", [128, 8, 32], I32)
 SCRATCH["CCD"] = ("dram", [128, 512], BF)
 SCRATCH["LD"] = ("dram", [3, 128, 512], BF)
+SCRATCH["FD1"] = ("dram", [3, 128, 256], BF)
+SCRATCH["FD2"] = ("dram", [3, 128, 512], BF)
 SCRATCH["FD3"] = ("dram", [3, 128, 256], BF)
+SCRATCH["LD3"] = ("dram", [3, 128, 768], BF)
 for _b in range(8):
     SCRATCH["PS%d" % _b] = ("psum", [128, 512], F32)
 
-MSGS = ["pl", "cc", "f1", "f2", "f3", "ci"] + ["%s%d" % (m, t) for t in (2, 3, 4) for m in ("lh", "fr", "qo", "va", "of", "oq")]
-LOCAL = ["pl", "cc", "nm", "x", "fo", "cct", "cil", "own", "nxt", "yn", "yp"] + ["%s%d" % (m, t) for t in (2, 3, 4, 5) for m in ("lt", "ft")] \
+MSGS = ["pl", "cc", "f1", "f2", "f3", "ci"] + ["%s%d" % (m, t) for t in (2, 3, 4) for m in ("lh", "fr", "fc", "qo", "va", "si", "of")]
+LOCAL = ["pl", "cc", "nm", "x", "xm", "fo", "cct", "cil", "own", "nxt", "yn", "yp0", "yp1"] + ["%s%d" % (m, t) for t in (2, 3, 4, 5) for m in ("lt", "ft", "fd")] \
     + ["nr%d" % t for t in (1, 2, 3, 4)]
 SEMAPHORES = ["eV", "eS", "eP", "eG"] + ["r_" + m for m in MSGS] + ["s_" + m for m in MSGS] + ["d_" + m for m in LOCAL]
 
 CFG = {
-    "q": {1: "VSSSSSSS", 2: "SSSSSSSS", 3: "SSSSSSSS", 4: "SSSSSSSS"},
-    "t": {2: "SSSSSSSS", 3: "SSSSSSSS", 4: "SSSSSSSS"},
-    "bg": {1: "SSSSSSSS", 2: "VVVVVVVV", 3: "VVVVVVVV", 4: "VVVVVVVV"},
-    "ba": {1: "SSSSSSSS", 2: "SSSSSSSS", 3: "SSSSSSSS", 4: "SSSSSSSS"},
-    "aa": {1: "SSSSSVSV", 2: "SSSSSVSV", 3: "SSSSSVSV", 4: "SSSSSVSV"},
-    "ag": {1: "VVVVVVVV", 2: "VVVVVVVV", 3: "VVVVVVVV", 4: "VVVVVVVV"},
-    "cm": {1: "SSSS", 2: "SSSS", 3: "SSSS", 4: "SSSS"},
-    "fin": "SSSSSSSS",
-    "at": (0, 1),
-    "vg": "S", "qg": "S",
+    "q": {t: "SSSSSSSS" for t in (1, 2, 3, 4)},
+    "t": {t: "SSSSSSSS" for t in (2, 3, 4)},
+    "b": {t: "SSSSSSSS" for t in (1, 2, 3, 4)},
+    "way": {1: "PPPPPPPP", 2: "DDPPPPPP", 3: "DDPPPPPP", 4: "DDPPPPPP"},
+    "ba": {t: "SSSSSSSS" for t in (1, 2, 3, 4)},
+    "aa": {t: "SSSSSSSS" for t in (1, 2, 3, 4)},
+    "cm": {1: "SSSV", 2: "SSSV", 3: "SSSV", 4: "SSSV"},
+    "fin": "SSSS",
+    "nc": "P", "ws": 1, "cie": 3, "sc": (0, 32, 96, 192, 256), "nwt": "V", "fat": (1, 3), "fo": 2, "qc": 8, "banks": (0, 1), "sp": 2, "acc": False, "early2": False, "pf": 1, "tw": "V", "lt": "V", "it": "G",
 }
-COST = {"cy": 0.00104, "g": 1.55, "s": 3.5, "fix": 0.06, "pe": 0.00052, "hop": 0.12, "self": 0.08,
-        "dma": 2.0, "rem": 2.5, "bw": 150e3, "rounds": 1, "steps": 24000, "tol": 0.2, "look": 0.15, "wait": 0.5}
-SPREAD = [({}, 2 / 170), ({"cy": 0.0009, "g": 1.15, "s": 2.0, "pe": 0.00045}, 1 / 130),
-          ({"cy": 0.00115, "g": 1.95, "s": 5.2, "pe": 0.0008, "hop": 0.2, "dma": 2.5, "rem": 3.2}, 1 / 230)]
+COST = {"cy": 0.0009, "g": 1.3, "s": 2.5, "fix": 0.06, "pe": 0.00045, "hop": 0.12, "self": 0.08,
+        "dma": 2.0, "rem": 2.5, "bw": 150e3, "steps": 240000}
+SPREAD = [({}, 1 / 130), ({"hop": 0.25, "self": 0.12, "dma": 2.6, "rem": 3.4, "g": 1.2, "s": 3.5}, 1 / 160),
+          ({"cy": 0.00085, "g": 1.1, "s": 2.0, "dma": 1.6, "rem": 2.0, "pe": 0.00055}, 1 / 135),
+          ({"cy": 0.00115, "g": 1.95, "s": 5.2, "pe": 0.0007, "hop": 0.2, "dma": 2.5, "rem": 3.2}, 1 / 210)]
 MEMO = {}
-SHIFT = {}
-GOALS = ["Gcc.0", "Gpl.0", "VPT.0", "VP2.0", "Gf1.0", "VNO.0", "SQW1.0", "SDB.0", "VTW.0", "SRB.0", "SCIW.0"]
-for _t in range(1, TV + 1):
-    GOALS += ["VLO.%d" % _t, "Gqo%d.%d" % (_t + 1, _t if _t > 1 else 0), "VQO.%d" % _t, "Glh%d.%d" % (_t + 1, _t), "VFR.%d" % _t,
-              "Gfr%d.%d" % (_t + 1, _t), "Gci.0", "VDL.%d" % _t, "VNO.%d" % _t, "Gof%d.%d" % (_t + 1, _t), "VOFF.%d" % _t,
-              "Goq%d.%d" % (_t + 1, _t), "STW.%d" % _t, "SDB.%d" % _t, "VDB.%d" % _t, "SRB.%d" % _t, "VRB.%d" % _t,
-              "SQW%d.%d" % ((_t + 1) % 2, _t)]
-GOALS = list(dict.fromkeys(GOALS))
-LATE = ["STW", "VTW", "SDB", "VDB", "PPS0", "PPS1", "SRB", "VRB", "SQW0", "SQW1", "VQW0", "VQW1", "VNHL", "GTW.0", "SCIW.0", "Gf2.0", "Gf3.0", "GCAND.0", "VQO.0"]
-LAZY = [x + ".0" for x in "VCOL VBSEL VB VBOUT VB0 VBBIG VB256 VB2 VIDN VI2 VNI VN2 VI64 VIBIG VNBIG VU VW VONES VNEG VSUM2 VTLE VMB SPS2 VTRI VREP "
-        "VDUM VOWN VM1 VCS VQW0 GNW GTO GOWN VBQ VIDF VLT VPI".split()]
 
 
 def build(g, core, T, topo, COST=COST):
     q = T.rank_of(core)
     ops = []
-    phase = [0, False]
+    phase = [0]
     cy, G, S, FIX = COST["cy"], COST["g"], COST["s"], COST["fix"]
     eng = {"V": g.vector, "S": g.scalar, "P": g.tensor, "G": g, "Y": g.sync}
+    ROWS = ("LT", "CAND")
 
     def a(name, lo=0, hi=None, st=None):
-        n = 512 if name[:2] == "PS" else SB[name][0]
-        hi = n if hi is None else hi
-        ap = T[name][:, lo:hi] if st is None else T[name][:, lo:hi:st]
+        ps = name[:2] == "PS"
+        hi = (512 if ps else SB[name][0]) if hi is None else hi
+        ten, at = (name, 0) if ps else HOME[name]
+        ap = T[ten][:, at + lo:at + hi] if st is None else T[ten][:, at + lo:at + hi:st]
         cnt = hi - lo if st is None else (hi - lo + st - 1) // st
-        two = name[:2] != "PS" and SB[name][1] in (BF, U16)
-        return {"ap": ap, "reg": [(name, lo, hi)], "n": cnt, "two": two, "ps": name[:2] == "PS", "ind": False}
+        two = not ps and SB[name][1] in (BF, U16)
+        return {"ap": ap, "reg": [(name, 0, 16) if name in ROWS else (name, lo, hi)], "n": cnt, "two": two, "ps": ps, "ind": False}
 
     def ind(win, off):
         return {"ap": win["ap"].indirect(off["ap"]), "reg": win["reg"], "off": off["reg"], "n": 16 * off["n"],
                 "two": False, "ps": False, "ind": True}
 
-    def add(e, fn, outs, ins, cost, kind="c", name=None):
+    def add(e, fn, outs, ins, cost, kind="c", name=None, hold=None):
         r, w = [], []
         for x in ins:
             if isinstance(x, dict):
@@ -100,8 +97,8 @@ def build(g, core, T, topo, COST=COST):
         for x in outs:
             w += x["reg"]
             r += x.get("off", [])
-        ops.append({"e": e, "fn": fn, "r": r, "w": w, "cost": cost, "kind": kind, "name": name,
-                    "key": "%s%s.%d" % (e, name or w[0][0], phase[0]), "late": phase[0] == 0 or phase[1]})
+        ops.append({"e": e, "fn": fn, "r": r, "w": w, "cost": cost, "kind": kind, "name": name, "hold": cost if hold is None else hold,
+                    "key": "%s%s.%d" % (e, name or w[0][0], phase[0])})
 
     def val(x):
         return x["ap"] if isinstance(x, dict) else x
@@ -127,11 +124,13 @@ def build(g, core, T, topo, COST=COST):
     def ms(o, c):
         add("V", lambda: g.vector.memset(o["ap"], c), [o], [], vcost(o, o, 0.5 if o["two"] else 1))
 
-    def act(o, i, f, bias=None):
-        if bias is None:
-            add("S", lambda: g.scalar.activation(o["ap"], i["ap"], f), [o], [i], vcost(o, i, 1))
-        else:
-            add("S", lambda: g.scalar.activation(o["ap"], i["ap"], f, bias=bias), [o], [i], vcost(o, i, 1))
+    def act(o, i, f, bias=None, scale=None):
+        kw = {}
+        if bias is not None:
+            kw["bias"] = val(bias)
+        if scale is not None:
+            kw["scale"] = val(scale)
+        add("S", lambda: g.scalar.activation(o["ap"], i["ap"], f, **kw), [o], [i, bias, scale], vcost(o, i, 1))
 
     def mm(items, first=True, last=True):
         def fn():
@@ -156,24 +155,30 @@ def build(g, core, T, topo, COST=COST):
         else:
             add("G", lambda: g.iota(o["ap"], pat, base, cm, allow_small_or_imprecise_dtypes=True), [o], [], 0.13 + 2 * cy * o["n"])
 
-    def clear(name, n, when):
-        for lo in range(0, n, 512):
-            hi = min(n, lo + 512)
-            iota(a(name, lo, hi), [[0, hi - lo]], 0, 0)
-            ops[-1]["when"] = when
+    def fill(name, lo, hi, c=0):
+        for at in range(lo, hi, 512):
+            n = min(hi - at, 512)
+            iota(a(name, at, at + n), [[0, n]], c, 0)
 
     def dma(e, name, pairs, outs, ins, nbytes):
-        add(e, lambda: [eng[e].dma_start(o, i) for o, i in pairs], outs, ins, COST["dma"] + nbytes / COST["bw"], "d", name)
+        add(e, lambda: [eng[e].dma_start(o, i) for o, i in pairs], outs, ins, COST["dma"] + nbytes / COST["bw"] + 0.1 * len(pairs), "d", name,
+            0.2 + 0.1 * len(pairs))
+
+    def rows(e, name, table, srcs, ins):
+        dma(e, name, [(T[table][r::16, 0:V], s) for r, s in srcs], [reg(table, r, r + 1) for r, _ in srcs], ins, 65536 * len(srcs))
 
     def send(name, step, src, dst_ap, dst_reg, nbytes):
         to = T.cores[(q + step) % N]
         fr = T.cores[(q - step) % N]
         rid, pid, _ = topo.addr(to)
         add("G", lambda: g.remote_dma(dst_ap, src["ap"], T.sem["r_" + name], T.sem["s_" + name], pid, rid, topo.mask(core, to)),
-            [], [src], COST["rem"] + nbytes / COST["bw"], "s", name)
+            [], [src], COST["rem"] + nbytes / COST["bw"], "s", name, 0.3)
         ops[-1]["cnt"] = len(topo.engines(core, to))
         add("R", None, [{"reg": dst_reg}], [], 0.0, "r", name)
         ops[-1]["cnt"] = len(topo.engines(fr, core))
+
+    def sendto(name, src, dst, nbytes, step=1):
+        send(name, step, src, dst["ap"], dst["reg"], nbytes)
 
     def od(mat, i):
         return a(mat, 15 - i, 143 - i)
@@ -181,101 +186,130 @@ def build(g, core, T, topo, COST=COST):
     def pick(out, mat, buf, lo, n):
         return [(out, od(mat, i), a(buf, lo + i, lo + 16 * n, 16)) for i in range(16)]
 
-    def col(k):
-        return a("COL", k, k + 1)
+    def col(k, name="COL"):
+        return a(name, k, k + 1)
 
     def reg(name, lo=0, hi=1 << 20):
         return {"reg": [(name, lo, hi)]}
 
-    dma("Y", "cc", [(T.CCo[:, :], T.cc[:, :])], [a("CCo")], [], 131072)
-    dma("S", "pl", [(T.PLo[:, :], T.pl[:, :])], [a("PLo")], [], 131072)
+    def gather(e, out, win, off):
+        if e == "V":
+            cp(out, ind(win, off))
+        else:
+            act(out, ind(win, off), AF.Identity)
+
+    def wide(cfg, out, win, offs):
+        n = V // len(cfg)
+        for k, e in enumerate(cfg):
+            gather(e, a(out, n * k, n * k + n), a(win), a(offs, n * k // 16, (n * k + n) // 16))
+
+    dma("Y", "cc", [(a("CCo")["ap"], T.cc[:, :])], [a("CCo")], [], 131072)
+    dma("S", "pl", [(a("PLo")["ap"], T.pl[:, :])], [a("PLo")], [], 131072)
     dma("Y", "fo", [(T.F4[:, :], T.fo[:, :])], [a("F4")], [], 1 << 20)
-    dma("Y", "nm", [(T.NI3[:, :, 16 * k:16 * k + 16], T.nm[k]) for k in range(8)], [reg("NI3")], [], 600000)
+    dma("Y", "nm", [(T.NI3[:, k, :], T.nm[k]) for k in range(8)], [reg("NI3")], [], 400000)
     dma("Y", "x", [(T.X[:, :], T.tx[:, :])], [a("X")], [], 1 << 20)
-    ms(a("CCT"), 0.0)
-    iota(a("IOT", 0, 256), [[1, 256]], 1, 0)
     iota(a("PI", 0, 1), [[0, 1]], 0, 1)
+    iota(a("IOT"), [[1, 256]], 1, 0)
     iota(col(0), [[0, 1]], 1, 1)
-    for n in (256, 512, 1024, 2048):
-        act(a("IOT", n, 2 * n), a("IOT", 0, n), AF.Identity, float(n))
+    if CFG["it"] == "G":
+        for n in range(0, V, 512):
+            iota(a("IT", n, n + 512), [[1, 32], [256, 16]], 1 + n // 16, 0)
+    else:
+        iota(a("IT", 0, 256), [[1, 16], [256, 16]], 1, 0)
+        for n in (256, 512, 1024, 2048):
+            act(a("IT", n, 2 * n), a("IT", 0, n), AF.Identity, float(n // 16))
     ts(a("IE", 0, 256), a("CCo"), 4, OP.logical_shift_right)
     ts(a("IE", 256, 512), a("CCo"), 15, OP.bitwise_and)
     cp(a("CHL", 0, 256), a("IE", 0, 256))
     ts(a("CHL", 256, 512), a("IE", 256, 512), 256.0, OP.mult)
     send("cc", 1, a("CHL"), T.CCD[:, :], [("CCD", 0, 512)], 131072)
-    send("pl", 1, a("PLo"), T.PLp[:, :], a("PLp")["reg"], 131072)
-    for t in (1, 2, 3):
-        send("f%d" % t, t, a("F4"), T["F%d" % t][:, :], a("F%d" % t)["reg"], 1 << 20)
-    dma("Y", "cct", [(T.CCT[2::16, :], T.CCD[:, 0:256]), (T.CCT[3::16, :], T.CCD[:, 256:512])], [a("CCT")], [reg("CCD")], 131072)
-    clear("TW", V, 1.5)
-    clear("CAND", V, 12.0)
-    dma("Y", "nxt", [(T.CAND[2::16, :], T.CHL[:, 0:256]), (T.CAND[3::16, :], T.CHL[:, 256:512])], [a("CAND")], [a("CHL")], 131072)
+    sendto("pl", a("PLo"), a("PLp"), 131072)
+    sendto("f1", a("F4"), a("F1"), 1 << 20)
 
-    ts(a("IC"), a("CCo"), 255, OP.bitwise_and)
-    ts(a("ID"), a("CCo"), 8, OP.logical_shift_right)
-    ts(a("RJ"), a("IC"), 16.0, OP.mult)
-    tt(a("RHO"), a("RJ"), a("ID"), OP.add)
-    cp(a("P2"), a("RHO"))
-    for k in range(4):
-        act(ind(a("CIW"), a("P2", 64 * k, 64 * k + 64)), a("IOT", 1024 * k, 1024 * k + 1024), AF.Silu)
-
-    k128, k144, k256 = a("IOT", 0, 128), a("IOT", 0, 144), a("IOT", 0, 256)
+    k128, k144, k256 = a("IOT", 0, 128), a("IOT", 0, 144), a("IOT")
     ts(a("PI", 1, 2), a("PI", 0, 1), 15, OP.bitwise_and)
     cp(col(1), a("PI", 1, 2))
-    tt(col(2), col(0), col(1), OP.subtract)
-    ts(col(3), col(2), 15.0, OP.add)
-    ts(col(4), col(1), 0.0, OP.is_equal)
-    ts(col(5), col(1), 2.0, OP.is_lt)
-    ts(col(6), col(1), 3.0, OP.is_equal, 1.0 / 256, OP.mult)
-    ts(col(10), col(1), 2.0, OP.is_equal)
-    ts(col(7), col(10), 16.0, OP.mult, col(6), OP.add)
-    ts(col(8), col(1), 1.0, OP.is_equal)
-    ts(col(9), col(1), 1.0, OP.add)
-    ts(col(22), col(1), 4.0, OP.is_lt, col(5), OP.subtract)
-    ts(col(23), col(1), 4.0, OP.is_equal, -8192.0, OP.mult)
-    ts(col(24), col(23), col(5), OP.add)
-    for nm_, w in (("BQ", col(22)), ("BSEL", col(24)), ("B", 1.0), ("BOUT", col(7)), ("B0", col(10)), ("B256", 256.0)):
-        ts(a(nm_), k144, col(3), OP.is_equal, w, OP.mult)
-    if any("V" in s for s in CFG["cm"].values()):
-        ts(a("B2"), k144, col(3), OP.is_equal, 2.0, OP.mult)
-    ts(a("IDF"), k128, col(0), OP.is_equal)
-    for nm_, w in (("IDN", 1.0), ("I2", 2.0), ("NI", -1.0), ("N2", -2.0), ("I64", 64.0), ("IBIG", 8192.0), ("NBIG", -8192.0)):
-        if (nm_ != "I2" or any("V" in s for s in CFG["ba"].values())) and (nm_ != "N2" or any("V" in s for s in CFG["aa"].values())):
-            ts(a(nm_), k128, col(0), OP.is_equal, w, OP.mult)
-    ts(a("U"), k128, col(2), OP.is_ge)
-    ts(a("W"), k128, col(3), OP.is_le)
-    tt(a("ONES"), a("U"), a("W"), OP.mult)
-    ts(a("NEG"), a("ONES"), -1.0, OP.mult)
-    ts(a("SUM2"), a("ONES"), col(5), OP.mult)
-    ts(a("U"), k128, col(0), OP.is_ge)
-    tt(a("TLE"), a("U"), a("W"), OP.mult)
-    for t in range(1, TV + 1):
-        ts(col(10 + t), col(1), float((STEP * t) % V % 16), OP.is_lt)
-        ts(a("MB", 128 * t - 128, 128 * t), a("ONES"), col(10 + t), OP.mult)
-    act(a("PS2", 256, 512), k256, AF.Identity)
-    iota(a("NW"), [[0, 16], [1, 16]], 0, 0)
-    ts(a("TRI"), a("NW"), col(1), OP.is_gt)
-    ts(a("REP"), a("IOT", 0, 16), -1.0, OP.add)
-    iota(a("TO", 0, 16), [[16, 16]], DUM0, 0)
-    ts(a("DUM"), a("TO", 0, 16), col(1), OP.add)
-    iota(a("FD"), [[16, 256]], V, 0)
-    iota(a("OWN", 0, 256), [[16, 256]], 0, 0)
-    ts(a("OWN", 256, 512), k256, 0.0, OP.mult, col(9), OP.add)
-    ms(a("M1"), -1.0)
-    ms(a("CS", 0, 1), 0.0)
-    ms(a("CS", 257, 258), 16.0)
-    ms(a("QW0", 0, 1), 0.0)
-    ms(a("QW1", 0, 1), 0.0)
-    ts(a("LT", 0, 64), a("IOT", 0, 64), col(8), OP.mult)
+    ts(a("ROW"), a("IOT", 0, 16), -1.0, OP.add, col(1), OP.is_equal)
+    ts(a("LOW"), a("IOT", 0, 16), -1.0, OP.add, col(1), OP.is_gt)
+
+    def row(r):
+        return col(r, "ROW")
+    ts(a("LC"), a("IOT", 0, 32), row(0), OP.mult, 64.0, OP.mult)
+    ts(a("LT", 0, 64), a("IOT", 0, 64), row(1), OP.mult)
     for k in range(6):
         n = 64 << k
-        ts(col(16 + k), col(4), float(n), OP.mult)
-        ts(a("LT", n, 2 * n), a("LT", 0, n), col(16 + k), OP.add)
+        if CFG["lt"] == "V":
+            ts(a("LT", n, 2 * n), a("LT", 0, n), col(n // 64 - 1, "LC"), OP.add)
+        else:
+            act(a("LT", n, 2 * n), a("LT", 0, n), AF.Identity, col(n // 64 - 1, "LC"))
+    rows("Y", "cct", "LT", [(2, T.CCD[:, 0:256]), (3, T.CCD[:, 256:512])], [reg("CCD")])
+    if CFG["tw"] == "G":
+        fill("TW", 0, V)
+    else:
+        for h in range(2):
+            ms(a("TW", 2048 * h, 2048 * h + 2048), 0.0)
+    fill("CAND", 0, V)
+    rows("Y", "nxt", "CAND", [(2, a("CHL", 0, 256)["ap"]), (3, a("CHL", 256, 512)["ap"])], [a("CHL")])
+    ts(col(2), col(0), col(1), OP.subtract)
+    ts(col(3), col(0), col(1), OP.subtract, 15.0, OP.add)
+    ts(col(4), col(4, "LOW"), col(2, "LOW"), OP.subtract)
+    ts(col(5), row(2), 4096.0, OP.mult, row(3), OP.add)
+    ts(col(6), col(5), 1.0 / 256, OP.mult)
+    ts(col(7), row(5), row(4), OP.subtract, row(6), OP.subtract)
+    ts(col(8), col(7), 8192.0, OP.mult, col(2, "LOW"), OP.add)
+    ts(col(9), row(5), -65536.0, OP.mult, 65537.0, OP.add)
+    ts(col(10), row(5), 65536.0, OP.mult, -65536.0, OP.add)
+    ts(col(11), col(1), 1.0, OP.add)
+    ts(col(12), row(1), float(V), OP.mult)
+    ts(a("B"), k144, col(3), OP.is_equal)
+    for nm_, w in (("BOUT", col(6)), ("BQ", col(4)), ("BSEL", col(8)), ("BH", 0.5), ("B0", row(2)), ("B256", 256.0)):
+        act(a(nm_), a("B"), AF.Identity, None, w)
+    ts(a("IDF"), k128, col(0), OP.is_equal)
+    for nm_, w in (("IDN", 1.0), ("I2", 2.0), ("NI", -1.0), ("N2", -2.0), ("I32", 32.0), ("IBIG", 8192.0), ("NBIG", -8192.0)):
+        act(a(nm_), a("IDF"), AF.Identity, None, w)
+    iota(a("NWT", 0, 128), [[16, 8], [0, 16]], 1, 0)
+    ts(a("ONES"), a("NWT", 0, 128), col(2), OP.is_equal)
+    add("G", lambda: g.affine_select(a("TLE")["ap"], a("ONES")["ap"], [[1, 128]], OP.is_ge, 0.0, 0, -1), [a("TLE")], [a("ONES")], 0.17 + 256 * cy)
+    for nm_, w in (("NEG", -1.0), ("ONEB", 8192.0), ("SUM2", col(2, "LOW"))):
+        act(a(nm_), a("ONES"), AF.Identity, None, w)
+    act(a("OUT4"), a("ONEB"), AF.Identity, None, row(4))
+    act(a("CAND", V, V + 16), a("IOT", 0, 16), AF.Identity, row(4), 0.0)
+    for t in range(1, TV + 1):
+        act(a("MB", 128 * t - 128, 128 * t), a("ONES"), AF.Identity, None, col((STEP * t) % V % 16, "LOW"))
+    iota(a("NW"), [[0, 16], [1, 16]], 0, 0)
+    if CFG["nwt"] == "V":
+        ts(a("TRI"), a("NW"), col(1), OP.is_gt)
+    else:
+        ts(a("TRB"), a("NW"), col(1), OP.is_le)
+    ts(a("REP"), a("IOT", 0, 16), -1.0, OP.add)
+    iota(a("K16"), [[1, 256]], 1, 0)
+    ts(a("DUMW"), a("K16"), row(0), OP.mult, col(12), OP.add)
+    iota(a("FD"), [[16, 256]], V, 1)
+    iota(a("OWN", 0, 256), [[16, 256]], 0, 0)
+    act(a("OWN", 256, 512), a("K16"), AF.Identity, col(11), 0.0)
+    fill("M1", 0, 256, -1)
+    fill("CS", 0, 1)
+    fill("CS", 257, 258, 16)
+    way = CFG["way"][TV]
+    mixed = "A" in way and "P" in way
+    if mixed:
+        dma("Y", "xm", [(T.XM[:, 512 * k:512 * k + 512], T.tx[:, 512 * k:512 * k + 512]) for k in range(8) if way[k] == "A"],
+            [a("XM", 512 * k, 512 * k + 512) for k in range(8) if way[k] == "A"], [], 131072 * way.count("A"))
+        for k in range(8):
+            if way[k] == "P":
+                fill("XM", 512 * k, 512 * k + 512)
+
+    tt(a("RHO"), a("CHL", 0, 256), a("CHL", 256, 512), OP.add)
+    cp(a("P2"), a("RHO"))
+    for k in range(8):
+        act(ind(a("CIW"), a("P2", 32 * k, 32 * k + 32)), a("IT", 512 * k, 512 * k + 512), AF.Silu)
+        if k < CFG["cie"]:
+            ops[-1]["lead"] = 40.0
 
     for h in range(2):
-        add("V", lambda h=h: g.vector.tensor_scalar(T.NF[:, 128 * h:128 * h + 128], T.NI3[:, h, :], 1.0, None, OP.add),
+        add("V", lambda h=h: g.vector.tensor_scalar(a("NF", 128 * h, 128 * h + 128)["ap"], T.NI3[:, :, 16 * h:16 * h + 16], 1.0, None, OP.add),
             [a("NF", 128 * h, 128 * h + 128)], [reg("NI3")], FIX + 128 * cy)
-        add("P", lambda h=h: g.tensor.transpose(T.PS7[:, 128 * h:128 * h + 128], T.NF[:, 128 * h:128 * h + 128], T.IDF[:, :]),
+        add("P", lambda h=h: g.tensor.transpose(T.PS7[:, 128 * h:128 * h + 128], a("NF", 128 * h, 128 * h + 128)["ap"], a("IDF")["ap"]),
             [a("PS7")], [a("NF", 128 * h, 128 * h + 128), a("IDF")], FIX + 512 * COST["pe"])
     for h in range(2):
         cp(a("NC", h, 256, 2), a("PS7", 128 * h, 128 * h + 128))
@@ -287,276 +321,360 @@ def build(g, core, T, topo, COST=COST):
         tt(a("NHL", 256, 512), a("NC"), a("NHL", 0, 256), OP.subtract)
 
     def name_rows(t):
-        dma("Y", "nr%d" % t, [(T.CAND[0::16, :], T.NHL[:, 0:256]), (T.CAND[1::16, :], T.NHL[:, 256:512])], [a("CAND")], [a("NHL")], 131072)
+        rows("Y", "nr%d" % t, "CAND", [(0, a("NHL", 0, 256)["ap"]), (1, a("NHL", 256, 512)["ap"])], [a("NHL")])
     names(1)
     name_rows(1)
 
-    def tilde(src, out):
-        ts(a("IA"), src, 15, OP.bitwise_and)
-        ts(a("IB"), src, 4, OP.logical_shift_right, 255, OP.bitwise_and)
-        ts(a("FA"), a("IA"), 256.0, OP.mult)
-        tt(a("FB"), a("FA"), a("IB"), OP.add)
-        cp(out, a("FB"))
-
-    def gather(e, out, win, off):
-        if e == "V":
-            cp(out, ind(win, off))
-        else:
-            act(out, ind(win, off), AF.Identity)
-
     def hints(t, offs):
-        for k in range(8):
-            gather(CFG["q"][t][k], a("QW%d" % (t % 2), 1 + 512 * k, 513 + 512 * k), a("CCT"), a(offs, 32 * k, 32 * k + 32))
-
-    dbank = [0]
+        wide(CFG["q"][t], "QW%d" % (t % 2), "LT", offs)
 
     def named(t):
         for k in range(8):
             lo, hi = 512 * k, 512 * k + 512
             w, off = a("F%d" % t), a("NO", 32 * k, 32 * k + 32)
-            if CFG["bg"][t][k] == "V":
-                tt(a("DB", lo, hi), ind(w, off), a("X", lo, hi), OP.subtract)
-                if CFG["ba"][t][k] == "V":
-                    ts(a("RB", lo, hi), a("DB", lo, hi), 0.0, OP.max)
-                else:
-                    act(a("RB", lo, hi), a("DB", lo, hi), AF.Abs)
-            else:
-                act(a("DB", lo, hi), ind(w, off), AF.Identity)
-                p = a("PS%d" % (dbank[0] % 2))
-                dbank[0] += 1
-                mm([(p, a("IDN"), a("DB", lo, hi)), (p, a("NI"), a("X", lo, hi))])
+            if CFG["way"][t][k] == "P":
+                gather(CFG["b"][t][k], a("BB", lo, hi), w, off)
+                continue
+            if CFG["way"][t][k] == "D":
+                gather("S", a("BB", lo, hi), w, off)
+                tt(a("RB", lo, hi), ind(w, off), a("X", lo, hi), OP.subtract)
+                continue
+            if CFG["way"][t][k] == "C":
+                gather("S", a("BB", lo, hi), w, off)
+                p = a("PS4")
+                mm([(p, a("IDN"), a("BB", lo, hi)), (p, a("NI"), a("X", lo, hi))])
                 act(a("RB", lo, hi), p, AF.Abs)
+                continue
+            tt(a("BB", lo, hi), ind(w, off), a("X", lo, hi), OP.subtract)
+            if CFG["ba"][t][k] == "V":
+                ts(a("RB", lo, hi), a("BB", lo, hi), 0.0, OP.max)
+            else:
+                act(a("RB", lo, hi), a("BB", lo, hi), AF.Abs)
 
-    tilde(a("PLp"), a("PT"))
+    ts(a("IA"), a("PLp"), 15, OP.bitwise_and)
+    ts(a("IB"), a("PLp"), 4, OP.logical_shift_right, 255, OP.bitwise_and)
+    ts(a("FA"), a("IA"), 256.0, OP.mult)
+    tt(a("FB"), a("FA"), a("IB"), OP.add)
+    cp(a("PT"), a("FB"))
     ts(a("FC"), a("PLp"), 0.0, OP.is_lt)
-    ts(a("FD"), a("FD"), col(1), OP.add)
     tt(a("DM"), a("FC"), a("FD"), OP.mult)
     hints(1, "PT")
-    for k in range(4):
-        p = a("PS%d" % (5 + k % 2), 0, 64)
-        mm(pick(p, "BQ", "QW1", 1 + 1024 * k, 64))
-        tt(a("FC", 64 * k, 64 * k + 64), p, a("DM", 64 * k, 64 * k + 64), OP.max)
-        cp(a("QO", 64 * k, 64 * k + 64), p)
-        cp(a("SO", 64 * k, 64 * k + 64), a("FC", 64 * k, 64 * k + 64))
-        cp(ind(a("TW"), a("SO", 64 * k, 64 * k + 64)), a("LT", 1024 * k, 1024 * k + 1024))
-    send("qo2", 1, a("QO"), T.QI2[:, :], a("QI2")["reg"], 65536)
-    named(1)
-    dma("Y", "cil", [(T.CIL[:, :], T.CIW[0::16, :])], [a("CIL")], [a("CIW")], 131072)
-    ts(a("CIL"), a("CIL"), -1.0, OP.add)
-    cp(a("IC"), a("CIL"))
-    tilde(a("IC"), a("CIo"))
-    send("ci", 1, a("CIo"), T.CIp[:, :], a("CIp")["reg"], 65536)
+    for k, (lo, hi) in enumerate(zip(CFG["sc"], CFG["sc"][1:])):
+        p = a("PS%d" % (5 + k % 2), 0, hi - lo)
+        mm(pick(p, "BOUT", "QW1", 16 * lo, hi - lo))
+        tt(a("FC", lo, hi), p, a("DM", lo, hi), OP.max)
+        cp(a("SO", lo, hi), a("FC", lo, hi))
+        cp(ind(a("TW"), a("SO", lo, hi)), a("LT", 16 * lo, 16 * hi))
+        if k in CFG["fat"]:
+            t = 2 + CFG["fat"].index(k)
+            sendto("f%d" % t, a("F4"), a("F%d" % t), 1 << 20, t)
+            ops[-2]["r"] = ops[-2]["r"] + a("SO", lo, hi)["reg"]
 
+    def pass_hints(t):
+        for h in range(4):
+            items = pick(a("PS4", 64 * h, 64 * h + 64), "BQ", "QW%d" % (t % 2), 1024 * h, 64)
+            for k in range(0, 16, CFG["qc"]):
+                mm(items[k:k + CFG["qc"]], k == 0, k + CFG["qc"] == 16)
+        cp(a("QO"), a("PS4", 0, 256))
+        if t == TV:
+            act(a("SGN"), a("PS4", 0, 256), AF.Identity, 96.0 - 127.5 / 512, 1.0 / 512)
+            act(a("FC"), a("PS4", 0, 256), AF.Identity, 8190.0 * 96, 16.0)
+        if t < TV:
+            sendto("qo%d" % (t + 1), a("QO"), a("QI%d" % (t + 1)), 65536)
+    pass_hints(1)
+    named(1)
+    dma("Y", "cil", [(a("CIL")["ap"], T.CIW[0::16, :])], [a("CIL")], [a("CIW")], 131072)
+    cp(a("IC"), a("CIL"))
+    ts(a("CIo"), a("IC"), -1.0, OP.add)
+    sendto("ci", a("CIo"), a("CIp"), 65536)
+    if CFG["early2"]:
+        hints(2, "QI2")
+
+    def table(t, name, rws, buf, lo, dram):
+        n = 256 * len(rws)
+        if t < TV:
+            send("%s%d" % (name[0], t + 1), 1, a(buf, lo, lo + n), dram[t - 1], [(name[0] + str(t), 0, n)], 256 * n)
+            rows("Y", "%s%d" % (name[1], t + 1), "LT", [(r, dram[t - 1][:, 256 * k:256 * k + 256]) for k, r in enumerate(rws)], [reg(name[0] + str(t))])
+        else:
+            rows("Y", "%s5" % name[1], "LT", [(r, a(buf, lo + 256 * k, lo + 256 * k + 256)["ap"]) for k, r in enumerate(rws)], [a(buf, lo, lo + n)])
+
+    def cut(items, first, last, n):
+        for k in range(0, len(items), n):
+            mm(items[k:k + n], first and k == 0, last and k + n >= len(items))
+
+    acc = CFG["acc"]
+    free, forced = a("FR", 0, 256), a("LHL", 512, 768) if CFG["fo"] == 1 else a("FR", 256, 512)
     for t in range(1, TV + 1):
         phase[0] = t
-        QW = "QW%d" % (t % 2)
+        QW, F = "QW%d" % (t % 2), a("F%d" % t)
         s = (STEP * t) % V
         ca = s // 16
-        if t > 1:
-            cp(ind(a("TW", 0, WW), a("OI%d" % t, 16, 32)), a("VI%d" % t))
-        for h in range(2):
-            lo, hi = 128 * h, 128 * h + 128
-            p = a("PS%d" % (3 + h), 128, 256)
-            mm([(p, od("BSEL", i), a("TW", 256 * i + lo, 256 * i + hi)) for i in range(16)])
-            ts(a("LO", lo, hi), p, -1.0, OP.add, 0.0, OP.max)
-            act(a("LHL", lo, hi), p, AF.Identity)
-            tt(a("LHL", 256 + lo, 256 + hi), p, a("LHL", lo, hi), OP.subtract)
-            tt(a("E1", lo, hi), p, a("NC", lo, hi), OP.is_equal)
-            ts(a("E2", lo, hi), a("LHL", lo, hi), 0.5, OP.is_lt, -1.0, OP.mult)
-        if t < TV:
-            send("lh%d" % (t + 1), 1, a("LHL"), T.LD[t - 1], [("LD%d" % t, 0, 512)], 131072)
-        def pass_hints(step):
-            if step == CFG["at"][0]:
-                cp(ind(a(QW), a("OI%d" % t, 0, 16)), a("VI%d" % t))
-            if 0 <= step - CFG["at"][1] < 4:
-                h = step - CFG["at"][1]
-                mm(pick(a("PS5", 64 * h, 64 * h + 64), "BQ", QW, 1 + 1024 * h, 64))
-            if step == CFG["at"][1] + 3:
-                cp(a("QO"), a("PS5", 0, 256))
-                if t < TV:
-                    send("qo%d" % (t + 1), 1, a("QO"), T["QI%d" % (t + 1)][:, :], a("QI%d" % (t + 1))["reg"], 65536)
-        if t == TV:
-            clear("TW", V + 16, 0.0)
-        if t < TV:
-            dma("Y", "lt%d" % (t + 1), [(T.LT[0::16, :], T.LD[t - 1][:, 0:256]), (T.LT[1::16, :], T.LD[t - 1][:, 256:512])],
-                [a("LT")], [reg("LD%d" % t)], 131072)
-        else:
-            dma("Y", "lt5", [(T.LT[0::16, :], T.LHL[:, 0:256]), (T.LT[1::16, :], T.LHL[:, 256:512])], [a("LT")], [a("LHL")], 131072)
-        for k in range(8):
-            lo, hi = 512 * k, 512 * k + 512
-            w, off = a("F%d" % t), a("LO", 32 * k, 32 * k + 32)
-            if CFG["ag"][t][k] == "V":
-                tt(a("DA", lo, hi), ind(w, off), a("X", lo, hi), OP.subtract)
-            else:
-                act(a("DA", lo, hi), ind(w, off), AF.Identity)
-                p = a("PS%d" % (0, 1, 6, 7)[(k + 2) % 4])
-                mm([(p, a("IDN"), a("DA", lo, hi)), (p, a("NI"), a("X", lo, hi))])
-                act(a("RA", lo, hi), p, AF.Abs)
-            p = a("PS%d" % (6, 7, 0, 1)[k % 4])
-            if CFG["bg"][t][k] == "V" and CFG["ba"][t][k] == "V":
-                items = [(p, a("I2"), a("RB", lo, hi)), (p, a("NI"), a("DB", lo, hi))]
-            else:
-                items = [(p, a("IDN"), a("RB", lo, hi))]
-            if CFG["ag"][t][k] == "S":
-                items += [(p, a("NI"), a("RA", lo, hi))]
-            elif CFG["aa"][t][k] == "V":
-                ts(a("RA", lo, hi), a("DA", lo, hi), 0.0, OP.max)
-                items += [(p, a("IDN"), a("DA", lo, hi)), (p, a("N2"), a("RA", lo, hi))]
-            else:
-                act(a("RA", lo, hi), a("DA", lo, hi), AF.Abs)
-                items += [(p, a("NI"), a("RA", lo, hi))]
-            mm(items)
-            if CFG["cm"][t][k // 2] == "V":
-                ts(a("SG", lo, hi), p, 0.5, OP.is_gt, -0.5, OP.add)
-            else:
-                act(a("SG", lo, hi), p, AF.Sign, -0.5)
-            if t > 1:
-                pass_hints(k)
-            if k % 2:
-                j = k // 2
-                p = a("PS2", 64 * j, 64 * j + 64)
-                mm([(p, a("I64"), a("E1", 64 * j, 64 * j + 64)), (p, a("I64"), a("E2", 64 * j, 64 * j + 64))]
-                   + pick(p, "B2" if CFG["cm"][t][j] == "V" else "B", "SG", 1024 * j, 64))
         votes = a("PS2", 0, 256)
-        ts(a("FR"), votes, 1.0, OP.is_lt)
-        add("V", lambda: g.vector.tensor_tensor_scan(T.CS[:, 1:257], T.FR[:, :], T.FR[:, :], 0.0, OP.add, OP.max),
-            [a("CS", 1, 257)], [a("FR")], FIX + 128 * cy)
-        if t < TV:
-            send("fr%d" % (t + 1), 1, a("FR"), T.FD3[t - 1], [("FD%d" % t, 0, 256)], 65536)
-            dma("Y", "ft%d" % (t + 1), [(T.LT[4::16, :], T.FD3[t - 1])], [a("LT")], [reg("FD%d" % t)], 65536)
+        mm([(votes, a("IDN"), a("M1"))], True, False)
+        for j in range(4):
+            p = a("PS3", 64 * j, 64 * j + 64)
+            mm(pick(p, "BSEL", "TW", 1024 * j, 64))
+            ts(a("LO", 64 * j, 64 * j + 64), p, -1.0, OP.add, 0.0, OP.max)
+            cm, late = CFG["cm"][t][j], []
+            for k in (2 * j, 2 * j + 1):
+                lo, hi = 512 * k, 512 * k + 512
+                u, b, x, p = a("UU", lo, hi), a("BB", lo, hi), a("X", lo, hi), a("PS%d" % CFG["banks"][k % len(CFG["banks"])])
+                listed = ind(F, a("LO", 32 * k, 32 * k + 32))
+                if CFG["way"][t][k] in "PD":
+                    tt(u, listed, b, OP.subtract)
+                    items = [(p, a("I2"), b), (p, a("N2"), x)] if CFG["way"][t][k] == "P" else [(p, a("I2"), a("RB", lo, hi))]
+                    if CFG["ws"]:
+                        mm(items, True, False)
+                        mm([(p, a("IDN"), u)], False, True)
+                    else:
+                        mm(items + [(p, a("IDN"), u)])
+                    tt(u, p, u, OP.mult)
+                    late.append(k)
+                    continue
+                rb, ra = a("RB", lo, hi), a("UR", lo, hi)
+                if CFG["way"][t][k] == "C":
+                    p = a("PS%d" % (6 + k % 2))
+                    act(u, listed, AF.Identity)
+                    mm([(p, a("NI"), x), (p, a("IDN"), u)])
+                    act(ra, p, AF.Abs)
+                    mm([(p, a("IDN"), rb), (p, a("NI"), ra)])
+                else:
+                    tt(u, listed, x, OP.subtract)
+                    mm([(p, a("I2"), rb), (p, a("NI"), b)] if CFG["ba"][t][k] == "V" else [(p, a("IDN"), rb)], True, False)
+                if CFG["way"][t][k] == "C":
+                    pass
+                elif CFG["aa"][t][k] == "V":
+                    ts(ra, u, 0.0, OP.max)
+                    mm([(p, a("IDN"), u), (p, a("N2"), ra)], False, True)
+                else:
+                    act(ra, u, AF.Abs)
+                    mm([(p, a("NI"), ra)], False, True)
+                if cm == "V":
+                    ts(u, p, 0.5, OP.is_gt, -0.5, OP.add)
+                else:
+                    act(u, p, AF.Sign, -0.5)
+            if late:
+                u = a("UU", 512 * late[0], 512 * late[-1] + 512)
+                if cm == "V":
+                    ts(u, u, -0.5, OP.is_lt, -0.5, OP.add)
+                else:
+                    act(u, u, AF.Sign, -0.5, -1.0)
+            mm(pick(a("PS2", 64 * j, 64 * j + 64), "B" if cm == "V" else "BH", "UU", 1024 * j, 64), False, False)
+        lst = a("PS3", 0, 256)
+        act(a("SGN"), lst, AF.Sign, -0.5)
+        last = [(votes, a("I32"), a("SGN"))]
+        if t > 1:
+            VI, SI, OI = a("VI%d" % t), "SI%d" % t, "OI%d" % t
+            p = a("PS4", 256, 512)
+            gather("S", a("XS"), a("X"), a(SI, 16, 32))
+            if "A" in way:
+                gather("S", a("BT"), a("BB"), a(SI, 16, 32))
+                if mixed:
+                    gather("S", a("XT"), a("XM"), a(SI, 16, 32))
+                mm([(p, a("IDN"), a("BT")), (p, a("IDN"), a("XT" if mixed else "XS"))])
+                act(a("BS"), p, AF.Identity)
+            else:
+                gather("S", a("BS"), a("BB"), a(SI, 16, 32))
+            tt(a("US"), ind(F, a(SI, 0, 16)), a("BS"), OP.subtract)
+            mm([(p, a("I2"), a("BS")), (p, a("N2"), a("XS")), (p, a("IDN"), a("US"))])
+            tt(a("US"), p, a("US"), OP.mult)
+            ts(a("US"), a("US"), -0.5, OP.is_lt, -0.5, OP.add)
+            mm([(p, a("IDN"), VI), (p, od("B", 5), a("US"))])
+            ts(a("VJ"), p, col(9), OP.min, col(10), OP.max)
+            cp(ind(a("TW", 0, WW), a(OI, 16, 32)), a("VJ"))
+            lst = a("PS3", 256, 512)
+            for h in range(0, 16, 4):
+                mm(pick(lst, "BSEL", "TW", 0, 256)[h:h + 4], h == 0, h == 12)
+            ts(forced, lst, 8191.5, OP.is_gt)
+            last.append((votes, a("IBIG"), forced))
+        tt(a("E1"), lst, a("NC"), OP.is_equal)
+        mm(last + [(votes, a("IBIG"), a("E1"))], False, True)
+        if t > 1 and acc:
+            mm([(lst, a("NBIG"), forced)], False, True)
+        act(a("LHL", 0, 256), lst, AF.Identity)
+        tt(a("LHL", 256, 512), lst, a("LHL", 0, 256), OP.subtract)
+        ts(free, votes, 31.5, OP.is_lt)
+        if t > 1 and CFG["fo"] == 2:
+            table(t, ("fc", "fd"), (6,), "FR", 256, T.FD3)
+        if t > 1 and CFG["fo"] == 1:
+            table(t, ("lh", "lt"), (0, 1, 6), "LHL", 0, T.LD3)
         else:
-            dma("Y", "ft5", [(T.LT[4::16, :], T.FR[:, :])], [a("LT")], [a("FR")], 65536)
-        p = a("PS6", 0, 256)
-        mm([(p, a("IDN"), a("LHL", 0, 256)), (p, a("IDN"), a("LHL", 256, 512)), (p, a("NBIG"), a("FR"))])
+            table(t, ("lh", "lt"), (0, 1), "LHL", 0, T.LD)
+        add("V", lambda: g.vector.tensor_tensor_scan(a("CS", 1, 257)["ap"], free["ap"], free["ap"], 0.0, OP.add, OP.max),
+            [a("CS", 1, 257)], [free], FIX + 128 * cy)
+        if t > 1 and CFG["fo"] == 0:
+            table(t, ("fr", "ft"), (4, 6), "FR", 0, T.FD2)
+        else:
+            table(t, ("fr", "ft"), (4,), "FR", 0, T.FD1)
+        if t > 1:
+            cp(ind(a(QW), a(OI, 0, 16)), VI)
+            pass_hints(t)
+        if t > 1 and acc:
+            p = lst
+            mm([(p, a("NBIG"), free)], False, True)
+        else:
+            p = a("PS0", 0, 256)
+            mm([(p, a("IDN"), a("LHL", 0, 256)), (p, a("IDN"), a("LHL", 256, 512))] + [(p, a("NBIG"), x) for x in ([forced, free] if t > 1 else [free])])
         act(a("LK"), p, AF.Identity)
-        p = a("PS6", 256, 512)
-        mm([(p, a("IDN"), a("NHL", 0, 256)), (p, a("IDN"), a("NHL", 256, 512)), (p, a("IBIG"), a("M1")), (p, a("IBIG"), a("FR"))])
+        p = a("PS1", 0, 256)
+        if CFG["nc"] == "P":
+            mm([(p, a("IDN"), a("NHL", 0, 256)), (p, a("IDN"), a("NHL", 256, 512)), (p, a("IBIG"), a("M1"))], True, False)
+            mm([(p, a("IBIG"), free)], False, True)
+        else:
+            mm([(a("PS1", 256, 512), a("IBIG"), free)])
+            tt(p, a("PS1", 256, 512), a("NC"), OP.min)
         tt(a("NC"), p, a("LK"), OP.max)
-        phase[1] = True
         names(t + 1)
         if t < TV:
             named(t + 1)
-            hints(t + 1, "QI%d" % (t + 1))
-            for k in range(8):
-                gather(CFG["t"][t + 1][k], a("TW", 512 * k, 512 * k + 512), a("LT"), a("CIp", 32 * k, 32 * k + 32))
-        phase[1] = False
+            wide(CFG["t"][t + 1], "TW", "LT", "CIp")
+            if t > 1 or not CFG["early2"]:
+                hints(t + 1, "QI%d" % (t + 1))
+        if t == TV:
+            fill("QW1", 0, V)
         below = [(a("ONES"), a("CS", ca, ca + 1)), (a("MB", 128 * t - 128, 128 * t), a("FR", ca, ca + 1))]
         tot, c16 = a("CS", 256, 257), a("CS", 257, 258)
-        pa, pt, px = a("PS3", 0, 1), a("PS3", 1, 2), a("PS3", 2, 3)
+        pa, pt, px = a("PS5", 0, 1), a("PS5", 1, 2), a("PS5", 2, 3)
         mms([[(pa, l, x) for l, x in below], [(pt, a("ONES"), tot), (pt, a("NEG"), c16)],
-             [(px, a("NEG"), tot), (px, a("ONES"), c16)] + [(px, l, x) for l, x in below]], a("PS3", 0, 3))
-        pb = a("PS5", 256, 257)
+             [(px, a("NEG"), tot), (px, a("ONES"), c16)] + [(px, l, x) for l, x in below]], a("PS5", 0, 3))
+        pb = a("PS7", 0, 1)
         mm([(pb, od("B", i), a("CS", 16 * i + 16, 16 * i + 17)) for i in range(16)])
-        mm(pick(a("PS4", 0, 16), "B", "CS", 1, 16))
-        p = a("PS7", 256, 512)
-        mm([(p, a("ONES"), a("CS", 0, 256)), (p, a("TLE"), a("FR"))])
-        act(a("CT"), a("PS4", 0, 16), AF.Identity)
+        three = 6 in CFG["banks"]
+        rkb = "PS2" if three else "PS6"
+        mm(pick(a(rkb, 256, 272), "B", "CS", 1, 16))
+        p = a(rkb, 0, 256)
+        mm([(p, a("ONES"), a("CS", 0, 256)), (p, a("TLE"), free)])
+        act(a("CT"), a(rkb, 256, 272), AF.Identity)
         act(a("RK"), p, AF.Identity)
         ts(a("DL", 0, 1), pt, pa, OP.min, 0.0, OP.max)
-        ts(a("RJ"), k256, px, OP.is_gt, a("DL", 0, 1), OP.mult)
-        ts(a("INV"), k256, -256.0, OP.add, pt, OP.is_gt)
-        tt(a("RHO"), a("RJ"), a("PS2", 256, 512), OP.add)
+        rj = a("PS5", 256, 512)
+        ts(rj, a("K16"), px, OP.is_gt, a("DL", 0, 1), OP.mult)
+        tt(a("RHO"), rj, k256, OP.add)
         ts(a("L1"), a("RHO"), pb, OP.is_gt, 16.0, OP.mult)
-        ph, pc, pp = a("PS4", 32, 48), a("PS3", 16, 32), a("PS4", 64, 80)
-        mm(pick(ph, "B", "L1", 0, 16))
-        ts(a("HO"), ph, 1.0 / 16, OP.mult, 15.0, OP.min)
-        act(a("CB"), ph, AF.Identity)
-        tt(a("L2"), ind(a("CT"), a("HO")), a("RHO"), OP.is_lt)
-        mm(pick(pc, "B", "L2", 0, 16) + [(pc, a("IDN"), a("CB"))])
-        ts(a("CO"), pc, 255.0, OP.min)
-        act(a("CB"), pc, AF.Identity)
-        tt(a("L3"), ind(a("RK"), a("CO")), a("RHO"), OP.is_lt)
-        mm(pick(pp, "B256", "L3", 0, 16) + [(pp, a("IDN"), a("CB"))])
-        ts(a("WO"), pp, float(V - 1), OP.min)
-        gather(CFG["vg"], a("VAL"), a("CAND"), a("WO"))
+        if acc:
+            ph = pc = pp = a("PS5", 32, 48)
+            mm(pick(ph, "B", "L1", 0, 16))
+            ts(a("HO"), ph, 1.0 / 16, OP.mult, 15.0, OP.min)
+            tt(a("L2"), ind(a("CT"), a("HO")), a("RHO"), OP.is_lt)
+            mm(pick(pc, "B", "L2", 0, 16), False, True)
+            ts(a("CO"), pc, 255.0, OP.min)
+            tt(a("L3"), ind(a("RK"), a("CO")), a("RHO"), OP.is_lt)
+            mm(pick(pp, "B256", "L3", 0, 16), False, True)
+        else:
+            ph, pc, pp = a("PS5", 32, 48), a("PS5", 48, 64), a("PS5", 64, 80)
+            mm(pick(ph, "B", "L1", 0, 16))
+            ts(a("HO"), ph, 1.0 / 16, OP.mult, 15.0, OP.min)
+            cp(a("CB"), ph)
+            tt(a("L2"), ind(a("CT"), a("HO")), a("RHO"), OP.is_lt)
+            mm(pick(pc, "B", "L2", 0, 16) + [(pc, a("IDN"), a("CB"))])
+            ts(a("CO"), pc, 255.0, OP.min)
+            cp(a("CB"), pc)
+            tt(a("L3"), ind(a("RK"), a("CO")), a("RHO"), OP.is_lt)
+            mm(pick(pp, "B256", "L3", 0, 16) + [(pp, a("IDN"), a("CB"))])
+        ts(a("WO"), pp, float(V), OP.min)
+        gather("S", a("VAL"), a("CAND"), a("WO"))
         if t < TV:
-            send("va%d" % (t + 1), 1, a("VAL"), T["VI%d" % (t + 1)][:, :], a("VI%d" % (t + 1))["reg"], 65536)
+            sendto("va%d" % (t + 1), a("VAL"), a("VI%d" % (t + 1)), 65536)
             name_rows(t + 1)
         if t == TV - 1:
-            dma("Y", "own", [(T.CAND[2::16, :], T.OWN[:, 0:256]), (T.CAND[3::16, :], T.OWN[:, 256:512])], [a("CAND")], [a("OWN")], 131072)
-        pn, pw, pl_, po, pq = a("PS3", 32, 48), a("PS2", 0, 256), a("PS7", 0, 256), a("PS6", 0, 16), a("PS4", 96, 112)
-        mm(pick(pn, "BSEL", "VAL", 0, 16))
+            rows("Y", "own", "CAND", [(2, a("OWN", 0, 256)["ap"]), (3, a("OWN", 256, 512)["ap"])], [a("OWN")])
+        no = 32 if t < TV else 16
+        pn, pw, pl_, pq = a("PS5", 96, 96 + no), a("PS4", 256, 512) if three else a("PS6", 0, 256), a("PS7", 0, 256), a("PS5", 128, 144)
+        mm(pick(a("PS5", 96, 112), "BSEL", "VAL", 0, 16))
         mm([(pw, a("SUM2"), a("VAL"))])
-        cp(a("NOF"), pn)
-        cp(a("NLF"), pn)
+        if CFG["sp"] == 2:
+            cp(a("NLF", 0, 16), a("PS5", 96, 112))
+            ts(a("SPC", 0, 16), a("PS5", 96, 112), -1.0, OP.add)
+        if t < TV:
+            p = a("PS5", 112, 128)
+            mm(pick(p, "BOUT", "VAL", 0, 16) + [(p, a("NI"), a("M1", 0, 16))])
+            if CFG["sp"] == 2:
+                ts(a("SPC", 16, 32), p, -1.0, OP.add)
+                act(a("NLF", 16, 32), p, AF.Identity)
+        if CFG["sp"] == 1:
+            ts(a("SPC", 0, no), pn, -1.0, OP.add)
+            cp(a("NLF", 0, no), pn)
+        if t < TV:
+            sendto("si%d" % (t + 1), a("SPC"), a("SI%d" % (t + 1)), 8192)
+        cp(a("NU"), pw)
         act(a("NW"), pw, AF.Identity)
-        gather(CFG["qg"], a("QG"), a(QW), a("NOF"))
+        gather("S", a("QG"), a(QW), a("SPC", 0, 16))
         mm(pick(pq, "B0", "QG", 0, 16))
-        mm([(pl_, a("ONES"), a("INV"))], True, False)
-        mm(pick(po, "BQ" if t < TV else "BSEL", "VAL", 0, 16), True, False)
+        mm([(pl_, a("OUT4"), a("VAL"))], True, False)
         at, items = 0, []
         for i in range(15):
             n = 240 - 16 * i
-            ts(a("EQ", at, at + n), a("NW", 256 - n, 256), a("NLF", i, i + 1), OP.is_equal)
-            items.append((a("PS7", 256 - n, 256), a("ONES"), a("EQ", at, at + n)))
+            ts(a("EQ", at, at + n), a("NU", 256 - n, 256), a("NLF", i, i + 1), OP.is_equal)
+            items.append((a("PS7", 256 - n, 256), a("ONEB"), a("EQ", at, at + n)))
             at += n
             if i in (3, 8, 14):
                 mm(items, False, False)
                 items = []
-        tt(a("NWT"), pw, a("TRI"), OP.mult)
-        tt(a("ED"), ind(a("NLF"), a("REP")), a("NWT"), OP.is_equal)
-        mm([(pl_, a("ONES"), a("ED"))], False, False)
+        if CFG["nwt"] == "V":
+            tt(a("NWT"), pw, a("TRI"), OP.mult)
+        else:
+            p = a("PS5", 256, 512)
+            mm([(p, a("SUM2"), a("VAL")), (p, a("NBIG"), a("TRB"))])
+            act(a("NWT"), p, AF.Identity)
+        tt(a("ED"), ind(a("NLF", 0, 16), a("REP")), a("NWT"), OP.is_equal)
+        mm([(pl_, a("ONEB"), a("ED"))], False, False)
         cp(a("QC"), pq)
         tt(a("EE"), ind(a("LK"), a("QC")), a("NW"), OP.is_equal)
-        mm([(pl_, a("ONES"), a("EE"))], False, True)
-        ts(a("LF"), pl_, 0.5, OP.is_gt, 512.0, OP.mult)
-        mm(pick(po, "B", "LF", 0, 16), False, True)
-        lo = 16 if t < TV else 0
-        tt(a("TO", lo, lo + 16), po, a("DUM"), OP.min)
-        cp(a("OFF", lo, lo + 16), a("TO", lo, lo + 16))
+        mm([(pl_, a("ONEB"), a("EE"))], False, True)
+        tt(a("LF"), pl_, a("DUMW"), OP.min)
+        if CFG["pf"] == 2:
+            for lo in range(160, 160 + no, 16):
+                mm(pick(a("PS5", lo, lo + 16), "BSEL", "LF", 0, 16))
+            tt(a("TO", 0, no), a("PS5", 160, 160 + no), a("NLF", 0, no), OP.max)
+        else:
+            mm(pick(a("PS5", 160, 176), "BSEL", "LF", 0, 16))
+            for lo in range(0, no, 16):
+                tt(a("TO", lo, lo + 16), a("PS5", 160, 176), a("NLF", lo, lo + 16), OP.max)
+        ts(a("OFF", 0, no), a("TO", 0, no), -1.0, OP.add)
         if t < TV:
-            OI = "OI%d" % (t + 1)
-            send("of%d" % (t + 1), 1, a("OFF", 16, 32), T[OI][:, 16:32], a(OI, 16, 32)["reg"], 4096)
-            ts(a("TO", 32, 48), a("TO", 16, 32), -4100.0, OP.add, 1000.0, OP.mult)
-            tt(a("TO", 48, 64), a("TO", 32, 48), a("NLF"), OP.max)
-            tt(a("TO", 0, 16), a("TO", 48, 64), a("DUM"), OP.min)
-            cp(a("OFF", 0, 16), a("TO", 0, 16))
-            send("oq%d" % (t + 1), 1, a("OFF", 0, 16), T[OI][:, 0:16], a(OI, 0, 16)["reg"], 4096)
+            sendto("of%d" % (t + 1), a("OFF"), a("OI%d" % (t + 1)), 8192)
 
-    for k in range(8):
-        gather(CFG["fin"][k], a("DA", 512 * k, 512 * k + 512), a("LT"), a("QO", 32 * k, 32 * k + 32))
-        if k % 4 == 3:
-            lo, hi = 128 * (k // 4), 128 * (k // 4) + 128
-            p = a("PS0", lo, hi)
-            mm(pick(p, "BSEL", "DA", 16 * lo, 128) + [(p, a("NI"), a("OWN", lo, hi)), (p, a("NI"), a("OWN", 256 + lo, 256 + hi))])
-            ts(a("E1", lo, hi), p, 0.0, OP.not_equal)
-            p = a("PS1", lo, hi)
-            mm(pick(p, "BOUT", "QW0", 1 + 16 * lo, 128), True, False)
-            mm([(p, a("NBIG"), a("E1", lo, hi))], False, True)
-            ts(a("Y0", lo, hi), p, -1.0, OP.max)
-    for k in range(8):
-        for h in range(2):
-            p = a("PS5", 32 * k + 16 * h, 32 * k + 16 * h + 16)
-            mm([(p, a("NHL", h, 256, 2), a("IDN", 16 * k, 16 * k + 16)), (p, a("NHL", 256 + h, 512, 2), a("IDN", 16 * k, 16 * k + 16))])
-    act(a("FA"), a("PS5", 0, 256), AF.Identity, -1.0)
-    dma("Y", "yn", [(T.yn[k], T.FA[:, 32 * k:32 * k + 32]) for k in range(8)], [], [a("FA")], 300000)
-    cp(ind(a("TW", 0, WW), a("OFF", 0, 16)), a("VAL"))
+    phase[0] = 5
+    for m in range(0, 8, 2):
+        mms([[(a("PS2", 32 * k + 16 * h, 32 * k + 16 * h + 16), a("NHL", 256 * d + h, 256 * d + 256, 2), a("IDN", 16 * k, 16 * k + 16)) for d in range(2)]
+             for k in (m, m + 1) for h in range(2)], a("PS2", 0, 256))
+    act(a("FA"), a("PS2", 0, 256), AF.Identity, -1.0)
+    dma("Y", "yn", [(T.yn[k], a("FA", 32 * k, 32 * k + 32)["ap"]) for k in range(8)], [], [a("FA")], 300000)
+    wide(CFG["fin"], "UU", "LT", "QO")
+    held, place = a("PS0", 0, 256), a("PS1", 0, 256)
+    mm([(place, a("NBIG"), a("SGN")), (place, a("I2"), a("SGN"))], True, False)
+    mm([(held, a("NI"), a("OWN", 0, 256)), (held, a("NI"), a("OWN", 256, 512))], True, False)
+    for h in range(4):
+        cut(pick(a("PS0", 64 * h, 64 * h + 64), "BSEL", "UU", 1024 * h, 64), False, h == 3, 8)
+    ts(a("E1"), held, 0.0, OP.not_equal)
+    mm([(place, a("NBIG"), a("E1"))], False, True)
+    tt(a("Y0"), place, a("FC"), OP.add)
+    cp(ind(a("QW1"), a("OFF", 0, 16)), a("VAL"))
     for h in range(2):
         p = a("PS%d" % (3 + h), 0, 128)
-        mm([(p, a("IDN"), a("M1", 0, 128))] + pick(p, "BQ", "TW", 1 + 2048 * h, 128))
+        mm([(p, a("IDN"), a("M1", 0, 128))], True, False)
+        mm(pick(p, "BQ", "QW1", 2048 * h, 128), False, True)
         tt(a("FB", 128 * h, 128 * h + 128), p, a("Y0", 128 * h, 128 * h + 128), OP.max)
-    dma("Y", "yp", [(T.yp[:, :], T.FB[:, :])], [], [a("FB")], 131072)
+        dma("YS"[h], "yp%d" % h, [(T.yp[:, 128 * h:128 * h + 128], a("FB", 128 * h, 128 * h + 128)["ap"])], [], [a("FB", 128 * h, 128 * h + 128)], 65536)
     return ops
 
 
 def hazards(ops):
     hist = {}
     sent = {}
+    above = []
     for i, o in enumerate(ops):
-        deps = {}
+        deps = set()
         acc = [(x, False) for x in o["r"]] + [(x, True) for x in o["w"]]
         for (nm_, lo, hi), wr in acc:
             bank = nm_[:2] == "PS"
             for j, l2, h2, w2 in hist.get(nm_, []):
-                over = lo < h2 and l2 < hi
-                if over and (wr or w2):
-                    deps[j] = deps.get(j, False) or (w2 and not wr)
-                elif bank and (ops[j]["e"] != o["e"] or wr):
-                    deps[j] = deps.get(j, False)
+                if (lo < h2 and l2 < hi and (wr or w2)) or (bank and (ops[j]["e"] != o["e"] or wr)):
+                    deps.add(j)
         if o["kind"] == "s":
             sent[o["name"]] = i
         if o["kind"] == "r":
-            deps = {sent[o["name"]]: True}
+            deps = {sent[o["name"]]}
         for (nm_, lo, hi), wr in acc:
             h = hist.setdefault(nm_, [])
             if wr and nm_[:2] != "PS":
@@ -564,170 +682,89 @@ def hazards(ops):
             elif nm_[:2] == "PS":
                 h[:] = h[-48:]
             h.append((i, lo, hi, wr))
-        deps.pop(i, None)
+        deps.discard(i)
         o["deps"] = deps
+        far = 0
+        for j in deps:
+            far |= above[j]
+        o["near"] = sorted(j for j in deps if not far >> j & 1)
+        for j in deps:
+            far |= 1 << j
+        above.append(far)
 
 
-def order(ops):
+def tables(ops, sets):
     n = len(ops)
+    en = ["VSPGYR".index(o["e"]) for o in ops]
+    full = [o["kind"] == "c" for o in ops]
+    tabs = []
+    for cost, c, w in sets:
+        dl = [[(j, (c["self"] if en[i] != 2 else 0.0) if en[j] == en[i] and full[j] else c["hop"]) for j in ops[i]["near"]] for i in range(n)]
+        tabs.append((cost, [cost[i] if full[i] else ops[i]["hold"] for i in range(n)], dl, w, en))
+    return tabs
+
+
+def play(s, tab, trace=False):
+    cost, hold, dl, _, en = tab
+    free, last = [0.0] * 6, [-1] * 6
+    t1, why = [0.0] * len(s), [-1] * len(s)
+    for i in s:
+        e = en[i]
+        t, y = free[e], last[e]
+        for j, d in dl[i]:
+            u = t1[j] + d
+            if u >= t:
+                t, y = u, j
+        t1[i] = t + cost[i]
+        free[e] = t + hold[i]
+        last[e] = i
+        why[i] = y
+    return (t1, why) if trace else max(t1)
+
+
+def event_order(ops, tab, look, tol):
+    cost, hold, dl, _, en = tab
+    n = len(cost)
+    way = [0.0] * n
+    lead = [o.get("lead", 0.0) for o in ops]
     succ = [[] for _ in range(n)]
-    for i, o in enumerate(ops):
-        for j in o["deps"]:
-            succ[j].append(i)
-    pri = [0.0] * n
-    early = [0.0] * n
-    for i, o in enumerate(ops):
-        early[i] = o["cost"] + max([early[j] for j in o["deps"]] + [0.0])
-    done = [False] * n
-    count = [0]
-
-    def pull(i):
-        stack = [(i, False)]
-        while stack:
-            j, ripe = stack.pop()
-            if ripe:
-                pri[j] = -count[0]
-                count[0] += 1
-            elif not done[j]:
-                done[j] = True
-                stack.append((j, True))
-                stack += [(k, False) for k in sorted(ops[j]["deps"], key=lambda k: early[k])]
-    stage = {k: x for x, k in enumerate(GOALS)}
-    for i in sorted(range(n), key=lambda i: (stage.get(ops[i]["key"], len(GOALS)), i)):
-        pull(i)
-    pri = [p + SHIFT.get(o["key"], 0.0) for p, o in zip(pri, ops)]
-    pred = [list(o["deps"]) for o in ops]
-    cost = [o["cost"] for o in ops]
-    hold = [o["cost"] if o["kind"] == "c" else 0.0 if o["e"] == "R" else 0.3 for o in ops]
-
-    def gap(j, i):
-        if ops[j]["e"] == ops[i]["e"] and ops[j]["kind"] == "c":
-            return COST["self"] if ops[i]["e"] != "P" else 1e-6
-        return COST["hop"]
-
-    def sweep(rank, back):
-        before, after = (succ, pred) if back else (pred, succ)
-        left = [len(x) for x in before]
-        t0 = [0.0] * n
-        busy = {e: [] for e in "VSPGYR"}
-        pool = sorted((rank[i], i) for i in range(n) if not left[i])
-        while pool:
-            i = pool.pop()[1]
-            t = max([t0[j] + cost[j] + (gap(i, j) if back else gap(j, i)) for j in before[i]] + [0.0])
-            lead = cost[i] - hold[i] if back else 0.0
-            t += lead
-            b = busy[ops[i]["e"]]
-            k = len(b)
-            while k and b[k - 1][1] > t:
-                k -= 1
-            fit = hold[i] - (COST["tol"] if hold[i] > 0.8 else 0.0)
-            while k < len(b) and b[k][0] < t + fit:
-                t = max(t, b[k][1])
-                k += 1
-            if hold[i]:
-                b.insert(k, (t, t + fit))
-            t0[i] = t - lead
-            for j in after[i]:
-                left[j] -= 1
-                if not left[j]:
-                    x = (rank[j], j)
-                    k = len(pool)
-                    while k and pool[k - 1] > x:
-                        k -= 1
-                    pool.insert(k, x)
-        return t0
-
-    best = None
-    rank = pri
-    for _ in range(COST["rounds"]):
-        t0 = sweep(rank, False)
-        end = max(t0[i] + cost[i] for i in range(n))
-        if best is None or end < best[0]:
-            best = (end, t0)
-        tb = sweep([t0[i] + cost[i] for i in range(n)], True)
-        rank = [tb[i] + cost[i] for i in range(n)]
-    for o, t in zip(ops, best[1]):
-        o["t0"], o["t1"] = t, t + o["cost"]
-    return sorted(range(n), key=lambda i: (best[1][i], i))
-
-
-def first_order(ops):
-    n = len(ops)
-    succ = [[] for _ in range(n)]
-    end = {}
-    for i, o in enumerate(ops):
-        end[o["key"][-1]] = i
-        for j in o["deps"]:
-            succ[j].append(i)
-    pri = []
-    for i, o in enumerate(ops):
-        k = o["key"][:-2] + (".0" if o["key"][-1] == "0" else "")
-        pri.append(end[o["key"][-1]] + LATE.index(k) / 100 + i / 1e6 if k in LATE and o.get("late", True) else i)
     for i in range(n - 1, -1, -1):
-        if ops[i]["key"] in LAZY:
-            pri[i] = min([pri[k] for k in succ[i]] + [n]) - 1e-3
-    left = [len(o["deps"]) for o in ops]
-    ready = [0.0] * n
-    free = {e: 0.0 for e in "VSPGYR"}
-    pool = {e: [] for e in "VSPGYR"}
-    for i, o in enumerate(ops):
-        if not left[i]:
-            pool[o["e"]].append(i)
+        way[i] += cost[i] + lead[i]
+        for j, d in dl[i]:
+            way[j] = max(way[j], way[i] + d)
+            succ[j].append((i, d))
+    left = [len(x) for x in dl]
+    ready, free = [0.0] * n, [0.0] * 6
+    pool = [[i for i in range(n) if not left[i] and en[i] == e] for e in range(6)]
     seq = []
     while len(seq) < n:
-        cand = []
-        for e in pool:
-            if pool[e]:
-                now = max(free[e], min(ready[i] for i in pool[e]))
-                i = min((i for i in pool[e] if ready[i] <= now + COST["look"]), key=lambda i: pri[i])
-                wide = ops[i]["kind"] == "c" and ops[i]["cost"] > 0.5 and e != "P"
-                if wide:
-                    i = min((k for k in pool[e] if ready[k] <= now + ops[i]["cost"] - COST["tol"] or k == i), key=lambda k: pri[k])
-                cand.append((now + (COST["wait"] if wide else 0.0), now, e, i))
-        _, now, e, i = min(cand)
+        best = None
+        for e in range(6):
+            p = pool[e]
+            if p:
+                now = max(free[e], min(ready[i] for i in p))
+                i = max((i for i in p if ready[i] <= now + look), key=lambda i: way[i])
+                if hold[i] > 0.45:
+                    i = max((k for k in p if k == i or ready[k] <= now + hold[i] * tol), key=lambda k: way[k])
+                st = max(now, ready[i])
+                if best is None or st < best[0]:
+                    best = (st, e, i)
+        st, e, i = best
         pool[e].remove(i)
-        o = ops[i]
-        t0 = max(now, ready[i])
-        t1 = t0 + o["cost"]
-        free[e] = t1 if o["kind"] == "c" else t0 + (0.0 if e == "R" else 0.3)
+        free[e] = st + hold[i]
         seq.append(i)
-        for k in succ[i]:
-            same = ops[k]["e"] == e and o["kind"] == "c"
-            ready[k] = max(ready[k], t1 + ((COST["self"] if e != "P" else 0.0) if same else COST["hop"]))
+        for k, d in succ[i]:
+            ready[k] = max(ready[k], st + cost[i] + d)
             left[k] -= 1
             if not left[k]:
-                pool[ops[k]["e"]].append(k)
+                pool[en[k]].append(k)
     return seq
 
 
-def polish(ops, seq, sets, steps):
+def polish(ops, seq, tabs, steps):
     n = len(ops)
-    qs = "VSPGYR"
-    en = [qs.index(o["e"]) for o in ops]
-    full = [o["kind"] == "c" for o in ops]
-    pred = [list(o["deps"]) for o in ops]
-    pset = [set(x) for x in pred]
-    tabs = []
-    for cost, c, w in sets:
-        dl = [[(j, (c["self"] if en[i] != 2 else 0.0) if en[j] == en[i] and full[j] else c["hop"]) for j in pred[i]] for i in range(n)]
-        tabs.append((cost, [cost[i] if full[i] else 0.0 if en[i] == 5 else 0.3 for i in range(n)], dl, w))
-
-    def play(s, tab, trace=False):
-        cost, hold, dl, _ = tab
-        free, last = [0.0] * 6, [-1] * 6
-        t1, why = [0.0] * n, [-1] * n
-        for i in s:
-            e = en[i]
-            t, y = free[e], last[e]
-            for j, d in dl[i]:
-                u = t1[j] + d
-                if u >= t:
-                    t, y = u, j
-            t1[i] = t + cost[i]
-            free[e] = t + hold[i]
-            last[e] = i
-            why[i] = y
-        return (t1, why) if trace else max(t1)
+    en = tabs[0][4]
+    pset = [set(o["near"]) for o in ops]
 
     def worth(s):
         return sum(play(s, tab) * tab[3] for tab in tabs)
@@ -759,7 +796,7 @@ def polish(ops, seq, sets, steps):
             while far and a > 0:
                 a -= 1
                 far -= en[seq[a]] == en[i]
-            need, up = set(pred[i]), [i]
+            need, up = set(pset[i]), [i]
             for x in reversed(seq[a:b]):
                 if x in need:
                     up.append(x)
@@ -785,26 +822,147 @@ def polish(ops, seq, sets, steps):
             seq, cur, pairs = new, w, None
             if w < best:
                 best, keep = w, new
-    t1, _ = play(keep, tabs[0], True)
-    for i, o in enumerate(ops):
-        o["t1"] = t1[i]
-        o["t0"] = t1[i] - o["cost"]
     return keep
 
 
-def plan(g, core, T, topo):
+def refine(ops, seq, tabs, steps, width=200, rounds=3, heat=0.003):
+    n = len(ops)
+    en = tabs[0][4]
+    pset = [set(o["near"]) for o in ops]
+    succ = []
+    for tab in tabs:
+        s = [[] for _ in range(n)]
+        for i in range(n):
+            for j, d in tab[2][i]:
+                s[j].append((i, d))
+        succ.append(s)
+    seed = [12345]
+
+    def rnd(k):
+        seed[0] = (seed[0] * 1103515245 + 12345) % 2147483648
+        return (seed[0] >> 8) % k
+
+    def frame(s, a, b):
+        out = []
+        inside = set(s[a:b])
+        for tab, sc in zip(tabs, succ):
+            cost, hold, dl, w, _ = tab
+            free, t1 = [0.0] * 6, [0.0] * n
+            for i in s[:a]:
+                t = max([free[en[i]]] + [t1[j] + d for j, d in dl[i]])
+                t1[i] = t + cost[i]
+                free[en[i]] = t + hold[i]
+            nxt, way = [0.0] * 6, [0.0] * n
+            for i in reversed(s[b:]):
+                way[i] = nxt[en[i]] = max(cost[i] + max([way[j] + d for j, d in sc[i]] + [0.0]), nxt[en[i]] + hold[i])
+            early, late, near = [0.0] * n, [0.0] * n, [None] * n
+            for i in inside:
+                early[i] = max([t1[j] + d for j, d in dl[i] if j not in inside] + [0.0])
+                late[i] = max([way[j] + d for j, d in sc[i] if j not in inside] + [0.0])
+                near[i] = [(j, d) for j, d in dl[i] if j in inside]
+            out.append((cost, hold, near, w, free, nxt, early, late))
+        return out
+
+    def run(part, fr):
+        total, pairs = 0.0, []
+        for cost, hold, near, w, free0, nxt, early, late in fr:
+            free, last = list(free0), [-1] * 6
+            t1, why = {}, {}
+            top, who = 0.0, -1
+            for i in part:
+                e = en[i]
+                t, y = free[e], last[e]
+                if early[i] > t:
+                    t, y = early[i], -1
+                for j, d in near[i]:
+                    u = t1[j] + d
+                    if u >= t:
+                        t, y = u, j
+                free[e] = t + hold[i]
+                last[e] = i
+                t += cost[i]
+                t1[i] = t
+                why[i] = y
+                if t + late[i] > top:
+                    top, who = t + late[i], i
+            for e in range(6):
+                if free[e] + nxt[e] > top:
+                    top, who = free[e] + nxt[e], last[e]
+            total += top * w
+            while who >= 0 and why[who] >= 0:
+                if why[who] not in pset[who]:
+                    pairs.append((why[who], who))
+                who = why[who]
+        return total, pairs
+
+    starts = list(range(0, max(n - width, 0) + width // 2, width // 2))
+    each = steps // (rounds * len(starts))
+    for a0 in starts * rounds:
+        b0 = min(n, a0 + width)
+        fr = frame(seq, a0, b0)
+        part = seq[a0:b0]
+        cur, pairs = run(part, fr)
+        best, keep = cur, part
+        for it in range(each):
+            if not pairs:
+                break
+            j, i = pairs[rnd(len(pairs))]
+            a, b = part.index(j), part.index(i)
+            far = rnd(6) if rnd(2) else 0
+            if rnd(2):
+                while far and a > 0:
+                    a -= 1
+                    far -= en[part[a]] == en[i]
+                need, up = set(pset[i]), [i]
+                for x in reversed(part[a:b]):
+                    if x in need:
+                        up.append(x)
+                        need |= pset[x]
+                if j in need:
+                    continue
+                u = set(up)
+                new = part[:a] + up[::-1] + [x for x in part[a:b] if x not in u] + part[b + 1:]
+            else:
+                while far and b < len(part) - 1:
+                    b += 1
+                    far -= en[part[b]] == en[j]
+                down = {j}
+                for x in part[a + 1:b + 1]:
+                    if pset[x] & down:
+                        down.add(x)
+                if i in down:
+                    continue
+                new = part[:a] + [x for x in part[a:b + 1] if x not in down] + [x for x in part[a:b + 1] if x in down] + part[b + 1:]
+            w, p2 = run(new, fr)
+            if w <= cur + heat * len(tabs) * (1 - it / each) * rnd(100) / 100:
+                part, cur, pairs = new, w, p2
+                if w < best:
+                    best, keep = w, new
+        seq = seq[:a0] + keep + seq[b0:]
+    return seq
+
+
+def timings(g, core, T, topo, ops):
     sets = []
     for ch, w in SPREAD:
         c = dict(COST)
         c.update(ch)
         sets.append(([o["cost"] for o in build(g, core, T, topo, c)], c, w))
+    return tables(ops, sets)
+
+
+def plan(g, core, T, topo):
     ops = build(g, core, T, topo, COST)
     hazards(ops)
     if "seq" not in MEMO:
-        MEMO["seq"] = polish(ops, first_order(ops), sets, COST["steps"])
-        MEMO["t"] = [(o["t0"], o["t1"]) for o in ops]
+        tabs = timings(g, core, T, topo, ops)
+        seq = min((event_order(ops, tab, look, tol) for tab in tabs for look in (0.02, 0.05, 0.1, 0.2) for tol in (0.0, 0.3, 0.5, 0.7)),
+                  key=lambda s: sum(play(s, tab) * tab[3] for tab in tabs))
+        MEMO["seq"] = refine(ops, seq, tabs, COST["steps"])
+        MEMO["t"] = play(MEMO["seq"], tabs[0], True)[0]
+        MEMO["tabs"] = tabs
     for o, t in zip(ops, MEMO["t"]):
-        o["t0"], o["t1"] = t
+        o["t1"] = t
     return ops, MEMO["seq"]
 
 

from concourse.mybir import AluOpType as OP, ActivationFunctionType as AF

N, V, C, STEP, TV = 4, 4096, 256, 995, 4
WW = V + C + 16
BF, F32, I32, U16 = "bfloat16", "float32", "int32", "uint16"

WIDE = {"X": (V, BF), "F1": (V, BF), "F2": (V, BF), "F3": (V, BF), "F4": (V, BF), "TW": (2 * V + 128, BF), "LT": (V, BF),
        "QW0": (WW, BF), "QW1": (WW, BF), "IT": (V, F32), "CIW": (V, F32), "BB": (V, BF), "RB": (V, BF), "UU": (V, BF), "UR": (V, BF),
        "XM": (V, BF), "CAND": (V + 16, BF)}
SMALL = {
    "PLo": (256, I32), "PLp": (256, I32), "CCo": (256, I32), "IA": (256, I32), "IB": (256, I32), "IC": (256, I32), "IE": (512, I32), "PI": (16, I32),
    "IOT": (256, F32), "FA": (256, F32), "FB": (256, F32), "FC": (256, F32), "FD": (256, F32), "DM": (256, F32), "CIL": (256, F32),
    "NF": (256, F32), "NC": (256, F32), "LK": (256, F32), "DL": (16, F32), "RHO": (256, F32), "CT": (16, F32), "RK": (256, F32),
    "NW": (256, F32), "NWT": (256, F32), "NLF": (32, F32), "TO": (32, F32), "COL": (16, F32), "ROW": (16, F32), "LOW": (16, F32), "LC": (32, F32),
    "IDF": (128, F32), "TRI": (256, F32), "Y0": (256, F32),
    "P2": (256, U16), "PT": (256, U16), "SO": (256, U16), "CIo": (256, U16), "CIp": (256, U16), "QO": (256, U16),
    "QI2": (256, U16), "QI3": (256, U16), "QI4": (256, U16), "NO": (256, U16), "LO": (256, U16), "HO": (16, U16), "CO": (16, U16), "WO": (16, U16),
    "NU": (256, U16), "QC": (16, U16), "SPC": (32, U16), "SI2": (32, U16), "SI3": (32, U16), "SI4": (32, U16),
    "OFF": (32, U16), "OI2": (32, U16), "OI3": (32, U16), "OI4": (32, U16), "REP": (16, U16),
    "CHL": (512, BF), "OWN": (512, BF), "NHL": (512, BF), "LHL": (768, BF), "E1": (256, BF), "SGN": (256, BF), "FR": (512, BF), "CS": (272, BF),
    "L1": (256, BF), "L2": (256, BF), "L3": (256, BF), "CB": (16, BF), "TRB": (256, BF), "OUT4": (128, BF), "QG": (256, BF), "EQ": (1920, BF),
    "ED": (256, BF), "EE": (256, BF), "LF": (256, BF), "VAL": (256, BF), "VI2": (256, BF), "VI3": (256, BF), "VI4": (256, BF),
    "BS": (256, BF), "BT": (256, BF), "XS": (256, BF), "XT": (256, BF), "US": (256, BF), "VJ": (256, BF), "K16": (256, BF), "DUMW": (256, BF), "M1": (256, BF),
    "B": (144, BF), "BH": (144, BF), "BSEL": (144, BF), "BOUT": (144, BF), "B0": (144, BF), "BQ": (144, BF), "B256": (144, BF),
    "IDN": (128, BF), "I2": (128, BF), "NI": (128, BF), "N2": (128, BF), "I32": (128, BF), "IBIG": (128, BF), "NBIG": (128, BF),
    "ONES": (128, BF), "ONEB": (128, BF), "NEG": (128, BF), "TLE": (128, BF), "SUM2": (128, BF), "MB": (512, BF),
}
SB = dict(WIDE)
SB.update(SMALL)
HOME, _fill = {k: (k, 0) for k in WIDE}, {}
for _k, (_n, _d) in SMALL.items():
    HOME[_k] = ("S" + _d, _fill.get(_d, 0))
    _fill[_d] = _fill.get(_d, 0) + _n
SCRATCH = {k: ("sbuf", [128, n], d) for k, (n, d) in WIDE.items()}
for _d, _n in _fill.items():
    SCRATCH["S" + _d] = ("sbuf", [128, _n], _d)
SCRATCH["NI3"] = ("sbuf", [128, 8, 32], I32)
SCRATCH["CCD"] = ("dram", [128, 512], BF)
SCRATCH["LD"] = ("dram", [3, 128, 512], BF)
SCRATCH["FD1"] = ("dram", [3, 128, 256], BF)
SCRATCH["FD2"] = ("dram", [3, 128, 512], BF)
SCRATCH["FD3"] = ("dram", [3, 128, 256], BF)
SCRATCH["LD3"] = ("dram", [3, 128, 768], BF)
for _b in range(8):
    SCRATCH["PS%d" % _b] = ("psum", [128, 512], F32)

MSGS = ["pl", "cc", "f1", "f2", "f3", "ci"] + ["%s%d" % (m, t) for t in (2, 3, 4) for m in ("lh", "fr", "fc", "qo", "va", "si", "of")]
LOCAL = ["pl", "cc", "nm", "x", "xm", "fo", "cct", "cil", "own", "nxt", "yn", "yp0", "yp1"] + ["%s%d" % (m, t) for t in (2, 3, 4, 5) for m in ("lt", "ft", "fd")] \
    + ["nr%d" % t for t in (1, 2, 3, 4)]
SEMAPHORES = ["eV", "eS", "eP", "eG"] + ["r_" + m for m in MSGS] + ["s_" + m for m in MSGS] + ["d_" + m for m in LOCAL]

CFG = {
    "q": {t: "SSSSSSSS" for t in (1, 2, 3, 4)},
    "t": {t: "SSSSSSSS" for t in (2, 3, 4)},
    "b": {t: "SSSSSSSS" for t in (1, 2, 3, 4)},
    "way": {1: "PPPPPPPP", 2: "DDPPPPPP", 3: "DDPPPPPP", 4: "DDPPPPPP"},
    "ba": {t: "SSSSSSSS" for t in (1, 2, 3, 4)},
    "aa": {t: "SSSSSSSS" for t in (1, 2, 3, 4)},
    "cm": {1: "SSSV", 2: "SSSV", 3: "SSSV", 4: "SSSV"},
    "fin": "SSSS",
    "nc": "P", "ws": 1, "cie": 3, "sc": (0, 32, 96, 192, 256), "nwt": "V", "fat": (1, 3), "fo": 2, "qc": 8, "banks": (0, 1), "sp": 2, "acc": False, "early2": False, "pf": 1, "tw": "V", "lt": "V", "it": "G",
}
COST = {"cy": 0.0009, "g": 1.3, "s": 2.5, "fix": 0.06, "pe": 0.00045, "hop": 0.12, "self": 0.08,
        "dma": 2.0, "rem": 2.5, "bw": 150e3, "steps": 240000}
SPREAD = [({}, 1 / 130), ({"hop": 0.25, "self": 0.12, "dma": 2.6, "rem": 3.4, "g": 1.2, "s": 3.5}, 1 / 160),
          ({"cy": 0.00085, "g": 1.1, "s": 2.0, "dma": 1.6, "rem": 2.0, "pe": 0.00055}, 1 / 135),
          ({"cy": 0.00115, "g": 1.95, "s": 5.2, "pe": 0.0007, "hop": 0.2, "dma": 2.5, "rem": 3.2}, 1 / 210)]
MEMO = {}


def build(g, core, T, topo, COST=COST):
    q = T.rank_of(core)
    ops = []
    phase = [0]
    cy, G, S, FIX = COST["cy"], COST["g"], COST["s"], COST["fix"]
    eng = {"V": g.vector, "S": g.scalar, "P": g.tensor, "G": g, "Y": g.sync}
    ROWS = ("LT", "CAND")

    def a(name, lo=0, hi=None, st=None):
        ps = name[:2] == "PS"
        hi = (512 if ps else SB[name][0]) if hi is None else hi
        ten, at = (name, 0) if ps else HOME[name]
        ap = T[ten][:, at + lo:at + hi] if st is None else T[ten][:, at + lo:at + hi:st]
        cnt = hi - lo if st is None else (hi - lo + st - 1) // st
        two = not ps and SB[name][1] in (BF, U16)
        return {"ap": ap, "reg": [(name, 0, 16) if name in ROWS else (name, lo, hi)], "n": cnt, "two": two, "ps": ps, "ind": False}

    def ind(win, off):
        return {"ap": win["ap"].indirect(off["ap"]), "reg": win["reg"], "off": off["reg"], "n": 16 * off["n"],
                "two": False, "ps": False, "ind": True}

    def add(e, fn, outs, ins, cost, kind="c", name=None, hold=None):
        r, w = [], []
        for x in ins:
            if isinstance(x, dict):
                r += x["reg"] + x.get("off", [])
        for x in outs:
            w += x["reg"]
            r += x.get("off", [])
        ops.append({"e": e, "fn": fn, "r": r, "w": w, "cost": cost, "kind": kind, "name": name, "hold": cost if hold is None else hold,
                    "key": "%s%s.%d" % (e, name or w[0][0], phase[0])})

    def val(x):
        return x["ap"] if isinstance(x, dict) else x

    def vcost(o, i, base):
        per = S if o["ind"] else G if i["ind"] else base
        return FIX + cy * max(64, per * o["n"])

    def cp(o, i):
        add("V", lambda: g.vector.tensor_copy(o["ap"], i["ap"]), [o], [i], vcost(o, i, 0.5 if o["two"] and i["two"] else 1))

    def tt(o, i0, i1, op):
        add("V", lambda: g.vector.tensor_tensor(o["ap"], i0["ap"], i1["ap"], op), [o], [i0, i1],
            vcost(o, i0, 1 if i0["ps"] or i1["ps"] else 2))

    def ts(o, i, s1, op0, s2=None, op1=None):
        c = vcost(o, i, 0.5 if o["two"] and i["two"] else 1)
        if op1 is None:
            add("V", lambda: g.vector.tensor_scalar(o["ap"], i["ap"], val(s1), None, op0), [o], [i, s1], c)
        else:
            add("V", lambda: g.vector.tensor_scalar(o["ap"], i["ap"], val(s1), val(s2), op0, op1), [o], [i, s1, s2], c)

    def ms(o, c):
        add("V", lambda: g.vector.memset(o["ap"], c), [o], [], vcost(o, o, 0.5 if o["two"] else 1))

    def act(o, i, f, bias=None, scale=None):
        kw = {}
        if bias is not None:
            kw["bias"] = val(bias)
        if scale is not None:
            kw["scale"] = val(scale)
        add("S", lambda: g.scalar.activation(o["ap"], i["ap"], f, **kw), [o], [i, bias, scale], vcost(o, i, 1))

    def mm(items, first=True, last=True):
        def fn():
            r = None
            for k, (o, l, x) in enumerate(items):
                r = g.tensor.matmul(o["ap"], l["ap"], x["ap"], first and k == 0, last and k == len(items) - 1)
            return r
        add("P", fn, [items[0][0]], [y for it in items for y in it[1:]], FIX + COST["pe"] * sum(max(64, it[2]["n"]) for it in items))

    def mms(groups, out):
        def fn():
            r = None
            for items in groups:
                for k, (o, l, x) in enumerate(items):
                    r = g.tensor.matmul(o["ap"], l["ap"], x["ap"], k == 0, k == len(items) - 1)
            return r
        add("P", fn, [out], [y for items in groups for it in items for y in it[1:]], FIX + COST["pe"] * 64 * sum(len(x) for x in groups))

    def iota(o, pat, base, cm):
        if SB[o["reg"][0][0]][1] == I32:
            add("G", lambda: g.iota(o["ap"], pat, base, cm), [o], [], 0.13 + 2 * cy * o["n"])
        else:
            add("G", lambda: g.iota(o["ap"], pat, base, cm, allow_small_or_imprecise_dtypes=True), [o], [], 0.13 + 2 * cy * o["n"])

    def fill(name, lo, hi, c=0):
        for at in range(lo, hi, 512):
            n = min(hi - at, 512)
            iota(a(name, at, at + n), [[0, n]], c, 0)

    def dma(e, name, pairs, outs, ins, nbytes):
        add(e, lambda: [eng[e].dma_start(o, i) for o, i in pairs], outs, ins, COST["dma"] + nbytes / COST["bw"] + 0.1 * len(pairs), "d", name,
            0.2 + 0.1 * len(pairs))

    def rows(e, name, table, srcs, ins):
        dma(e, name, [(T[table][r::16, 0:V], s) for r, s in srcs], [reg(table, r, r + 1) for r, _ in srcs], ins, 65536 * len(srcs))

    def send(name, step, src, dst_ap, dst_reg, nbytes):
        to = T.cores[(q + step) % N]
        fr = T.cores[(q - step) % N]
        rid, pid, _ = topo.addr(to)
        add("G", lambda: g.remote_dma(dst_ap, src["ap"], T.sem["r_" + name], T.sem["s_" + name], pid, rid, topo.mask(core, to)),
            [], [src], COST["rem"] + nbytes / COST["bw"], "s", name, 0.3)
        ops[-1]["cnt"] = len(topo.engines(core, to))
        add("R", None, [{"reg": dst_reg}], [], 0.0, "r", name)
        ops[-1]["cnt"] = len(topo.engines(fr, core))

    def sendto(name, src, dst, nbytes, step=1):
        send(name, step, src, dst["ap"], dst["reg"], nbytes)

    def od(mat, i):
        return a(mat, 15 - i, 143 - i)

    def pick(out, mat, buf, lo, n):
        return [(out, od(mat, i), a(buf, lo + i, lo + 16 * n, 16)) for i in range(16)]

    def col(k, name="COL"):
        return a(name, k, k + 1)

    def reg(name, lo=0, hi=1 << 20):
        return {"reg": [(name, lo, hi)]}

    def gather(e, out, win, off):
        if e == "V":
            cp(out, ind(win, off))
        else:
            act(out, ind(win, off), AF.Identity)

    def wide(cfg, out, win, offs):
        n = V // len(cfg)
        for k, e in enumerate(cfg):
            gather(e, a(out, n * k, n * k + n), a(win), a(offs, n * k // 16, (n * k + n) // 16))

    dma("Y", "cc", [(a("CCo")["ap"], T.cc[:, :])], [a("CCo")], [], 131072)
    dma("S", "pl", [(a("PLo")["ap"], T.pl[:, :])], [a("PLo")], [], 131072)
    dma("Y", "fo", [(T.F4[:, :], T.fo[:, :])], [a("F4")], [], 1 << 20)
    dma("Y", "nm", [(T.NI3[:, k, :], T.nm[k]) for k in range(8)], [reg("NI3")], [], 400000)
    dma("Y", "x", [(T.X[:, :], T.tx[:, :])], [a("X")], [], 1 << 20)
    iota(a("PI", 0, 1), [[0, 1]], 0, 1)
    iota(a("IOT"), [[1, 256]], 1, 0)
    iota(col(0), [[0, 1]], 1, 1)
    if CFG["it"] == "G":
        for n in range(0, V, 512):
            iota(a("IT", n, n + 512), [[1, 32], [256, 16]], 1 + n // 16, 0)
    else:
        iota(a("IT", 0, 256), [[1, 16], [256, 16]], 1, 0)
        for n in (256, 512, 1024, 2048):
            act(a("IT", n, 2 * n), a("IT", 0, n), AF.Identity, float(n // 16))
    ts(a("IE", 0, 256), a("CCo"), 4, OP.logical_shift_right)
    ts(a("IE", 256, 512), a("CCo"), 15, OP.bitwise_and)
    cp(a("CHL", 0, 256), a("IE", 0, 256))
    ts(a("CHL", 256, 512), a("IE", 256, 512), 256.0, OP.mult)
    send("cc", 1, a("CHL"), T.CCD[:, :], [("CCD", 0, 512)], 131072)
    sendto("pl", a("PLo"), a("PLp"), 131072)
    sendto("f1", a("F4"), a("F1"), 1 << 20)

    k128, k144, k256 = a("IOT", 0, 128), a("IOT", 0, 144), a("IOT")
    ts(a("PI", 1, 2), a("PI", 0, 1), 15, OP.bitwise_and)
    cp(col(1), a("PI", 1, 2))
    ts(a("ROW"), a("IOT", 0, 16), -1.0, OP.add, col(1), OP.is_equal)
    ts(a("LOW"), a("IOT", 0, 16), -1.0, OP.add, col(1), OP.is_gt)

    def row(r):
        return col(r, "ROW")
    ts(a("LC"), a("IOT", 0, 32), row(0), OP.mult, 64.0, OP.mult)
    ts(a("LT", 0, 64), a("IOT", 0, 64), row(1), OP.mult)
    for k in range(6):
        n = 64 << k
        if CFG["lt"] == "V":
            ts(a("LT", n, 2 * n), a("LT", 0, n), col(n // 64 - 1, "LC"), OP.add)
        else:
            act(a("LT", n, 2 * n), a("LT", 0, n), AF.Identity, col(n // 64 - 1, "LC"))
    rows("Y", "cct", "LT", [(2, T.CCD[:, 0:256]), (3, T.CCD[:, 256:512])], [reg("CCD")])
    if CFG["tw"] == "G":
        fill("TW", 0, V)
    else:
        for h in range(2):
            ms(a("TW", 2048 * h, 2048 * h + 2048), 0.0)
    fill("CAND", 0, V)
    rows("Y", "nxt", "CAND", [(2, a("CHL", 0, 256)["ap"]), (3, a("CHL", 256, 512)["ap"])], [a("CHL")])
    ts(col(2), col(0), col(1), OP.subtract)
    ts(col(3), col(0), col(1), OP.subtract, 15.0, OP.add)
    ts(col(4), col(4, "LOW"), col(2, "LOW"), OP.subtract)
    ts(col(5), row(2), 4096.0, OP.mult, row(3), OP.add)
    ts(col(6), col(5), 1.0 / 256, OP.mult)
    ts(col(7), row(5), row(4), OP.subtract, row(6), OP.subtract)
    ts(col(8), col(7), 8192.0, OP.mult, col(2, "LOW"), OP.add)
    ts(col(9), row(5), -65536.0, OP.mult, 65537.0, OP.add)
    ts(col(10), row(5), 65536.0, OP.mult, -65536.0, OP.add)
    ts(col(11), col(1), 1.0, OP.add)
    ts(col(12), row(1), float(V), OP.mult)
    ts(a("B"), k144, col(3), OP.is_equal)
    for nm_, w in (("BOUT", col(6)), ("BQ", col(4)), ("BSEL", col(8)), ("BH", 0.5), ("B0", row(2)), ("B256", 256.0)):
        act(a(nm_), a("B"), AF.Identity, None, w)
    ts(a("IDF"), k128, col(0), OP.is_equal)
    for nm_, w in (("IDN", 1.0), ("I2", 2.0), ("NI", -1.0), ("N2", -2.0), ("I32", 32.0), ("IBIG", 8192.0), ("NBIG", -8192.0)):
        act(a(nm_), a("IDF"), AF.Identity, None, w)
    iota(a("NWT", 0, 128), [[16, 8], [0, 16]], 1, 0)
    ts(a("ONES"), a("NWT", 0, 128), col(2), OP.is_equal)
    add("G", lambda: g.affine_select(a("TLE")["ap"], a("ONES")["ap"], [[1, 128]], OP.is_ge, 0.0, 0, -1), [a("TLE")], [a("ONES")], 0.17 + 256 * cy)
    for nm_, w in (("NEG", -1.0), ("ONEB", 8192.0), ("SUM2", col(2, "LOW"))):
        act(a(nm_), a("ONES"), AF.Identity, None, w)
    act(a("OUT4"), a("ONEB"), AF.Identity, None, row(4))
    act(a("CAND", V, V + 16), a("IOT", 0, 16), AF.Identity, row(4), 0.0)
    for t in range(1, TV + 1):
        act(a("MB", 128 * t - 128, 128 * t), a("ONES"), AF.Identity, None, col((STEP * t) % V % 16, "LOW"))
    iota(a("NW"), [[0, 16], [1, 16]], 0, 0)
    if CFG["nwt"] == "V":
        ts(a("TRI"), a("NW"), col(1), OP.is_gt)
    else:
        ts(a("TRB"), a("NW"), col(1), OP.is_le)
    ts(a("REP"), a("IOT", 0, 16), -1.0, OP.add)
    iota(a("K16"), [[1, 256]], 1, 0)
    ts(a("DUMW"), a("K16"), row(0), OP.mult, col(12), OP.add)
    iota(a("FD"), [[16, 256]], V, 1)
    iota(a("OWN", 0, 256), [[16, 256]], 0, 0)
    act(a("OWN", 256, 512), a("K16"), AF.Identity, col(11), 0.0)
    fill("M1", 0, 256, -1)
    fill("CS", 0, 1)
    fill("CS", 257, 258, 16)
    way = CFG["way"][TV]
    mixed = "A" in way and "P" in way
    if mixed:
        dma("Y", "xm", [(T.XM[:, 512 * k:512 * k + 512], T.tx[:, 512 * k:512 * k + 512]) for k in range(8) if way[k] == "A"],
            [a("XM", 512 * k, 512 * k + 512) for k in range(8) if way[k] == "A"], [], 131072 * way.count("A"))
        for k in range(8):
            if way[k] == "P":
                fill("XM", 512 * k, 512 * k + 512)

    tt(a("RHO"), a("CHL", 0, 256), a("CHL", 256, 512), OP.add)
    cp(a("P2"), a("RHO"))
    for k in range(8):
        act(ind(a("CIW"), a("P2", 32 * k, 32 * k + 32)), a("IT", 512 * k, 512 * k + 512), AF.Silu)
        if k < CFG["cie"]:
            ops[-1]["lead"] = 40.0

    for h in range(2):
        add("V", lambda h=h: g.vector.tensor_scalar(a("NF", 128 * h, 128 * h + 128)["ap"], T.NI3[:, :, 16 * h:16 * h + 16], 1.0, None, OP.add),
            [a("NF", 128 * h, 128 * h + 128)], [reg("NI3")], FIX + 128 * cy)
        add("P", lambda h=h: g.tensor.transpose(T.PS7[:, 128 * h:128 * h + 128], a("NF", 128 * h, 128 * h + 128)["ap"], a("IDF")["ap"]),
            [a("PS7")], [a("NF", 128 * h, 128 * h + 128), a("IDF")], FIX + 512 * COST["pe"])
    for h in range(2):
        cp(a("NC", h, 256, 2), a("PS7", 128 * h, 128 * h + 128))

    def names(t):
        if t <= TV:
            ts(a("NO"), a("NC"), -1.0, OP.add)
        act(a("NHL", 0, 256), a("NC"), AF.Identity)
        tt(a("NHL", 256, 512), a("NC"), a("NHL", 0, 256), OP.subtract)

    def name_rows(t):
        rows("Y", "nr%d" % t, "CAND", [(0, a("NHL", 0, 256)["ap"]), (1, a("NHL", 256, 512)["ap"])], [a("NHL")])
    names(1)
    name_rows(1)

    def hints(t, offs):
        wide(CFG["q"][t], "QW%d" % (t % 2), "LT", offs)

    def named(t):
        for k in range(8):
            lo, hi = 512 * k, 512 * k + 512
            w, off = a("F%d" % t), a("NO", 32 * k, 32 * k + 32)
            if CFG["way"][t][k] == "P":
                gather(CFG["b"][t][k], a("BB", lo, hi), w, off)
                continue
            if CFG["way"][t][k] == "D":
                gather("S", a("BB", lo, hi), w, off)
                tt(a("RB", lo, hi), ind(w, off), a("X", lo, hi), OP.subtract)
                continue
            if CFG["way"][t][k] == "C":
                gather("S", a("BB", lo, hi), w, off)
                p = a("PS4")
                mm([(p, a("IDN"), a("BB", lo, hi)), (p, a("NI"), a("X", lo, hi))])
                act(a("RB", lo, hi), p, AF.Abs)
                continue
            tt(a("BB", lo, hi), ind(w, off), a("X", lo, hi), OP.subtract)
            if CFG["ba"][t][k] == "V":
                ts(a("RB", lo, hi), a("BB", lo, hi), 0.0, OP.max)
            else:
                act(a("RB", lo, hi), a("BB", lo, hi), AF.Abs)

    ts(a("IA"), a("PLp"), 15, OP.bitwise_and)
    ts(a("IB"), a("PLp"), 4, OP.logical_shift_right, 255, OP.bitwise_and)
    ts(a("FA"), a("IA"), 256.0, OP.mult)
    tt(a("FB"), a("FA"), a("IB"), OP.add)
    cp(a("PT"), a("FB"))
    ts(a("FC"), a("PLp"), 0.0, OP.is_lt)
    tt(a("DM"), a("FC"), a("FD"), OP.mult)
    hints(1, "PT")
    for k, (lo, hi) in enumerate(zip(CFG["sc"], CFG["sc"][1:])):
        p = a("PS%d" % (5 + k % 2), 0, hi - lo)
        mm(pick(p, "BOUT", "QW1", 16 * lo, hi - lo))
        tt(a("FC", lo, hi), p, a("DM", lo, hi), OP.max)
        cp(a("SO", lo, hi), a("FC", lo, hi))
        cp(ind(a("TW"), a("SO", lo, hi)), a("LT", 16 * lo, 16 * hi))
        if k in CFG["fat"]:
            t = 2 + CFG["fat"].index(k)
            sendto("f%d" % t, a("F4"), a("F%d" % t), 1 << 20, t)
            ops[-2]["r"] = ops[-2]["r"] + a("SO", lo, hi)["reg"]

    def pass_hints(t):
        for h in range(4):
            items = pick(a("PS4", 64 * h, 64 * h + 64), "BQ", "QW%d" % (t % 2), 1024 * h, 64)
            for k in range(0, 16, CFG["qc"]):
                mm(items[k:k + CFG["qc"]], k == 0, k + CFG["qc"] == 16)
        cp(a("QO"), a("PS4", 0, 256))
        if t == TV:
            act(a("SGN"), a("PS4", 0, 256), AF.Identity, 96.0 - 127.5 / 512, 1.0 / 512)
            act(a("FC"), a("PS4", 0, 256), AF.Identity, 8190.0 * 96, 16.0)
        if t < TV:
            sendto("qo%d" % (t + 1), a("QO"), a("QI%d" % (t + 1)), 65536)
    pass_hints(1)
    named(1)
    dma("Y", "cil", [(a("CIL")["ap"], T.CIW[0::16, :])], [a("CIL")], [a("CIW")], 131072)
    cp(a("IC"), a("CIL"))
    ts(a("CIo"), a("IC"), -1.0, OP.add)
    sendto("ci", a("CIo"), a("CIp"), 65536)
    if CFG["early2"]:
        hints(2, "QI2")

    def table(t, name, rws, buf, lo, dram):
        n = 256 * len(rws)
        if t < TV:
            send("%s%d" % (name[0], t + 1), 1, a(buf, lo, lo + n), dram[t - 1], [(name[0] + str(t), 0, n)], 256 * n)
            rows("Y", "%s%d" % (name[1], t + 1), "LT", [(r, dram[t - 1][:, 256 * k:256 * k + 256]) for k, r in enumerate(rws)], [reg(name[0] + str(t))])
        else:
            rows("Y", "%s5" % name[1], "LT", [(r, a(buf, lo + 256 * k, lo + 256 * k + 256)["ap"]) for k, r in enumerate(rws)], [a(buf, lo, lo + n)])

    def cut(items, first, last, n):
        for k in range(0, len(items), n):
            mm(items[k:k + n], first and k == 0, last and k + n >= len(items))

    acc = CFG["acc"]
    free, forced = a("FR", 0, 256), a("LHL", 512, 768) if CFG["fo"] == 1 else a("FR", 256, 512)
    for t in range(1, TV + 1):
        phase[0] = t
        QW, F = "QW%d" % (t % 2), a("F%d" % t)
        s = (STEP * t) % V
        ca = s // 16
        votes = a("PS2", 0, 256)
        mm([(votes, a("IDN"), a("M1"))], True, False)
        for j in range(4):
            p = a("PS3", 64 * j, 64 * j + 64)
            mm(pick(p, "BSEL", "TW", 1024 * j, 64))
            ts(a("LO", 64 * j, 64 * j + 64), p, -1.0, OP.add, 0.0, OP.max)
            cm, late = CFG["cm"][t][j], []
            for k in (2 * j, 2 * j + 1):
                lo, hi = 512 * k, 512 * k + 512
                u, b, x, p = a("UU", lo, hi), a("BB", lo, hi), a("X", lo, hi), a("PS%d" % CFG["banks"][k % len(CFG["banks"])])
                listed = ind(F, a("LO", 32 * k, 32 * k + 32))
                if CFG["way"][t][k] in "PD":
                    tt(u, listed, b, OP.subtract)
                    items = [(p, a("I2"), b), (p, a("N2"), x)] if CFG["way"][t][k] == "P" else [(p, a("I2"), a("RB", lo, hi))]
                    if CFG["ws"]:
                        mm(items, True, False)
                        mm([(p, a("IDN"), u)], False, True)
                    else:
                        mm(items + [(p, a("IDN"), u)])
                    tt(u, p, u, OP.mult)
                    late.append(k)
                    continue
                rb, ra = a("RB", lo, hi), a("UR", lo, hi)
                if CFG["way"][t][k] == "C":
                    p = a("PS%d" % (6 + k % 2))
                    act(u, listed, AF.Identity)
                    mm([(p, a("NI"), x), (p, a("IDN"), u)])
                    act(ra, p, AF.Abs)
                    mm([(p, a("IDN"), rb), (p, a("NI"), ra)])
                else:
                    tt(u, listed, x, OP.subtract)
                    mm([(p, a("I2"), rb), (p, a("NI"), b)] if CFG["ba"][t][k] == "V" else [(p, a("IDN"), rb)], True, False)
                if CFG["way"][t][k] == "C":
                    pass
                elif CFG["aa"][t][k] == "V":
                    ts(ra, u, 0.0, OP.max)
                    mm([(p, a("IDN"), u), (p, a("N2"), ra)], False, True)
                else:
                    act(ra, u, AF.Abs)
                    mm([(p, a("NI"), ra)], False, True)
                if cm == "V":
                    ts(u, p, 0.5, OP.is_gt, -0.5, OP.add)
                else:
                    act(u, p, AF.Sign, -0.5)
            if late:
                u = a("UU", 512 * late[0], 512 * late[-1] + 512)
                if cm == "V":
                    ts(u, u, -0.5, OP.is_lt, -0.5, OP.add)
                else:
                    act(u, u, AF.Sign, -0.5, -1.0)
            mm(pick(a("PS2", 64 * j, 64 * j + 64), "B" if cm == "V" else "BH", "UU", 1024 * j, 64), False, False)
        lst = a("PS3", 0, 256)
        act(a("SGN"), lst, AF.Sign, -0.5)
        last = [(votes, a("I32"), a("SGN"))]
        if t > 1:
            VI, SI, OI = a("VI%d" % t), "SI%d" % t, "OI%d" % t
            p = a("PS4", 256, 512)
            gather("S", a("XS"), a("X"), a(SI, 16, 32))
            if "A" in way:
                gather("S", a("BT"), a("BB"), a(SI, 16, 32))
                if mixed:
                    gather("S", a("XT"), a("XM"), a(SI, 16, 32))
                mm([(p, a("IDN"), a("BT")), (p, a("IDN"), a("XT" if mixed else "XS"))])
                act(a("BS"), p, AF.Identity)
            else:
                gather("S", a("BS"), a("BB"), a(SI, 16, 32))
            tt(a("US"), ind(F, a(SI, 0, 16)), a("BS"), OP.subtract)
            mm([(p, a("I2"), a("BS")), (p, a("N2"), a("XS")), (p, a("IDN"), a("US"))])
            tt(a("US"), p, a("US"), OP.mult)
            ts(a("US"), a("US"), -0.5, OP.is_lt, -0.5, OP.add)
            mm([(p, a("IDN"), VI), (p, od("B", 5), a("US"))])
            ts(a("VJ"), p, col(9), OP.min, col(10), OP.max)
            cp(ind(a("TW", 0, WW), a(OI, 16, 32)), a("VJ"))
            lst = a("PS3", 256, 512)
            for h in range(0, 16, 4):
                mm(pick(lst, "BSEL", "TW", 0, 256)[h:h + 4], h == 0, h == 12)
            ts(forced, lst, 8191.5, OP.is_gt)
            last.append((votes, a("IBIG"), forced))
        tt(a("E1"), lst, a("NC"), OP.is_equal)
        mm(last + [(votes, a("IBIG"), a("E1"))], False, True)
        if t > 1 and acc:
            mm([(lst, a("NBIG"), forced)], False, True)
        act(a("LHL", 0, 256), lst, AF.Identity)
        tt(a("LHL", 256, 512), lst, a("LHL", 0, 256), OP.subtract)
        ts(free, votes, 31.5, OP.is_lt)
        if t > 1 and CFG["fo"] == 2:
            table(t, ("fc", "fd"), (6,), "FR", 256, T.FD3)
        if t > 1 and CFG["fo"] == 1:
            table(t, ("lh", "lt"), (0, 1, 6), "LHL", 0, T.LD3)
        else:
            table(t, ("lh", "lt"), (0, 1), "LHL", 0, T.LD)
        add("V", lambda: g.vector.tensor_tensor_scan(a("CS", 1, 257)["ap"], free["ap"], free["ap"], 0.0, OP.add, OP.max),
            [a("CS", 1, 257)], [free], FIX + 128 * cy)
        if t > 1 and CFG["fo"] == 0:
            table(t, ("fr", "ft"), (4, 6), "FR", 0, T.FD2)
        else:
            table(t, ("fr", "ft"), (4,), "FR", 0, T.FD1)
        if t > 1:
            cp(ind(a(QW), a(OI, 0, 16)), VI)
            pass_hints(t)
        if t > 1 and acc:
            p = lst
            mm([(p, a("NBIG"), free)], False, True)
        else:
            p = a("PS0", 0, 256)
            mm([(p, a("IDN"), a("LHL", 0, 256)), (p, a("IDN"), a("LHL", 256, 512))] + [(p, a("NBIG"), x) for x in ([forced, free] if t > 1 else [free])])
        act(a("LK"), p, AF.Identity)
        p = a("PS1", 0, 256)
        if CFG["nc"] == "P":
            mm([(p, a("IDN"), a("NHL", 0, 256)), (p, a("IDN"), a("NHL", 256, 512)), (p, a("IBIG"), a("M1"))], True, False)
            mm([(p, a("IBIG"), free)], False, True)
        else:
            mm([(a("PS1", 256, 512), a("IBIG"), free)])
            tt(p, a("PS1", 256, 512), a("NC"), OP.min)
        tt(a("NC"), p, a("LK"), OP.max)
        names(t + 1)
        if t < TV:
            named(t + 1)
            wide(CFG["t"][t + 1], "TW", "LT", "CIp")
            if t > 1 or not CFG["early2"]:
                hints(t + 1, "QI%d" % (t + 1))
        if t == TV:
            fill("QW1", 0, V)
        below = [(a("ONES"), a("CS", ca, ca + 1)), (a("MB", 128 * t - 128, 128 * t), a("FR", ca, ca + 1))]
        tot, c16 = a("CS", 256, 257), a("CS", 257, 258)
        pa, pt, px = a("PS5", 0, 1), a("PS5", 1, 2), a("PS5", 2, 3)
        mms([[(pa, l, x) for l, x in below], [(pt, a("ONES"), tot), (pt, a("NEG"), c16)],
             [(px, a("NEG"), tot), (px, a("ONES"), c16)] + [(px, l, x) for l, x in below]], a("PS5", 0, 3))
        pb = a("PS7", 0, 1)
        mm([(pb, od("B", i), a("CS", 16 * i + 16, 16 * i + 17)) for i in range(16)])
        three = 6 in CFG["banks"]
        rkb = "PS2" if three else "PS6"
        mm(pick(a(rkb, 256, 272), "B", "CS", 1, 16))
        p = a(rkb, 0, 256)
        mm([(p, a("ONES"), a("CS", 0, 256)), (p, a("TLE"), free)])
        act(a("CT"), a(rkb, 256, 272), AF.Identity)
        act(a("RK"), p, AF.Identity)
        ts(a("DL", 0, 1), pt, pa, OP.min, 0.0, OP.max)
        rj = a("PS5", 256, 512)
        ts(rj, a("K16"), px, OP.is_gt, a("DL", 0, 1), OP.mult)
        tt(a("RHO"), rj, k256, OP.add)
        ts(a("L1"), a("RHO"), pb, OP.is_gt, 16.0, OP.mult)
        if acc:
            ph = pc = pp = a("PS5", 32, 48)
            mm(pick(ph, "B", "L1", 0, 16))
            ts(a("HO"), ph, 1.0 / 16, OP.mult, 15.0, OP.min)
            tt(a("L2"), ind(a("CT"), a("HO")), a("RHO"), OP.is_lt)
            mm(pick(pc, "B", "L2", 0, 16), False, True)
            ts(a("CO"), pc, 255.0, OP.min)
            tt(a("L3"), ind(a("RK"), a("CO")), a("RHO"), OP.is_lt)
            mm(pick(pp, "B256", "L3", 0, 16), False, True)
        else:
            ph, pc, pp = a("PS5", 32, 48), a("PS5", 48, 64), a("PS5", 64, 80)
            mm(pick(ph, "B", "L1", 0, 16))
            ts(a("HO"), ph, 1.0 / 16, OP.mult, 15.0, OP.min)
            cp(a("CB"), ph)
            tt(a("L2"), ind(a("CT"), a("HO")), a("RHO"), OP.is_lt)
            mm(pick(pc, "B", "L2", 0, 16) + [(pc, a("IDN"), a("CB"))])
            ts(a("CO"), pc, 255.0, OP.min)
            cp(a("CB"), pc)
            tt(a("L3"), ind(a("RK"), a("CO")), a("RHO"), OP.is_lt)
            mm(pick(pp, "B256", "L3", 0, 16) + [(pp, a("IDN"), a("CB"))])
        ts(a("WO"), pp, float(V), OP.min)
        gather("S", a("VAL"), a("CAND"), a("WO"))
        if t < TV:
            sendto("va%d" % (t + 1), a("VAL"), a("VI%d" % (t + 1)), 65536)
            name_rows(t + 1)
        if t == TV - 1:
            rows("Y", "own", "CAND", [(2, a("OWN", 0, 256)["ap"]), (3, a("OWN", 256, 512)["ap"])], [a("OWN")])
        no = 32 if t < TV else 16
        pn, pw, pl_, pq = a("PS5", 96, 96 + no), a("PS4", 256, 512) if three else a("PS6", 0, 256), a("PS7", 0, 256), a("PS5", 128, 144)
        mm(pick(a("PS5", 96, 112), "BSEL", "VAL", 0, 16))
        mm([(pw, a("SUM2"), a("VAL"))])
        if CFG["sp"] == 2:
            cp(a("NLF", 0, 16), a("PS5", 96, 112))
            ts(a("SPC", 0, 16), a("PS5", 96, 112), -1.0, OP.add)
        if t < TV:
            p = a("PS5", 112, 128)
            mm(pick(p, "BOUT", "VAL", 0, 16) + [(p, a("NI"), a("M1", 0, 16))])
            if CFG["sp"] == 2:
                ts(a("SPC", 16, 32), p, -1.0, OP.add)
                act(a("NLF", 16, 32), p, AF.Identity)
        if CFG["sp"] == 1:
            ts(a("SPC", 0, no), pn, -1.0, OP.add)
            cp(a("NLF", 0, no), pn)
        if t < TV:
            sendto("si%d" % (t + 1), a("SPC"), a("SI%d" % (t + 1)), 8192)
        cp(a("NU"), pw)
        act(a("NW"), pw, AF.Identity)
        gather("S", a("QG"), a(QW), a("SPC", 0, 16))
        mm(pick(pq, "B0", "QG", 0, 16))
        mm([(pl_, a("OUT4"), a("VAL"))], True, False)
        at, items = 0, []
        for i in range(15):
            n = 240 - 16 * i
            ts(a("EQ", at, at + n), a("NU", 256 - n, 256), a("NLF", i, i + 1), OP.is_equal)
            items.append((a("PS7", 256 - n, 256), a("ONEB"), a("EQ", at, at + n)))
            at += n
            if i in (3, 8, 14):
                mm(items, False, False)
                items = []
        if CFG["nwt"] == "V":
            tt(a("NWT"), pw, a("TRI"), OP.mult)
        else:
            p = a("PS5", 256, 512)
            mm([(p, a("SUM2"), a("VAL")), (p, a("NBIG"), a("TRB"))])
            act(a("NWT"), p, AF.Identity)
        tt(a("ED"), ind(a("NLF", 0, 16), a("REP")), a("NWT"), OP.is_equal)
        mm([(pl_, a("ONEB"), a("ED"))], False, False)
        cp(a("QC"), pq)
        tt(a("EE"), ind(a("LK"), a("QC")), a("NW"), OP.is_equal)
        mm([(pl_, a("ONEB"), a("EE"))], False, True)
        tt(a("LF"), pl_, a("DUMW"), OP.min)
        if CFG["pf"] == 2:
            for lo in range(160, 160 + no, 16):
                mm(pick(a("PS5", lo, lo + 16), "BSEL", "LF", 0, 16))
            tt(a("TO", 0, no), a("PS5", 160, 160 + no), a("NLF", 0, no), OP.max)
        else:
            mm(pick(a("PS5", 160, 176), "BSEL", "LF", 0, 16))
            for lo in range(0, no, 16):
                tt(a("TO", lo, lo + 16), a("PS5", 160, 176), a("NLF", lo, lo + 16), OP.max)
        ts(a("OFF", 0, no), a("TO", 0, no), -1.0, OP.add)
        if t < TV:
            sendto("of%d" % (t + 1), a("OFF"), a("OI%d" % (t + 1)), 8192)

    phase[0] = 5
    for m in range(0, 8, 2):
        mms([[(a("PS2", 32 * k + 16 * h, 32 * k + 16 * h + 16), a("NHL", 256 * d + h, 256 * d + 256, 2), a("IDN", 16 * k, 16 * k + 16)) for d in range(2)]
             for k in (m, m + 1) for h in range(2)], a("PS2", 0, 256))
    act(a("FA"), a("PS2", 0, 256), AF.Identity, -1.0)
    dma("Y", "yn", [(T.yn[k], a("FA", 32 * k, 32 * k + 32)["ap"]) for k in range(8)], [], [a("FA")], 300000)
    wide(CFG["fin"], "UU", "LT", "QO")
    held, place = a("PS0", 0, 256), a("PS1", 0, 256)
    mm([(place, a("NBIG"), a("SGN")), (place, a("I2"), a("SGN"))], True, False)
    mm([(held, a("NI"), a("OWN", 0, 256)), (held, a("NI"), a("OWN", 256, 512))], True, False)
    for h in range(4):
        cut(pick(a("PS0", 64 * h, 64 * h + 64), "BSEL", "UU", 1024 * h, 64), False, h == 3, 8)
    ts(a("E1"), held, 0.0, OP.not_equal)
    mm([(place, a("NBIG"), a("E1"))], False, True)
    tt(a("Y0"), place, a("FC"), OP.add)
    cp(ind(a("QW1"), a("OFF", 0, 16)), a("VAL"))
    for h in range(2):
        p = a("PS%d" % (3 + h), 0, 128)
        mm([(p, a("IDN"), a("M1", 0, 128))], True, False)
        mm(pick(p, "BQ", "QW1", 2048 * h, 128), False, True)
        tt(a("FB", 128 * h, 128 * h + 128), p, a("Y0", 128 * h, 128 * h + 128), OP.max)
        dma("YS"[h], "yp%d" % h, [(T.yp[:, 128 * h:128 * h + 128], a("FB", 128 * h, 128 * h + 128)["ap"])], [], [a("FB", 128 * h, 128 * h + 128)], 65536)
    return ops


def hazards(ops):
    hist = {}
    sent = {}
    above = []
    for i, o in enumerate(ops):
        deps = set()
        acc = [(x, False) for x in o["r"]] + [(x, True) for x in o["w"]]
        for (nm_, lo, hi), wr in acc:
            bank = nm_[:2] == "PS"
            for j, l2, h2, w2 in hist.get(nm_, []):
                if (lo < h2 and l2 < hi and (wr or w2)) or (bank and (ops[j]["e"] != o["e"] or wr)):
                    deps.add(j)
        if o["kind"] == "s":
            sent[o["name"]] = i
        if o["kind"] == "r":
            deps = {sent[o["name"]]}
        for (nm_, lo, hi), wr in acc:
            h = hist.setdefault(nm_, [])
            if wr and nm_[:2] != "PS":
                h[:] = [e for e in h if not (lo <= e[1] and e[2] <= hi)]
            elif nm_[:2] == "PS":
                h[:] = h[-48:]
            h.append((i, lo, hi, wr))
        deps.discard(i)
        o["deps"] = deps
        far = 0
        for j in deps:
            far |= above[j]
        o["near"] = sorted(j for j in deps if not far >> j & 1)
        for j in deps:
            far |= 1 << j
        above.append(far)


def tables(ops, sets):
    n = len(ops)
    en = ["VSPGYR".index(o["e"]) for o in ops]
    full = [o["kind"] == "c" for o in ops]
    tabs = []
    for cost, c, w in sets:
        dl = [[(j, (c["self"] if en[i] != 2 else 0.0) if en[j] == en[i] and full[j] else c["hop"]) for j in ops[i]["near"]] for i in range(n)]
        tabs.append((cost, [cost[i] if full[i] else ops[i]["hold"] for i in range(n)], dl, w, en))
    return tabs


def play(s, tab, trace=False):
    cost, hold, dl, _, en = tab
    free, last = [0.0] * 6, [-1] * 6
    t1, why = [0.0] * len(s), [-1] * len(s)
    for i in s:
        e = en[i]
        t, y = free[e], last[e]
        for j, d in dl[i]:
            u = t1[j] + d
            if u >= t:
                t, y = u, j
        t1[i] = t + cost[i]
        free[e] = t + hold[i]
        last[e] = i
        why[i] = y
    return (t1, why) if trace else max(t1)


def event_order(ops, tab, look, tol):
    cost, hold, dl, _, en = tab
    n = len(cost)
    way = [0.0] * n
    lead = [o.get("lead", 0.0) for o in ops]
    succ = [[] for _ in range(n)]
    for i in range(n - 1, -1, -1):
        way[i] += cost[i] + lead[i]
        for j, d in dl[i]:
            way[j] = max(way[j], way[i] + d)
            succ[j].append((i, d))
    left = [len(x) for x in dl]
    ready, free = [0.0] * n, [0.0] * 6
    pool = [[i for i in range(n) if not left[i] and en[i] == e] for e in range(6)]
    seq = []
    while len(seq) < n:
        best = None
        for e in range(6):
            p = pool[e]
            if p:
                now = max(free[e], min(ready[i] for i in p))
                i = max((i for i in p if ready[i] <= now + look), key=lambda i: way[i])
                if hold[i] > 0.45:
                    i = max((k for k in p if k == i or ready[k] <= now + hold[i] * tol), key=lambda k: way[k])
                st = max(now, ready[i])
                if best is None or st < best[0]:
                    best = (st, e, i)
        st, e, i = best
        pool[e].remove(i)
        free[e] = st + hold[i]
        seq.append(i)
        for k, d in succ[i]:
            ready[k] = max(ready[k], st + cost[i] + d)
            left[k] -= 1
            if not left[k]:
                pool[en[k]].append(k)
    return seq


def polish(ops, seq, tabs, steps):
    n = len(ops)
    en = tabs[0][4]
    pset = [set(o["near"]) for o in ops]

    def worth(s):
        return sum(play(s, tab) * tab[3] for tab in tabs)
    seed = [12345]

    def rnd(k):
        seed[0] = (seed[0] * 1103515245 + 12345) % 2147483648
        return (seed[0] >> 8) % k
    cur = best = worth(seq)
    keep = seq
    pairs = None
    for it in range(steps):
        if pairs is None or it % 8 == 0:
            t1, why = play(seq, tabs[rnd(len(tabs))], True)
            i = max(range(n), key=lambda x: t1[x])
            pairs = []
            while why[i] >= 0:
                if why[i] not in pset[i]:
                    pairs.append((why[i], i))
                i = why[i]
            if not pairs:
                break
        j, i = pairs[rnd(len(pairs))]
        a, b = seq.index(j), seq.index(i)
        if a >= b:
            continue
        far = rnd(4) if rnd(2) else 0
        if rnd(2):
            while far and a > 0:
                a -= 1
                far -= en[seq[a]] == en[i]
            need, up = set(pset[i]), [i]
            for x in reversed(seq[a:b]):
                if x in need:
                    up.append(x)
                    need |= pset[x]
            if j in need:
                continue
            u = set(up)
            new = seq[:a] + up[::-1] + [x for x in seq[a:b] if x not in u] + seq[b + 1:]
        else:
            while far and b < n - 1:
                b += 1
                far -= en[seq[b]] == en[j]
            down = {j}
            for x in seq[a + 1:b + 1]:
                if pset[x] & down:
                    down.add(x)
            if i in down:
                continue
            part = seq[a:b + 1]
            new = seq[:a] + [x for x in part if x not in down] + [x for x in part if x in down] + seq[b + 1:]
        w = worth(new)
        if w <= cur + 0.004 * (1 - it / steps) * rnd(100) / 100:
            seq, cur, pairs = new, w, None
            if w < best:
                best, keep = w, new
    return keep


def refine(ops, seq, tabs, steps, width=200, rounds=3, heat=0.003):
    n = len(ops)
    en = tabs[0][4]
    pset = [set(o["near"]) for o in ops]
    succ = []
    for tab in tabs:
        s = [[] for _ in range(n)]
        for i in range(n):
            for j, d in tab[2][i]:
                s[j].append((i, d))
        succ.append(s)
    seed = [12345]

    def rnd(k):
        seed[0] = (seed[0] * 1103515245 + 12345) % 2147483648
        return (seed[0] >> 8) % k

    def frame(s, a, b):
        out = []
        inside = set(s[a:b])
        for tab, sc in zip(tabs, succ):
            cost, hold, dl, w, _ = tab
            free, t1 = [0.0] * 6, [0.0] * n
            for i in s[:a]:
                t = max([free[en[i]]] + [t1[j] + d for j, d in dl[i]])
                t1[i] = t + cost[i]
                free[en[i]] = t + hold[i]
            nxt, way = [0.0] * 6, [0.0] * n
            for i in reversed(s[b:]):
                way[i] = nxt[en[i]] = max(cost[i] + max([way[j] + d for j, d in sc[i]] + [0.0]), nxt[en[i]] + hold[i])
            early, late, near = [0.0] * n, [0.0] * n, [None] * n
            for i in inside:
                early[i] = max([t1[j] + d for j, d in dl[i] if j not in inside] + [0.0])
                late[i] = max([way[j] + d for j, d in sc[i] if j not in inside] + [0.0])
                near[i] = [(j, d) for j, d in dl[i] if j in inside]
            out.append((cost, hold, near, w, free, nxt, early, late))
        return out

    def run(part, fr):
        total, pairs = 0.0, []
        for cost, hold, near, w, free0, nxt, early, late in fr:
            free, last = list(free0), [-1] * 6
            t1, why = {}, {}
            top, who = 0.0, -1
            for i in part:
                e = en[i]
                t, y = free[e], last[e]
                if early[i] > t:
                    t, y = early[i], -1
                for j, d in near[i]:
                    u = t1[j] + d
                    if u >= t:
                        t, y = u, j
                free[e] = t + hold[i]
                last[e] = i
                t += cost[i]
                t1[i] = t
                why[i] = y
                if t + late[i] > top:
                    top, who = t + late[i], i
            for e in range(6):
                if free[e] + nxt[e] > top:
                    top, who = free[e] + nxt[e], last[e]
            total += top * w
            while who >= 0 and why[who] >= 0:
                if why[who] not in pset[who]:
                    pairs.append((why[who], who))
                who = why[who]
        return total, pairs

    starts = list(range(0, max(n - width, 0) + width // 2, width // 2))
    each = steps // (rounds * len(starts))
    for a0 in starts * rounds:
        b0 = min(n, a0 + width)
        fr = frame(seq, a0, b0)
        part = seq[a0:b0]
        cur, pairs = run(part, fr)
        best, keep = cur, part
        for it in range(each):
            if not pairs:
                break
            j, i = pairs[rnd(len(pairs))]
            a, b = part.index(j), part.index(i)
            far = rnd(6) if rnd(2) else 0
            if rnd(2):
                while far and a > 0:
                    a -= 1
                    far -= en[part[a]] == en[i]
                need, up = set(pset[i]), [i]
                for x in reversed(part[a:b]):
                    if x in need:
                        up.append(x)
                        need |= pset[x]
                if j in need:
                    continue
                u = set(up)
                new = part[:a] + up[::-1] + [x for x in part[a:b] if x not in u] + part[b + 1:]
            else:
                while far and b < len(part) - 1:
                    b += 1
                    far -= en[part[b]] == en[j]
                down = {j}
                for x in part[a + 1:b + 1]:
                    if pset[x] & down:
                        down.add(x)
                if i in down:
                    continue
                new = part[:a] + [x for x in part[a:b + 1] if x not in down] + [x for x in part[a:b + 1] if x in down] + part[b + 1:]
            w, p2 = run(new, fr)
            if w <= cur + heat * len(tabs) * (1 - it / each) * rnd(100) / 100:
                part, cur, pairs = new, w, p2
                if w < best:
                    best, keep = w, new
        seq = seq[:a0] + keep + seq[b0:]
    return seq


def timings(g, core, T, topo, ops):
    sets = []
    for ch, w in SPREAD:
        c = dict(COST)
        c.update(ch)
        sets.append(([o["cost"] for o in build(g, core, T, topo, c)], c, w))
    return tables(ops, sets)


def plan(g, core, T, topo):
    ops = build(g, core, T, topo, COST)
    hazards(ops)
    if "seq" not in MEMO:
        tabs = timings(g, core, T, topo, ops)
        seq = min((event_order(ops, tab, look, tol) for tab in tabs for look in (0.02, 0.05, 0.1, 0.2) for tol in (0.0, 0.3, 0.5, 0.7)),
                  key=lambda s: sum(play(s, tab) * tab[3] for tab in tabs))
        MEMO["seq"] = refine(ops, seq, tabs, COST["steps"])
        MEMO["t"] = play(MEMO["seq"], tabs[0], True)[0]
        MEMO["tabs"] = tabs
    for o, t in zip(ops, MEMO["t"]):
        o["t1"] = t
    return ops, MEMO["seq"]


def emit(g, T, ops, seq):
    eng = {"V": g.vector, "S": g.scalar, "P": g.tensor, "G": g, "Y": g.sync}
    known = {e: {} for e in eng}
    count = {}
    for i in seq:
        o = ops[i]
        e = o["e"]
        if o["kind"] == "r":
            o["tok"], o["clock"] = ("r_" + o["name"], o["cnt"]), {}
            count[o["tok"][0]] = o["cnt"]
            continue
        kn = known[e]
        for j in sorted(o["deps"], key=lambda j: -ops[j]["t1"]):
            d = ops[j]
            if d["e"] == e == "P":
                continue
            s, v = d["tok"]
            if kn.get(s, 0) >= v:
                continue
            eng[e].wait_ge(T.sem[s], v)
            kn[s] = v
            for s2, v2 in d["clock"].items():
                kn[s2] = max(kn.get(s2, 0), v2)
        r = o["fn"]()
        if o["kind"] == "c":
            s = "e" + e
            count[s] = count.get(s, 0) + 1
            r.then_inc(T.sem[s], 1)
        elif o["kind"] == "d":
            s = "d_" + o["name"]
            for x in r:
                x.then_inc(T.sem[s], 16)
            count[s] = 16 * len(r)
        else:
            s = "s_" + o["name"]
            count[s] = o["cnt"]
        o["tok"], o["clock"] = (s, count[s]), dict(kn)
    seen = {}
    for kn in known.values():
        for s, v in kn.items():
            seen[s] = max(seen.get(s, 0), v)
    for s, v in count.items():
        if seen.get(s, 0) < v:
            g.sync.wait_ge(T.sem[s], v)


def rank_program(g, core, T, topo):
    if T.rank_of(core) is None:
        return
    ops, seq = plan(g, core, T, topo)
    emit(g, T, ops, seq)
